import numpy as np
import ml_dtypes


def mxq(x, axis, fmt="e4m3"):
    dtype, down = {"e4m3": (ml_dtypes.float8_e4m3fn, 7), "e5m2": (ml_dtypes.float8_e5m2, 14)}[fmt]
    v = np.moveaxis(np.asarray(x, np.float32).astype(ml_dtypes.bfloat16).astype(np.float64), axis, -1)
    blocks = v.reshape(v.shape[:-1] + (-1, 32))
    amax = np.abs(blocks).max(-1, keepdims=True)
    byte = np.maximum(np.where(amax > 0, np.frexp(amax)[1] - 1 + 127, 0) - down, 1)
    scale = np.exp2(byte - 127.0)
    codes = (blocks / scale).astype(np.float32).astype(dtype).astype(np.float64)
    return np.moveaxis((codes * scale).reshape(v.shape), -1, axis)


WIDE = False


def mx_kscale(k):
    if not WIDE:
        return np.ones(k)
    levels = np.array([10, -10, 5, -5, 0])
    if k % 512:
        return np.exp2(np.random.permutation(np.resize(levels, k // 32))).repeat(32)
    a = np.empty((k // 512, 16))
    for p in range(k // 512):
        a[p, :8] = np.random.permutation(np.resize(levels, 8))
        for g in range(8):
            far = levels[np.abs(levels - a[p, g]) >= 10]
            a[p, g + 8] = far[np.random.randint(len(far))]
    return np.exp2(a.ravel()).repeat(32)


BF16 = ml_dtypes.bfloat16


def bf(x):
    return np.asarray(x, np.float32).astype(BF16)


def f64(x):
    return np.asarray(x).astype(np.float64)


E2M1 = np.array([0.0, 0.5, 1.0, 1.5, 2.0, 3.0, 4.0, 6.0, -0.0, -0.5, -1.0, -1.5, -2.0, -3.0, -4.0, -6.0])


def pack_weight(w, fmt):
    k, n = w.shape
    w = f64(bf(w)).reshape(k // 32, 32, n)
    amax = np.abs(w).max(1)
    if fmt == "e4m3":
        byte = np.frexp(amax)[1] - 1 + 127 - 7
    else:
        mant, ex = np.frexp(amax / 6.0)
        byte = np.where(mant > 0.5, ex, ex - 1) + 127
    byte = np.clip(np.where(amax > 0, byte, 1), 1, 254)
    scaled = (w * np.exp2(127.0 - byte)[:, None, :]).reshape(k, n).astype(np.float32)
    by_word = np.ascontiguousarray(scaled.reshape(k // 512, 128, 4, n).transpose(0, 1, 3, 2))
    if fmt == "e4m3":
        words = by_word.astype(ml_dtypes.float8_e4m3fn).view(np.uint8)
    else:
        c = by_word.astype(ml_dtypes.float4_e2m1fn).view(np.uint8) & 0xF
        words = c[..., 0::2] | (c[..., 1::2] << 4)
    return np.ascontiguousarray(words), np.ascontiguousarray(byte.astype(np.uint8).reshape(k // 512, 16, n))


def unpack_weight(words, scales, fmt):
    g, p, n, _ = words.shape
    if fmt == "e4m3":
        vals = np.ascontiguousarray(words).view(ml_dtypes.float8_e4m3fn).astype(np.float64)
    else:
        nib = np.empty((g, p, n, 4), np.uint8)
        nib[..., 0::2] = words & 0xF
        nib[..., 1::2] = words >> 4
        vals = E2M1[nib]
    vals = vals * np.repeat(np.exp2(scales.astype(np.float64) - 127.0), 8, axis=1)[..., None]
    return vals.transpose(0, 1, 3, 2).reshape(g * 512, n)
def pack4(w):
    words, scales = pack_weight(w, "e2m1")
    return words.reshape(words.shape[0], 128, -1), scales


def unpack4(words, scales):
    return unpack_weight(words.reshape(words.shape[0], 128, -1, 2), scales, "e2m1")


M, K, F, A, R = 1024, 1024, 1536, 1024, 512


def draw0():
    s, t, u = mx_kscale(K), mx_kscale(F), mx_kscale(M)
    x = bf(np.random.standard_normal((M, K)) * s * u[:, None])
    w = bf(np.random.standard_normal((K, F)) / np.sqrt(K) / s[:, None] * t)
    p_words, p_scales = pack4(np.random.standard_normal((F, A)) / np.sqrt(F) / t[:, None])
    backup = bf(np.random.standard_normal((R, M)) / np.sqrt(M) / u)
    invtemp = bf((1 + 0.2 * np.random.standard_normal(M)) / u)
    vgain = bf((1 + 0.2 * np.random.standard_normal(F)) / t)
    return {"x": x, "w": w, "p_words": p_words, "p_scales": p_scales,
            "backup": backup, "invtemp": invtemp, "vgain": vgain}


def core(x, w, p_words, p_scales, backup, invtemp, vgain):
    h = np.maximum(mxq(f64(x), 1, "e4m3") @ mxq(f64(w), 0, "e4m3"), 0.0)
    logits = mxq(h, 1, "e4m3") @ unpack4(p_words, p_scales)
    policy = logits * f64(invtemp)[:, None]
    backed = mxq(f64(backup), 1, "e4m3") @ mxq(h, 0, "e4m3")
    value = backed * f64(vgain)
    return policy, value


def e4m3fn_bytes(y):
    return np.clip(np.asarray(y, np.float64), -448.0, 448.0).astype(np.float32).astype(ml_dtypes.float8_e4m3fn).view(np.uint8)


def e4m3fn_values(b):
    return np.asarray(b, np.uint8).view(ml_dtypes.float8_e4m3fn).astype(np.float64)


def setup_inputs():
    d = draw0()
    x0 = np.asarray(d['backup']).astype(np.float64)
    s = (np.max(np.abs(x0), axis=(0,), keepdims=True) / 448.0).astype(np.float32)
    out = {}
    for k, v in d.items():
        if k == 'backup':
            out['backup_bytes'] = e4m3fn_bytes(x0 / s.astype(np.float64))
            out['backup_scale'] = s
        else:
            out[k] = v
    return out


def reference(x, w, p_words, p_scales, backup_bytes, backup_scale, invtemp, vgain):
    return core(x, w, p_words, p_scales, e4m3fn_values(backup_bytes) * backup_scale.astype(np.float64), invtemp, vgain)

@@ -1,0 +1,397 @@
+from contextlib import ExitStack
+
+import concourse.mybir as mybir
+from concourse.masks import make_identity
+
+M, K, F, A, R = 1024, 1024, 1536, 1024, 512
+FLOPS = 2 * (M * K * F + M * F * A + R * M * F)
+
+F32 = mybir.dt.float32
+BF16 = mybir.dt.bfloat16
+I32 = mybir.dt.int32
+U32 = mybir.dt.uint32
+U8 = mybir.dt.uint8
+FP8 = mybir.dt.float8_e4m3fn
+FP8X4 = mybir.dt.float8_e4m3fn_x4
+FP4X4 = mybir.dt.float4_e2m1fn_x4
+ACT = mybir.ActivationFunctionType
+ALU = mybir.AluOpType
+
+P = 128
+NF = F // 512
+NS = M // 512
+
+
+def tile_policy_value_heads_s8_kernel(
+    tc, x, w, p_words, p_scales, backup_bytes, backup_scale, invtemp, vgain, policy, value
+):
+    nc = tc.nc
+    with ExitStack() as ctx:
+        keep = ctx.enter_context(tc.tile_pool(name="keep", bufs=1))
+        wstage = ctx.enter_context(tc.tile_pool(name="wstage", bufs=3))
+        xstage = ctx.enter_context(tc.tile_pool(name="xstage", bufs=4))
+        hstage = ctx.enter_context(tc.tile_pool(name="hstage", bufs=3))
+        ostage = ctx.enter_context(tc.tile_pool(name="ostage", bufs=4))
+        psum = ctx.enter_context(tc.psum_pool(name="psum", bufs=8))
+
+        def persistent(name, width, dtype):
+            return keep.tile([P, width], dtype, name=name, align_bytes=64)
+
+        def new_bank():
+            return psum.tile([P, 512], F32, name="bank")
+
+        ctx.enter_context(tc.manual_schedule())
+
+        warm = persistent("warm", 1, F32)
+        nc.vector.memset(warm[:], 0.0)
+        nc.scalar.activation(out=warm[:], in_=warm[:], func=ACT.Relu)
+        ident = persistent("ident", P, F32)
+        make_identity(nc, ident[:])
+        ps = keep.tile([P, NF, A], U8, name="ps", align_bytes=64)
+        nc.gpsimd.memset(ps[:].rearrange("p g n -> p (g n)").bitcast(I32), 0)
+        vrow = persistent("vrow", F, BF16)
+        nc.vector.memset(vrow[:], 0.0)
+        ones = persistent("ones", P, BF16)
+        nc.vector.memset(ones[:], 1.0)
+
+        w_raw, x_raw = {}, {}
+        x_view = x.rearrange("(s q t) k -> s t q k", s=NS, t=4)
+
+        def load_w(f, g):
+            w_raw[f, g] = keep.tile([P, 4, 512], BF16, name=f"w_raw{f}{g}", align_bytes=64)
+            nc.sync.dma_start(
+                out=w_raw[f, g][:],
+                in_=w[512 * g : 512 * (g + 1), 512 * f : 512 * (f + 1)].rearrange("(p j) c -> p j c", j=4),
+            )
+
+        def load_x(s, t):
+            x_raw[s, t] = persistent(f"x_raw{s}{t}", K, BF16)
+            nc.sync.dma_start(out=x_raw[s, t][:], in_=x_view[s, t])
+
+        load_w(0, 0)
+        load_w(0, 1)
+        for t in range(4):
+            load_x(0, t)
+        nc.sync.dma_start(out=vrow[0:1, :], in_=vgain.rearrange("(o c) -> o c", o=1))
+        load_w(1, 0)
+        load_w(1, 1)
+        for t in range(4):
+            load_x(1, t)
+        load_w(2, 0)
+        load_w(2, 1)
+        b_raw = keep.tile([P, 4, M], U8, name="b_raw", align_bytes=64)
+        nc.sync.dma_start(out=b_raw[:], in_=backup_bytes.rearrange("(t r) k -> r t k", r=P))
+        inv16 = keep.tile([P, NS, 4], BF16, name="inv16", align_bytes=64)
+        nc.sync.dma_start(out=inv16[:], in_=invtemp.rearrange("(s q t) -> q s t", s=NS, t=4))
+        bscale = keep.tile([P, NS, 4], F32, name="bscale", align_bytes=64)
+        nc.sync.dma_start(out=bscale[:], in_=backup_scale.rearrange("o (s q t) -> q (o s) t", s=NS, t=4))
+        pw = keep.tile([P, NF, 2 * A], U8, name="pw", align_bytes=64)
+        nc.sync.dma_start(out=pw[:].bitcast(I32), in_=p_words.rearrange("g p n -> p g n").bitcast(I32))
+        for c in range(4):
+            nc.sync.dma_start(
+                out=ps[32 * c : 32 * c + 4].bitcast(I32),
+                in_=p_scales[:, 4 * c : 4 * c + 4, :].rearrange("g r n -> r g n").bitcast(I32),
+            )
+
+        def copy(engine, out, in_):
+            if engine == "S":
+                nc.scalar.copy(out=out, in_=in_)
+            else:
+                nc.vector.tensor_copy(out=out, in_=in_)
+
+        w_codes, w_scales, w_grp = {}, {}, {}
+
+        def w_interleave(f, g, engine, lo=0, hi=4):
+            if (f, g) not in w_grp:
+                w_grp[f, g] = wstage.tile([P, 2048], BF16, name="w_grp", align_bytes=64)
+            out = w_grp[f, g][:].rearrange("p (t m j) -> p t m j", t=4, j=4)
+            in_ = w_raw[f, g][:].rearrange("p j (m t) -> p t m j", t=4)
+            copy(engine, out[:, lo:hi], in_[:, lo:hi])
+
+        def w_quantize(f, g):
+            w_codes[f, g] = persistent(f"w_codes{f}{g}", 512, U32)
+            w_scales[f, g] = persistent(f"w_scales{f}{g}", 512, U8)
+            nc.vector.quantize_mx(out=w_codes[f, g][:].bitcast(FP8X4), scales=w_scales[f, g][:], in_=w_grp[f, g][:])
+
+        x_codes, x_scales, x_grp = {}, {}, {}
+
+        def x_turn(s, t, engine):
+            bank = new_bank()
+            words = x_raw[s, t][:].bitcast(F32)
+            for g in range(2):
+                for u in range(2):
+                    i = 2 * g + u
+                    nc.tensor.transpose(
+                        bank[:, P * i : P * (i + 1)], words[:, 256 * g + u : 256 * (g + 1) : 2], ident[:]
+                    )
+            x_grp[s, t] = xstage.tile([P, 1024], BF16, name="x_grp", align_bytes=64)
+            copy(
+                engine,
+                x_grp[s, t][:].bitcast(F32).rearrange("p (g q u) -> p g q u", g=2, u=2),
+                bank[:].rearrange("p (g u q) -> p g q u", g=2, u=2),
+            )
+
+        def x_quantize(s, t):
+            x_codes[s, t] = persistent(f"x_codes{s}{t}", 256, U32)
+            x_scales[s, t] = persistent(f"x_scales{s}{t}", 256, U8)
+            nc.vector.quantize_mx(out=x_codes[s, t][:].bitcast(FP8X4), scales=x_scales[s, t][:], in_=x_grp[s, t][:])
+
+        h_grp, hf_codes, hf_scales, hs_codes, hs_scales, hs_grp = {}, {}, {}, {}, {}, {}
+
+        def trunk(s, f, t, engine):
+            bank = new_bank()
+            for j in range(4):
+                cols = slice(P * j, P * (j + 1))
+                for g in range(2):
+                    k_cols = slice(P * g, P * (g + 1))
+                    nc.tensor.matmul_mx(
+                        out=bank[:, cols],
+                        lhsT=w_codes[f, g][:, cols].bitcast(FP8X4),
+                        lhsT_scale=w_scales[f, g][:, cols],
+                        rhs=x_codes[s, t][:, k_cols].bitcast(FP8X4),
+                        rhs_scale=x_scales[s, t][:, k_cols],
+                        start=(g == 0),
+                        stop=(g == 1),
+                    )
+            if (s, f) not in h_grp:
+                h_grp[s, f] = persistent(f"h_grp{s}{f}", 2048, BF16)
+                hf_codes[s, f] = persistent(f"hf_codes{s}{f}", 512, U32)
+                hf_scales[s, f] = persistent(f"hf_scales{s}{f}", 512, U8)
+            out = h_grp[s, f][:, 512 * t : 512 * (t + 1)].rearrange("p (q j) -> p q j", j=4)
+            in_ = bank[:].rearrange("p (j q) -> p q j", j=4)
+            if engine == "S":
+                nc.scalar.activation(out=out, in_=in_, func=ACT.Relu)
+            else:
+                nc.vector.tensor_relu(out=out, in_=in_)
+
+        def hf_quantize(s, f):
+            for h in range(2):
+                nc.vector.quantize_mx(
+                    out=hf_codes[s, f][:, 256 * h : 256 * (h + 1)].bitcast(FP8X4),
+                    scales=hf_scales[s, f][:, 256 * h : 256 * (h + 1)],
+                    in_=h_grp[s, f][:, 1024 * h : 1024 * (h + 1)],
+                )
+
+        h_flat = {}
+
+        def h_flatten(s, f, engine):
+            h_flat[s, f] = hstage.tile([P, 1024], F32, name="h_flat")
+            copy(
+                engine,
+                h_flat[s, f][:].rearrange("p (i u q) -> p i u q", i=4, u=2),
+                h_grp[s, f][:].bitcast(F32).rearrange("p (i q u) -> p i u q", i=4, u=2),
+            )
+
+        def h_turn(f, engines, ss=(0, 1)):
+            banks = {}
+            for s in ss:
+                hs_grp[s, f] = hstage.tile([P, 2048], BF16, name="hs_grp", align_bytes=64)
+                words = h_grp[s, f][:].bitcast(F32)
+                for u in range(2):
+                    banks[s, u] = new_bank()
+                    for t in range(4):
+                        if (s, f) in h_flat:
+                            c0 = 256 * t + P * u
+                            in_ = h_flat[s, f][:, c0 : c0 + P]
+                        else:
+                            in_ = words[:, 256 * t + u : 256 * (t + 1) : 2]
+                        nc.tensor.transpose(banks[s, u][:, P * t : P * (t + 1)], in_, ident[:])
+            for s in ss:
+                for u in range(2):
+                    copy(
+                        engines[2 * s + u],
+                        hs_grp[s, f][:].rearrange("p (m u e t) -> p u m e t", u=2, e=2, t=4)[:, u],
+                        banks[s, u][:].bitcast(BF16).rearrange("p (t m e) -> p m e t", t=4, e=2),
+                    )
+
+        def hs_quantize(s, f):
+            hs_codes[s, f] = persistent(f"hs_codes{s}{f}", 512, U32)
+            hs_scales[s, f] = persistent(f"hs_scales{s}{f}", 512, U8)
+            nc.vector.quantize_mx(
+                out=hs_codes[s, f][:].bitcast(FP8X4), scales=hs_scales[s, f][:], in_=hs_grp[s, f][:]
+            )
+
+        b_wide = keep.tile([P, 4, M], BF16, name="b_wide", align_bytes=64)
+        b_grp = [persistent(f"b_grp{g}", 2048, BF16) for g in range(NS)]
+        b_codes = [persistent(f"b_codes{g}", 512, U32) for g in range(NS)]
+        b_scales = [persistent(f"b_scales{g}", 512, U8) for g in range(NS)]
+
+        def b_widen(t, engine):
+            copy(engine, b_wide[:, t, :], b_raw[:, t, :].bitcast(FP8))
+
+        b_flat = {}
+
+        def b_flatten(t, engine):
+            b_flat[t] = persistent(f"b_flat{t}", 512, F32)
+            copy(
+                engine,
+                b_flat[t][:].rearrange("p (g u q) -> p g u q", g=2, u=2),
+                b_wide[:, t, :].bitcast(F32).rearrange("p (g q u) -> p g u q", g=2, u=2),
+            )
+
+        b_bank = {}
+
+        def b_turn(g, h):
+            bank = new_bank()
+            b_bank[g, h] = bank
+            for a in range(2):
+                words = b_wide[:, 2 * h + a, :].bitcast(F32)
+                for u in range(2):
+                    c0 = 256 * u + P * a
+                    if 2 * h + a in b_flat:
+                        in_ = b_flat[2 * h + a][:, 256 * g + P * u : 256 * g + P * (u + 1)]
+                    else:
+                        in_ = words[:, 256 * g + u : 256 * (g + 1) : 2]
+                    nc.tensor.transpose(bank[:, c0 : c0 + P], in_, ident[:])
+
+        def b_scale(g, h):
+            nc.vector.tensor_tensor(
+                out=b_grp[g][:, 1024 * h : 1024 * (h + 1)].rearrange("p (r u e) -> p r u e", u=2, e=2),
+                in0=b_bank[g, h][:].bitcast(BF16).rearrange("p (u r e) -> p r u e", u=2, e=2),
+                in1=bscale[:, g, :].rearrange("p (u e) -> p u e", e=2).unsqueeze(1).to_broadcast([P, 256, 2, 2]),
+                op=ALU.mult,
+            )
+
+        def b_quantize(g):
+            nc.vector.quantize_mx(out=b_codes[g][:].bitcast(FP8X4), scales=b_scales[g][:], in_=b_grp[g][:])
+
+        inv = persistent("inv", 8, F32)
+        vg = persistent("vg", F, F32)
+
+        def spread_gain():
+            for c in range(NF):
+                bank = new_bank()
+                cols = slice(512 * c, 512 * (c + 1))
+                nc.tensor.matmul(bank[:], lhsT=ones[:], rhs=vrow[:, cols], start=True, stop=True)
+                nc.scalar.copy(out=vg[:, cols], in_=bank[:])
+
+        def load_inv():
+            nc.scalar.copy(out=inv[:], in_=inv16[:].rearrange("p s t -> p (s t)"))
+
+        p_view = policy.rearrange("(s q t) a -> s t q a", s=NS, t=4)
+
+        def policy_unit(s, t, n, engine):
+            bank = new_bank()
+            rows = slice(P * t, P * (t + 1))
+            for f in range(NF):
+                nc.tensor.matmul_mx(
+                    out=bank[:],
+                    lhsT=hf_codes[s, f][:, rows].bitcast(FP8X4),
+                    lhsT_scale=hf_scales[s, f][:, rows],
+                    rhs=pw[:, f, 1024 * n : 1024 * (n + 1)].bitcast(FP4X4),
+                    rhs_scale=ps[:, f, 512 * n : 512 * (n + 1)],
+                    start=(f == 0),
+                    stop=(f == NF - 1),
+                )
+            result = ostage.tile([P, 512], F32, name="p_out")
+            factor = inv[:, 4 * s + t : 4 * s + t + 1]
+            if engine == "S":
+                nc.scalar.activation(out=result[:], in_=bank[:], func=ACT.Copy, scale=factor)
+            else:
+                nc.vector.tensor_scalar(out=result[:], in0=bank[:], scalar1=factor, scalar2=None, op0=ALU.mult)
+            nc.sync.dma_start(out=p_view[s, t, :, 512 * n : 512 * (n + 1)], in_=result[:])
+
+        def value_unit(r, f):
+            bank = new_bank()
+            rows = slice(P * r, P * (r + 1))
+            cols = slice(512 * f, 512 * (f + 1))
+            for s in range(NS):
+                nc.tensor.matmul_mx(
+                    out=bank[:],
+                    lhsT=b_codes[s][:, rows].bitcast(FP8X4),
+                    lhsT_scale=b_scales[s][:, rows],
+                    rhs=hs_codes[s, f][:].bitcast(FP8X4),
+                    rhs_scale=hs_scales[s, f][:],
+                    start=(s == 0),
+                    stop=(s == NS - 1),
+                )
+            result = ostage.tile([P, 512], F32, name="v_out")
+            nc.vector.tensor_tensor(out=result[:], in0=bank[:], in1=vg[:, cols], op=ALU.mult)
+            nc.sync.dma_start(out=value[rows, cols], in_=result[:])
+
+        for g in range(2):
+            w_interleave(0, g, "V")
+        for g in range(2):
+            w_quantize(0, g)
+        for t in range(4):
+            x_turn(0, t, "S")
+        spread_gain()
+        for t in range(4):
+            x_quantize(0, t)
+        for t in range(4):
+            trunk(0, 0, t, "S")
+        for g in range(2):
+            w_interleave(1, g, "V")
+        for g in range(2):
+            w_quantize(1, g)
+        for t in range(4):
+            x_turn(1, t, "S")
+        for t in range(4):
+            x_quantize(1, t)
+        for t in range(4):
+            trunk(0, 1, t, "S")
+        for g in range(2):
+            w_interleave(2, g, "V")
+        for g in range(2):
+            w_quantize(2, g)
+        for t in range(4):
+            trunk(1, 0, t, "S")
+        hf_quantize(0, 0)
+        for t in range(4):
+            b_widen(t, "V")
+        for t in range(4):
+            trunk(1, 1, t, "S")
+        hf_quantize(0, 1)
+        hf_quantize(1, 0)
+        for t in range(4):
+            trunk(0, 2, t, "S")
+        for t in range(4):
+            b_flatten(t, "V")
+        h_flatten(0, 0, "V")
+        h_flatten(1, 0, "V")
+        hf_quantize(1, 1)
+        for t in range(4):
+            trunk(1, 2, t, "SSVS"[t])
+        hf_quantize(0, 2)
+        load_inv()
+        for n in range(2):
+            policy_unit(0, 0, n, "S")
+        h_turn(0, "VSVS")
+        hf_quantize(1, 2)
+        for g in range(2):
+            for h in range(2):
+                b_turn(g, h)
+        h_flatten(0, 1, "S")
+        for g in range(2):
+            for h in range(2):
+                b_scale(g, h)
+        for t in range(1, 4):
+            for n in range(2):
+                policy_unit(0, t, n, "S")
+        h_flatten(1, 1, "S")
+        hs_quantize(0, 0)
+        hs_quantize(1, 0)
+        b_quantize(0)
+        b_quantize(1)
+        for n in range(2):
+            policy_unit(1, 0, n, "S")
+        h_turn(1, "SVSS")
+        h_flatten(0, 2, "S")
+        h_flatten(1, 2, "S")
+        for r in range(4):
+            value_unit(r, 0)
+        for n in range(2):
+            policy_unit(1, 1, n, "S")
+        hs_quantize(0, 1)
+        hs_quantize(1, 1)
+        h_turn(2, "SVSS")
+        for r in range(4):
+            value_unit(r, 1)
+        hs_quantize(0, 2)
+        hs_quantize(1, 2)
+        for n in range(2):
+            policy_unit(1, 2, n, "S")
+        for r in range(4):
+            value_unit(r, 2)
+        for n in range(2):
+            policy_unit(1, 3, n, "SV"[n])

@@ -28,10 +28,8 @@ def tile_policy_value_heads_s8_kernel(
     nc = tc.nc
     with ExitStack() as ctx:
         keep = ctx.enter_context(tc.tile_pool(name="keep", bufs=1))
-        wstage = ctx.enter_context(tc.tile_pool(name="wstage", bufs=3))
-        xstage = ctx.enter_context(tc.tile_pool(name="xstage", bufs=4))
-        hstage = ctx.enter_context(tc.tile_pool(name="hstage", bufs=3))
-        ostage = ctx.enter_context(tc.tile_pool(name="ostage", bufs=4))
+        stage = ctx.enter_context(tc.tile_pool(name="stage", bufs=3))
+        ostage = ctx.enter_context(tc.tile_pool(name="ostage", bufs=6))
         psum = ctx.enter_context(tc.psum_pool(name="psum", bufs=8))
 
         def persistent(name, width, dtype):
@@ -42,13 +40,11 @@ def tile_policy_value_heads_s8_kernel(
 
         ctx.enter_context(tc.manual_schedule())
 
-        warm = persistent("warm", 1, F32)
-        nc.vector.memset(warm[:], 0.0)
-        nc.scalar.activation(out=warm[:], in_=warm[:], func=ACT.Relu)
         ident = persistent("ident", P, F32)
         make_identity(nc, ident[:])
         ps = keep.tile([P, NF, A], U8, name="ps", align_bytes=64)
         nc.gpsimd.memset(ps[:].rearrange("p g n -> p (g n)").bitcast(I32), 0)
+
         vrow = persistent("vrow", F, BF16)
         nc.vector.memset(vrow[:], 0.0)
         ones = persistent("ones", P, BF16)
@@ -68,30 +64,41 @@ def tile_policy_value_heads_s8_kernel(
             x_raw[s, t] = persistent(f"x_raw{s}{t}", K, BF16)
             nc.sync.dma_start(out=x_raw[s, t][:], in_=x_view[s, t])
 
+        bcol = persistent("bcol", 8, F32)
+        nc.scalar.dma_start(out=bcol[:], in_=backup_scale.rearrange("o (p i) -> p (o i)", p=P))
+        nc.scalar.dma_start(out=vrow[0:1, :], in_=vgain.rearrange("(o c) -> o c", o=1))
+        inv16 = keep.tile([P, NS, 4], BF16, name="inv16", align_bytes=64)
+        nc.scalar.dma_start(out=inv16[:], in_=invtemp.rearrange("(s q t) -> q s t", s=NS, t=4))
+
+        b_raw = keep.tile([P, 4, M], U8, name="b_raw", align_bytes=64)
+        pw = keep.tile([P, NF, 2 * A], U8, name="pw", align_bytes=64)
+
+        def load_b():
+            nc.sync.dma_start(out=b_raw[:], in_=backup_bytes.rearrange("(t r) k -> r t k", r=P))
+
+        def load_p():
+            for c in range(4):
+                nc.sync.dma_start(
+                    out=ps[32 * c : 32 * c + 4].bitcast(I32),
+                    in_=p_scales[:, 4 * c : 4 * c + 4, :].rearrange("g r n -> r g n").bitcast(I32),
+                )
+            nc.sync.dma_start(out=pw[:].bitcast(I32), in_=p_words.rearrange("g p n -> p g n").bitcast(I32))
+
         load_w(0, 0)
+        load_x(0, 0)
         load_w(0, 1)
-        for t in range(4):
+        for t in range(1, 4):
             load_x(0, t)
-        nc.sync.dma_start(out=vrow[0:1, :], in_=vgain.rearrange("(o c) -> o c", o=1))
         load_w(1, 0)
+        load_x(1, 0)
+        load_x(1, 1)
         load_w(1, 1)
-        for t in range(4):
-            load_x(1, t)
+        load_x(1, 2)
+        load_x(1, 3)
         load_w(2, 0)
         load_w(2, 1)
-        b_raw = keep.tile([P, 4, M], U8, name="b_raw", align_bytes=64)
-        nc.sync.dma_start(out=b_raw[:], in_=backup_bytes.rearrange("(t r) k -> r t k", r=P))
-        inv16 = keep.tile([P, NS, 4], BF16, name="inv16", align_bytes=64)
-        nc.sync.dma_start(out=inv16[:], in_=invtemp.rearrange("(s q t) -> q s t", s=NS, t=4))
-        bscale = keep.tile([P, NS, 4], F32, name="bscale", align_bytes=64)
-        nc.sync.dma_start(out=bscale[:], in_=backup_scale.rearrange("o (s q t) -> q (o s) t", s=NS, t=4))
-        pw = keep.tile([P, NF, 2 * A], U8, name="pw", align_bytes=64)
-        nc.sync.dma_start(out=pw[:].bitcast(I32), in_=p_words.rearrange("g p n -> p g n").bitcast(I32))
-        for c in range(4):
-            nc.sync.dma_start(
-                out=ps[32 * c : 32 * c + 4].bitcast(I32),
-                in_=p_scales[:, 4 * c : 4 * c + 4, :].rearrange("g r n -> r g n").bitcast(I32),
-            )
+        load_b()
+        load_p()
 
         def copy(engine, out, in_):
             if engine == "S":
@@ -99,299 +106,320 @@ def tile_policy_value_heads_s8_kernel(
             else:
                 nc.vector.tensor_copy(out=out, in_=in_)
 
-        w_codes, w_scales, w_grp = {}, {}, {}
+        def quantize(name, grouped, width):
+            codes = persistent(name + "_codes", width // 4, U32)
+            scales = persistent(name + "_scales", width // 4, U8)
+            nc.vector.quantize_mx(out=codes[:].bitcast(FP8X4), scales=scales[:], in_=grouped)
+            return codes, scales
 
-        def w_interleave(f, g, engine, lo=0, hi=4):
-            if (f, g) not in w_grp:
-                w_grp[f, g] = wstage.tile([P, 2048], BF16, name="w_grp", align_bytes=64)
-            out = w_grp[f, g][:].rearrange("p (t m j) -> p t m j", t=4, j=4)
-            in_ = w_raw[f, g][:].rearrange("p j (m t) -> p t m j", t=4)
-            copy(engine, out[:, lo:hi], in_[:, lo:hi])
+        def interleave(engine, grouped, planes, lo, hi):
+            out = grouped.rearrange("p (c i t) -> p c t i", i=4, t=4)
+            in_ = planes.rearrange("p t (c i) -> p c t i", i=4)
+            copy(engine, out[:, lo // 4 : hi // 4], in_[:, lo // 4 : hi // 4])
 
-        def w_quantize(f, g):
-            w_codes[f, g] = persistent(f"w_codes{f}{g}", 512, U32)
-            w_scales[f, g] = persistent(f"w_scales{f}{g}", 512, U8)
-            nc.vector.quantize_mx(out=w_codes[f, g][:].bitcast(FP8X4), scales=w_scales[f, g][:], in_=w_grp[f, g][:])
+        inv = persistent("inv", 8, F32)
+        vg = persistent("vg", F, F32)
+        bs = persistent("bs", M, F32)
 
-        x_codes, x_scales, x_grp = {}, {}, {}
+        def widen_small():
+            nc.scalar.activation(out=inv[:], in_=inv16[:].rearrange("p s t -> p (s t)"), func=ACT.Copy)
 
-        def x_turn(s, t, engine):
+        def spread(dst, cols, c, engine):
+            per = cols.shape[1]
             bank = new_bank()
-            words = x_raw[s, t][:].bitcast(F32)
-            for g in range(2):
-                for u in range(2):
-                    i = 2 * g + u
-                    nc.tensor.transpose(
-                        bank[:, P * i : P * (i + 1)], words[:, 256 * g + u : 256 * (g + 1) : 2], ident[:]
-                    )
-            x_grp[s, t] = xstage.tile([P, 1024], BF16, name="x_grp", align_bytes=64)
+            for i in range(4):
+                column = cols[:, 4 * c + i : 4 * c + i + 1].to_broadcast([P, P])
+                nc.tensor.transpose(bank[:, P * i : P * (i + 1)], column, ident[:])
             copy(
                 engine,
-                x_grp[s, t][:].bitcast(F32).rearrange("p (g q u) -> p g q u", g=2, u=2),
-                bank[:].rearrange("p (g u q) -> p g q u", g=2, u=2),
+                dst[:].rearrange("p (q i) -> p q i", i=per)[:, :, 4 * c : 4 * c + 4],
+                bank[:].rearrange("p (i q) -> p q i", i=4),
             )
 
-        def x_quantize(s, t):
-            x_codes[s, t] = persistent(f"x_codes{s}{t}", 256, U32)
-            x_scales[s, t] = persistent(f"x_scales{s}{t}", 256, U8)
-            nc.vector.quantize_mx(out=x_codes[s, t][:].bitcast(FP8X4), scales=x_scales[s, t][:], in_=x_grp[s, t][:])
+        gain_bank = {}
 
-        h_grp, hf_codes, hf_scales, hs_codes, hs_scales, hs_grp = {}, {}, {}, {}, {}, {}
+        def gain_mm(c):
+            gain_bank[c] = new_bank()
+            nc.tensor.matmul(
+                gain_bank[c][:], lhsT=ones[:], rhs=vrow[:, 512 * c : 512 * (c + 1)], start=True, stop=True
+            )
 
-        def trunk(s, f, t, engine):
+        def gain_copy(c, engine):
+            copy(engine, vg[:, 512 * c : 512 * (c + 1)], gain_bank[c][:])
+
+        w_mx, w_grp = {}, {}
+
+        def w_interleave(f, g, engine, lo=0, hi=512):
+            if (f, g) not in w_grp:
+                w_grp[f, g] = stage.tile([P, 2048], BF16, name="w_grp", align_bytes=64)
+            interleave(engine, w_grp[f, g][:], w_raw[f, g][:], lo, hi)
+
+        def w_quantize(f, g):
+            w_mx[f, g] = quantize(f"w{f}{g}", w_grp[f, g][:], 2048)
+
+        def turn(sources):
             bank = new_bank()
-            for j in range(4):
-                cols = slice(P * j, P * (j + 1))
-                for g in range(2):
-                    k_cols = slice(P * g, P * (g + 1))
-                    nc.tensor.matmul_mx(
-                        out=bank[:, cols],
-                        lhsT=w_codes[f, g][:, cols].bitcast(FP8X4),
-                        lhsT_scale=w_scales[f, g][:, cols],
-                        rhs=x_codes[s, t][:, k_cols].bitcast(FP8X4),
-                        rhs_scale=x_scales[s, t][:, k_cols],
-                        start=(g == 0),
-                        stop=(g == 1),
-                    )
-            if (s, f) not in h_grp:
-                h_grp[s, f] = persistent(f"h_grp{s}{f}", 2048, BF16)
-                hf_codes[s, f] = persistent(f"hf_codes{s}{f}", 512, U32)
-                hf_scales[s, f] = persistent(f"hf_scales{s}{f}", 512, U8)
-            out = h_grp[s, f][:, 512 * t : 512 * (t + 1)].rearrange("p (q j) -> p q j", j=4)
-            in_ = bank[:].rearrange("p (j q) -> p q j", j=4)
+            for i, words in enumerate(sources):
+                nc.tensor.transpose(bank[:, P * i : P * (i + 1)], words, ident[:])
+            return bank
+
+        def pair_up(engine, grouped, bank):
+            copy(
+                engine,
+                grouped.bitcast(F32).rearrange("p (a q u) -> p a q u", a=2, u=2),
+                bank[:].rearrange("p (a u q) -> p a q u", a=2, u=2),
+            )
+
+        x_bank, x_grp, x_mx = {}, {}, {}
+
+        def x_turn(s, t):
+            words = x_raw[s, t][:].bitcast(F32)
+            x_bank[s, t] = turn([words[:, 256 * g + u : 256 * (g + 1) : 2] for g in range(2) for u in range(2)])
+
+        def x_copy(s, t, engine):
+            x_grp[s, t] = stage.tile([P, 1024], BF16, name="x_grp", align_bytes=64, bufs=4)
+            pair_up(engine, x_grp[s, t][:], x_bank[s, t])
+
+        def x_quantize(s, t):
+            x_mx[s, t] = quantize(f"x{s}{t}", x_grp[s, t][:], 1024)
+
+        h_bank, h_plain = {}, {}
+
+        def trunk(s, t, f, passes=range(2)):
+            if (s, t, f) not in h_bank:
+                h_bank[s, t, f] = new_bank()
+            codes, scales = x_mx[s, t]
+            for g in passes:
+                cols = slice(P * g, P * (g + 1))
+                nc.tensor.matmul_mx(
+                    out=h_bank[s, t, f][:],
+                    lhsT=codes[:, cols].bitcast(FP8X4),
+                    lhsT_scale=scales[:, cols],
+                    rhs=w_mx[f, g][0][:].bitcast(FP8X4),
+                    rhs_scale=w_mx[f, g][1][:],
+                    start=(g == 0),
+                    stop=(g == 1),
+                )
+
+        def relu(s, t, f, engine):
+            if (s, f) not in h_plain:
+                h_plain[s, f] = persistent(f"h_plain{s}{f}", 2048, BF16)
+            out = h_plain[s, f][:, 512 * t : 512 * (t + 1)].rearrange("p (u m e) -> p u m e", u=2, e=2)
+            in_ = h_bank[s, t, f][:].rearrange("p (m u e) -> p u m e", u=2, e=2)
             if engine == "S":
                 nc.scalar.activation(out=out, in_=in_, func=ACT.Relu)
             else:
                 nc.vector.tensor_relu(out=out, in_=in_)
 
+        ht_bank, hf_grp, hf_mx, hs_grp, hs_mx = {}, {}, {}, {}, {}
+
+        def h_turn(s, f, a):
+            words = h_plain[s, f][:].bitcast(F32)
+            ht_bank[s, f, a] = turn([words[:, P * i : P * (i + 1)] for i in range(4 * a, 4 * a + 4)])
+
+        def h_copy(s, f, a, engine):
+            if (s, f) not in hf_grp:
+                hf_grp[s, f] = stage.tile([P, 2048], BF16, name="hf_grp", align_bytes=64)
+            pair_up(engine, hf_grp[s, f][:, 1024 * a : 1024 * (a + 1)], ht_bank[s, f, a])
+
         def hf_quantize(s, f):
-            for h in range(2):
-                nc.vector.quantize_mx(
-                    out=hf_codes[s, f][:, 256 * h : 256 * (h + 1)].bitcast(FP8X4),
-                    scales=hf_scales[s, f][:, 256 * h : 256 * (h + 1)],
-                    in_=h_grp[s, f][:, 1024 * h : 1024 * (h + 1)],
-                )
+            hf_mx[s, f] = quantize(f"hf{s}{f}", hf_grp[s, f][:], 2048)
 
-        h_flat = {}
-
-        def h_flatten(s, f, engine):
-            h_flat[s, f] = hstage.tile([P, 1024], F32, name="h_flat")
-            copy(
-                engine,
-                h_flat[s, f][:].rearrange("p (i u q) -> p i u q", i=4, u=2),
-                h_grp[s, f][:].bitcast(F32).rearrange("p (i q u) -> p i u q", i=4, u=2),
-            )
-
-        def h_turn(f, engines, ss=(0, 1)):
-            banks = {}
-            for s in ss:
-                hs_grp[s, f] = hstage.tile([P, 2048], BF16, name="hs_grp", align_bytes=64)
-                words = h_grp[s, f][:].bitcast(F32)
-                for u in range(2):
-                    banks[s, u] = new_bank()
-                    for t in range(4):
-                        if (s, f) in h_flat:
-                            c0 = 256 * t + P * u
-                            in_ = h_flat[s, f][:, c0 : c0 + P]
-                        else:
-                            in_ = words[:, 256 * t + u : 256 * (t + 1) : 2]
-                        nc.tensor.transpose(banks[s, u][:, P * t : P * (t + 1)], in_, ident[:])
-            for s in ss:
-                for u in range(2):
-                    copy(
-                        engines[2 * s + u],
-                        hs_grp[s, f][:].rearrange("p (m u e t) -> p u m e t", u=2, e=2, t=4)[:, u],
-                        banks[s, u][:].bitcast(BF16).rearrange("p (t m e) -> p m e t", t=4, e=2),
-                    )
+        def h_interleave(s, f, engine, lo=0, hi=512):
+            if (s, f) not in hs_grp:
+                hs_grp[s, f] = stage.tile([P, 2048], BF16, name="hs_grp", align_bytes=64)
+            interleave(engine, hs_grp[s, f][:], h_plain[s, f][:].rearrange("p (t c) -> p t c", t=4), lo, hi)
 
         def hs_quantize(s, f):
-            hs_codes[s, f] = persistent(f"hs_codes{s}{f}", 512, U32)
-            hs_scales[s, f] = persistent(f"hs_scales{s}{f}", 512, U8)
-            nc.vector.quantize_mx(
-                out=hs_codes[s, f][:].bitcast(FP8X4), scales=hs_scales[s, f][:], in_=hs_grp[s, f][:]
-            )
+            hs_mx[s, f] = quantize(f"hs{s}{f}", hs_grp[s, f][:], 2048)
 
-        b_wide = keep.tile([P, 4, M], BF16, name="b_wide", align_bytes=64)
-        b_grp = [persistent(f"b_grp{g}", 2048, BF16) for g in range(NS)]
-        b_codes = [persistent(f"b_codes{g}", 512, U32) for g in range(NS)]
-        b_scales = [persistent(f"b_scales{g}", 512, U8) for g in range(NS)]
+        b16, b_bank, b_mx = {}, {}, {}
+        b_grp = [persistent(f"b_grp{s}", 2048, BF16) for s in range(NS)]
 
-        def b_widen(t, engine):
-            copy(engine, b_wide[:, t, :], b_raw[:, t, :].bitcast(FP8))
+        def b_scale(r):
+            b16[r] = persistent(f"b16{r}", M, BF16)
+            nc.vector.tensor_tensor(out=b16[r][:], in0=b_raw[:, r, :].bitcast(FP8), in1=bs[:], op=ALU.mult)
 
-        b_flat = {}
+        def b_turn(s, a):
+            sources = []
+            for r in (2 * a, 2 * a + 1):
+                words = b16[r][:].bitcast(F32)
+                sources.extend(words[:, 256 * s + u : 256 * (s + 1) : 2] for u in range(2))
+            b_bank[s, a] = turn(sources)
 
-        def b_flatten(t, engine):
-            b_flat[t] = persistent(f"b_flat{t}", 512, F32)
-            copy(
-                engine,
-                b_flat[t][:].rearrange("p (g u q) -> p g u q", g=2, u=2),
-                b_wide[:, t, :].bitcast(F32).rearrange("p (g q u) -> p g u q", g=2, u=2),
-            )
+        def b_copy(s, a, engine):
+            pair_up(engine, b_grp[s][:, 1024 * a : 1024 * (a + 1)], b_bank[s, a])
 
-        b_bank = {}
-
-        def b_turn(g, h):
-            bank = new_bank()
-            b_bank[g, h] = bank
-            for a in range(2):
-                words = b_wide[:, 2 * h + a, :].bitcast(F32)
-                for u in range(2):
-                    c0 = 256 * u + P * a
-                    if 2 * h + a in b_flat:
-                        in_ = b_flat[2 * h + a][:, 256 * g + P * u : 256 * g + P * (u + 1)]
-                    else:
-                        in_ = words[:, 256 * g + u : 256 * (g + 1) : 2]
-                    nc.tensor.transpose(bank[:, c0 : c0 + P], in_, ident[:])
-
-        def b_scale(g, h):
-            nc.vector.tensor_tensor(
-                out=b_grp[g][:, 1024 * h : 1024 * (h + 1)].rearrange("p (r u e) -> p r u e", u=2, e=2),
-                in0=b_bank[g, h][:].bitcast(BF16).rearrange("p (u r e) -> p r u e", u=2, e=2),
-                in1=bscale[:, g, :].rearrange("p (u e) -> p u e", e=2).unsqueeze(1).to_broadcast([P, 256, 2, 2]),
-                op=ALU.mult,
-            )
-
-        def b_quantize(g):
-            nc.vector.quantize_mx(out=b_codes[g][:].bitcast(FP8X4), scales=b_scales[g][:], in_=b_grp[g][:])
-
-        inv = persistent("inv", 8, F32)
-        vg = persistent("vg", F, F32)
-
-        def spread_gain():
-            for c in range(NF):
-                bank = new_bank()
-                cols = slice(512 * c, 512 * (c + 1))
-                nc.tensor.matmul(bank[:], lhsT=ones[:], rhs=vrow[:, cols], start=True, stop=True)
-                nc.scalar.copy(out=vg[:, cols], in_=bank[:])
-
-        def load_inv():
-            nc.scalar.copy(out=inv[:], in_=inv16[:].rearrange("p s t -> p (s t)"))
+        def b_quantize(s):
+            b_mx[s] = quantize(f"b{s}", b_grp[s][:], 2048)
 
         p_view = policy.rearrange("(s q t) a -> s t q a", s=NS, t=4)
+        p_bank, v_bank = {}, {}
 
-        def policy_unit(s, t, n, engine):
-            bank = new_bank()
+        def policy_mm(s, t, n):
+            p_bank[s, t, n] = new_bank()
             rows = slice(P * t, P * (t + 1))
             for f in range(NF):
                 nc.tensor.matmul_mx(
-                    out=bank[:],
-                    lhsT=hf_codes[s, f][:, rows].bitcast(FP8X4),
-                    lhsT_scale=hf_scales[s, f][:, rows],
+                    out=p_bank[s, t, n][:],
+                    lhsT=hf_mx[s, f][0][:, rows].bitcast(FP8X4),
+                    lhsT_scale=hf_mx[s, f][1][:, rows],
                     rhs=pw[:, f, 1024 * n : 1024 * (n + 1)].bitcast(FP4X4),
                     rhs_scale=ps[:, f, 512 * n : 512 * (n + 1)],
                     start=(f == 0),
                     stop=(f == NF - 1),
                 )
+
+        def policy_out(s, t, n, engine):
             result = ostage.tile([P, 512], F32, name="p_out")
             factor = inv[:, 4 * s + t : 4 * s + t + 1]
             if engine == "S":
-                nc.scalar.activation(out=result[:], in_=bank[:], func=ACT.Copy, scale=factor)
+                nc.scalar.activation(out=result[:], in_=p_bank[s, t, n][:], func=ACT.Copy, scale=factor)
             else:
-                nc.vector.tensor_scalar(out=result[:], in0=bank[:], scalar1=factor, scalar2=None, op0=ALU.mult)
+                nc.vector.tensor_scalar(
+                    out=result[:], in0=p_bank[s, t, n][:], scalar1=factor, scalar2=None, op0=ALU.mult
+                )
             nc.sync.dma_start(out=p_view[s, t, :, 512 * n : 512 * (n + 1)], in_=result[:])
 
-        def value_unit(r, f):
-            bank = new_bank()
+        def value_mm(r, f):
+            v_bank[r, f] = new_bank()
             rows = slice(P * r, P * (r + 1))
-            cols = slice(512 * f, 512 * (f + 1))
             for s in range(NS):
                 nc.tensor.matmul_mx(
-                    out=bank[:],
-                    lhsT=b_codes[s][:, rows].bitcast(FP8X4),
-                    lhsT_scale=b_scales[s][:, rows],
-                    rhs=hs_codes[s, f][:].bitcast(FP8X4),
-                    rhs_scale=hs_scales[s, f][:],
+                    out=v_bank[r, f][:],
+                    lhsT=b_mx[s][0][:, rows].bitcast(FP8X4),
+                    lhsT_scale=b_mx[s][1][:, rows],
+                    rhs=hs_mx[s, f][0][:].bitcast(FP8X4),
+                    rhs_scale=hs_mx[s, f][1][:],
                     start=(s == 0),
                     stop=(s == NS - 1),
                 )
-            result = ostage.tile([P, 512], F32, name="v_out")
-            nc.vector.tensor_tensor(out=result[:], in0=bank[:], in1=vg[:, cols], op=ALU.mult)
-            nc.sync.dma_start(out=value[rows, cols], in_=result[:])
 
-        for g in range(2):
-            w_interleave(0, g, "V")
-        for g in range(2):
-            w_quantize(0, g)
-        for t in range(4):
-            x_turn(0, t, "S")
-        spread_gain()
-        for t in range(4):
-            x_quantize(0, t)
-        for t in range(4):
-            trunk(0, 0, t, "S")
-        for g in range(2):
-            w_interleave(1, g, "V")
-        for g in range(2):
-            w_quantize(1, g)
-        for t in range(4):
-            x_turn(1, t, "S")
-        for t in range(4):
-            x_quantize(1, t)
-        for t in range(4):
-            trunk(0, 1, t, "S")
-        for g in range(2):
-            w_interleave(2, g, "V")
-        for g in range(2):
-            w_quantize(2, g)
-        for t in range(4):
-            trunk(1, 0, t, "S")
-        hf_quantize(0, 0)
-        for t in range(4):
-            b_widen(t, "V")
-        for t in range(4):
-            trunk(1, 1, t, "S")
-        hf_quantize(0, 1)
-        hf_quantize(1, 0)
-        for t in range(4):
-            trunk(0, 2, t, "S")
-        for t in range(4):
-            b_flatten(t, "V")
-        h_flatten(0, 0, "V")
-        h_flatten(1, 0, "V")
-        hf_quantize(1, 1)
-        for t in range(4):
-            trunk(1, 2, t, "SSVS"[t])
-        hf_quantize(0, 2)
-        load_inv()
-        for n in range(2):
-            policy_unit(0, 0, n, "S")
-        h_turn(0, "VSVS")
-        hf_quantize(1, 2)
-        for g in range(2):
-            for h in range(2):
-                b_turn(g, h)
-        h_flatten(0, 1, "S")
-        for g in range(2):
-            for h in range(2):
-                b_scale(g, h)
-        for t in range(1, 4):
+        def value_out(r, f):
+            cols = slice(512 * f, 512 * (f + 1))
+            result = ostage.tile([P, 512], F32, name="v_out")
+            nc.vector.tensor_tensor(
+                out=result[:].rearrange("p (m u e) -> p m u e", u=2, e=2),
+                in0=v_bank[r, f][:].rearrange("p (u m e) -> p m u e", u=2, e=2),
+                in1=vg[:, cols].rearrange("p (m u e) -> p m u e", u=2, e=2),
+                op=ALU.mult,
+            )
+            nc.sync.dma_start(out=value[P * r : P * (r + 1), cols], in_=result[:])
+
+        def trunk_run(s, f, engines, tiles=range(4)):
+            for t in tiles:
+                trunk(s, t, f)
+                relu(s, t, f, engines[t])
+
+        def h_run(s, f, engines):
+            for a in range(2):
+                h_turn(s, f, a)
+                h_copy(s, f, a, engines[a])
+
+        def b_run(s, engines):
+            for a in range(2):
+                b_turn(s, a)
+                b_copy(s, a, engines[a])
+
+        def x_run(s, tiles, engine):
+            for t in tiles:
+                x_turn(s, t)
+                x_copy(s, t, engine)
+
+        def policy_run(s, t, engines="SS"):
             for n in range(2):
-                policy_unit(0, t, n, "S")
-        h_flatten(1, 1, "S")
+                policy_mm(s, t, n)
+                policy_out(s, t, n, engines[n])
+
+        def value_run(f, rows):
+            for r in rows:
+                value_mm(r, f)
+                value_out(r, f)
+
+        widen_small()
+        for c in range(2):
+            spread(bs, bcol, c, "S")
+        w_interleave(0, 0, "V")
+        x_run(0, [0], "S")
+        for c in range(3):
+            gain_mm(c)
+            gain_copy(c, "S")
+        w_quantize(0, 0)
+        w_interleave(0, 1, "V")
+        x_quantize(0, 0)
+        w_quantize(0, 1)
+        x_run(0, [1, 2], "S")
+        trunk_run(0, 0, "SSSS", [0])
+        x_run(0, [3], "S")
+        x_quantize(0, 1)
+        x_quantize(0, 2)
+        w_interleave(1, 0, "V")
+        x_quantize(0, 3)
+        w_quantize(1, 0)
+        trunk_run(0, 0, "SSSS", [1, 2])
+        x_run(1, [0, 1], "S")
+        trunk_run(0, 0, "SSSS", [3])
+        w_interleave(1, 1, "V")
+        x_quantize(1, 0)
+        x_quantize(1, 1)
+        w_quantize(1, 1)
+        x_run(1, [2, 3], "S")
+        trunk_run(1, 0, "SSSS", range(2))
+        w_interleave(2, 0, "V")
+        x_quantize(1, 2)
+        x_quantize(1, 3)
+        w_quantize(2, 0)
+        w_interleave(2, 1, "V")
+        trunk_run(0, 1, "SSSS")
+        h_run(0, 0, "SS")
+        w_quantize(2, 1)
+        trunk_run(1, 0, "SSSS", range(2, 4))
+        trunk_run(0, 2, "SSSS")
+        b_scale(0)
+        hf_quantize(0, 0)
+        b_scale(1)
+        b_scale(2)
+        h_run(0, 1, "VV")
+        trunk_run(1, 1, "SSSS", range(2))
+        h_run(0, 2, "VV")
+        hf_quantize(0, 1)
+        hf_quantize(0, 2)
+        trunk_run(1, 1, "SSSS", range(2, 4))
+        b_scale(3)
+        h_run(1, 0, "SS")
+        policy_run(0, 0)
+        h_interleave(0, 0, "V")
+        h_interleave(1, 0, "V")
+        b_run(0, "SS")
+        policy_run(0, 1)
         hs_quantize(0, 0)
         hs_quantize(1, 0)
+        b_run(1, "SS")
         b_quantize(0)
+        hf_quantize(1, 0)
+        trunk_run(1, 2, "SSSS")
         b_quantize(1)
-        for n in range(2):
-            policy_unit(1, 0, n, "S")
-        h_turn(1, "SVSS")
-        h_flatten(0, 2, "S")
-        h_flatten(1, 2, "S")
-        for r in range(4):
-            value_unit(r, 0)
-        for n in range(2):
-            policy_unit(1, 1, n, "S")
+        h_interleave(0, 1, "V")
+        h_interleave(1, 1, "V")
+        h_run(1, 1, "SS")
+        value_run(0, range(2))
+        policy_run(0, 2)
         hs_quantize(0, 1)
         hs_quantize(1, 1)
-        h_turn(2, "SVSS")
-        for r in range(4):
-            value_unit(r, 1)
+        h_run(1, 2, "SS")
+        value_run(0, range(2, 4))
+        hf_quantize(1, 1)
+        hf_quantize(1, 2)
+        h_interleave(0, 2, "V")
+        policy_run(0, 3)
+        value_run(1, range(2))
+        h_interleave(1, 2, "V")
         hs_quantize(0, 2)
+        policy_run(1, 0)
         hs_quantize(1, 2)
-        for n in range(2):
-            policy_unit(1, 2, n, "S")
-        for r in range(4):
-            value_unit(r, 2)
-        for n in range(2):
-            policy_unit(1, 3, n, "SV"[n])
+        value_run(1, range(2, 4))
+        policy_run(1, 1)
+        value_run(2, range(2))
+        policy_run(1, 2)
+        value_run(2, range(2, 4))
+        policy_run(1, 3, "SV")

@@ -45,11 +45,6 @@ def tile_policy_value_heads_s8_kernel(
         ps = keep.tile([P, NF, A], U8, name="ps", align_bytes=64)
         nc.gpsimd.memset(ps[:].rearrange("p g n -> p (g n)").bitcast(I32), 0)
 
-        vrow = persistent("vrow", F, BF16)
-        nc.vector.memset(vrow[:], 0.0)
-        ones = persistent("ones", P, BF16)
-        nc.vector.memset(ones[:], 1.0)
-
         w_raw, x_raw = {}, {}
         x_view = x.rearrange("(s q t) k -> s t q k", s=NS, t=4)
 
@@ -66,12 +61,16 @@ def tile_policy_value_heads_s8_kernel(
 
         bcol = persistent("bcol", 8, F32)
         nc.scalar.dma_start(out=bcol[:], in_=backup_scale.rearrange("o (p i) -> p (o i)", p=P))
-        nc.scalar.dma_start(out=vrow[0:1, :], in_=vgain.rearrange("(o c) -> o c", o=1))
         inv16 = keep.tile([P, NS, 4], BF16, name="inv16", align_bytes=64)
         nc.scalar.dma_start(out=inv16[:], in_=invtemp.rearrange("(s q t) -> q s t", s=NS, t=4))
 
         b_raw = keep.tile([P, 4, M], U8, name="b_raw", align_bytes=64)
         pw = keep.tile([P, NF, 2 * A], U8, name="pw", align_bytes=64)
+
+        vg = persistent("vg", F, BF16)
+
+        def load_gain():
+            nc.sync.dma_start(out=vg[:], in_=vgain.partition_broadcast(P))
 
         def load_b():
             nc.sync.dma_start(out=b_raw[:], in_=backup_bytes.rearrange("(t r) k -> r t k", r=P))
@@ -85,20 +84,20 @@ def tile_policy_value_heads_s8_kernel(
             nc.sync.dma_start(out=pw[:].bitcast(I32), in_=p_words.rearrange("g p n -> p g n").bitcast(I32))
 
         load_w(0, 0)
-        load_x(0, 0)
-        load_w(0, 1)
-        for t in range(1, 4):
+        for t in range(4):
             load_x(0, t)
-        load_w(1, 0)
+        load_w(0, 1)
         load_x(1, 0)
         load_x(1, 1)
-        load_w(1, 1)
+        load_w(1, 0)
         load_x(1, 2)
         load_x(1, 3)
+        load_w(1, 1)
         load_w(2, 0)
         load_w(2, 1)
         load_b()
         load_p()
+        load_gain()
 
         def copy(engine, out, in_):
             if engine == "S":
@@ -118,7 +117,6 @@ def tile_policy_value_heads_s8_kernel(
             copy(engine, out[:, lo // 4 : hi // 4], in_[:, lo // 4 : hi // 4])
 
         inv = persistent("inv", 8, F32)
-        vg = persistent("vg", F, F32)
         bs = persistent("bs", M, F32)
 
         def widen_small():
@@ -135,17 +133,6 @@ def tile_policy_value_heads_s8_kernel(
                 dst[:].rearrange("p (q i) -> p q i", i=per)[:, :, 4 * c : 4 * c + 4],
                 bank[:].rearrange("p (i q) -> p q i", i=4),
             )
-
-        gain_bank = {}
-
-        def gain_mm(c):
-            gain_bank[c] = new_bank()
-            nc.tensor.matmul(
-                gain_bank[c][:], lhsT=ones[:], rhs=vrow[:, 512 * c : 512 * (c + 1)], start=True, stop=True
-            )
-
-        def gain_copy(c, engine):
-            copy(engine, vg[:, 512 * c : 512 * (c + 1)], gain_bank[c][:])
 
         w_mx, w_grp = {}, {}
 
@@ -233,18 +220,29 @@ def tile_policy_value_heads_s8_kernel(
         def hs_quantize(s, f):
             hs_mx[s, f] = quantize(f"hs{s}{f}", hs_grp[s, f][:], 2048)
 
-        b16, b_bank, b_mx = {}, {}, {}
+        b16, b_flat, b_bank, b_mx = {}, {}, {}, {}
         b_grp = [persistent(f"b_grp{s}", 2048, BF16) for s in range(NS)]
 
         def b_scale(r):
             b16[r] = persistent(f"b16{r}", M, BF16)
             nc.vector.tensor_tensor(out=b16[r][:], in0=b_raw[:, r, :].bitcast(FP8), in1=bs[:], op=ALU.mult)
 
+        def b_flatten(r, engine):
+            b_flat[r] = persistent(f"b_flat{r}", 512, F32)
+            copy(
+                engine,
+                b_flat[r][:].rearrange("p (s u q) -> p s u q", s=2, u=2),
+                b16[r][:].bitcast(F32).rearrange("p (s q u) -> p s u q", s=2, u=2),
+            )
+
         def b_turn(s, a):
             sources = []
             for r in (2 * a, 2 * a + 1):
-                words = b16[r][:].bitcast(F32)
-                sources.extend(words[:, 256 * s + u : 256 * (s + 1) : 2] for u in range(2))
+                if r in b_flat:
+                    sources.extend(b_flat[r][:, 256 * s + P * u : 256 * s + P * (u + 1)] for u in range(2))
+                else:
+                    words = b16[r][:].bitcast(F32)
+                    sources.extend(words[:, 256 * s + u : 256 * (s + 1) : 2] for u in range(2))
             b_bank[s, a] = turn(sources)
 
         def b_copy(s, a, engine):
@@ -280,6 +278,29 @@ def tile_policy_value_heads_s8_kernel(
                     out=result[:], in0=p_bank[s, t, n][:], scalar1=factor, scalar2=None, op0=ALU.mult
                 )
             nc.sync.dma_start(out=p_view[s, t, :, 512 * n : 512 * (n + 1)], in_=result[:])
+
+        def policy_half(s, t, c, engine):
+            bank = new_bank()
+            rows = slice(P * t, P * (t + 1))
+            for j in range(2):
+                n0 = 256 * c + P * j
+                for f in range(NF):
+                    nc.tensor.matmul_mx(
+                        out=bank[:, P * j : P * (j + 1)],
+                        lhsT=hf_mx[s, f][0][:, rows].bitcast(FP8X4),
+                        lhsT_scale=hf_mx[s, f][1][:, rows],
+                        rhs=pw[:, f, 2 * n0 : 2 * (n0 + P)].bitcast(FP4X4),
+                        rhs_scale=ps[:, f, n0 : n0 + P],
+                        start=(f == 0),
+                        stop=(f == NF - 1),
+                    )
+            result = ostage.tile([P, 256], F32, name="p_half", bufs=2)
+            factor = inv[:, 4 * s + t : 4 * s + t + 1]
+            if engine == "S":
+                nc.scalar.activation(out=result[:], in_=bank[:, 0:256], func=ACT.Copy, scale=factor)
+            else:
+                nc.vector.tensor_scalar(out=result[:], in0=bank[:, 0:256], scalar1=factor, scalar2=None, op0=ALU.mult)
+            nc.sync.dma_start(out=p_view[s, t, :, 256 * c : 256 * (c + 1)], in_=result[:])
 
         def value_mm(r, f):
             v_bank[r, f] = new_bank()
@@ -340,86 +361,92 @@ def tile_policy_value_heads_s8_kernel(
         for c in range(2):
             spread(bs, bcol, c, "S")
         w_interleave(0, 0, "V")
-        x_run(0, [0], "S")
-        for c in range(3):
-            gain_mm(c)
-            gain_copy(c, "S")
+        x_run(0, range(4), "S")
         w_quantize(0, 0)
-        w_interleave(0, 1, "V")
-        x_quantize(0, 0)
-        w_quantize(0, 1)
-        x_run(0, [1, 2], "S")
-        trunk_run(0, 0, "SSSS", [0])
-        x_run(0, [3], "S")
-        x_quantize(0, 1)
-        x_quantize(0, 2)
-        w_interleave(1, 0, "V")
+        for t in range(3):
+            x_quantize(0, t)
+        w_interleave(0, 1, "S", 352, 512)
+        w_interleave(0, 1, "V", 0, 352)
         x_quantize(0, 3)
-        w_quantize(1, 0)
-        trunk_run(0, 0, "SSSS", [1, 2])
+        w_quantize(0, 1)
+        for t in range(3):
+            trunk(0, t, 0, [0])
         x_run(1, [0, 1], "S")
-        trunk_run(0, 0, "SSSS", [3])
-        w_interleave(1, 1, "V")
+        trunk(0, 3, 0, [0])
+        for t in range(4):
+            trunk(0, t, 0, [1])
+        for t in range(2):
+            relu(0, t, 0, "S")
+        w_interleave(1, 0, "V")
         x_quantize(1, 0)
         x_quantize(1, 1)
-        w_quantize(1, 1)
+        w_quantize(1, 0)
         x_run(1, [2, 3], "S")
+        for t in range(2, 4):
+            relu(0, t, 0, "S")
         trunk_run(1, 0, "SSSS", range(2))
-        w_interleave(2, 0, "V")
+        w_interleave(1, 1, "V")
         x_quantize(1, 2)
         x_quantize(1, 3)
-        w_quantize(2, 0)
-        w_interleave(2, 1, "V")
-        trunk_run(0, 1, "SSSS")
+        w_quantize(1, 1)
         h_run(0, 0, "SS")
-        w_quantize(2, 1)
         trunk_run(1, 0, "SSSS", range(2, 4))
-        trunk_run(0, 2, "SSSS")
-        b_scale(0)
-        hf_quantize(0, 0)
-        b_scale(1)
-        b_scale(2)
-        h_run(0, 1, "VV")
+        w_interleave(2, 0, "V")
+        w_interleave(2, 1, "V")
+        w_quantize(2, 0)
+        w_quantize(2, 1)
+        trunk_run(0, 1, "SSSS")
         trunk_run(1, 1, "SSSS", range(2))
-        h_run(0, 2, "VV")
-        hf_quantize(0, 1)
-        hf_quantize(0, 2)
-        trunk_run(1, 1, "SSSS", range(2, 4))
+        hf_quantize(0, 0)
+        trunk_run(0, 2, "SSSS")
+        for r in range(3):
+            b_scale(r)
+        h_run(0, 1, "VV")
         b_scale(3)
-        h_run(1, 0, "SS")
-        policy_run(0, 0)
+        trunk_run(1, 1, "SSSS", range(2, 4))
+        h_run(0, 2, "VS")
+        hf_quantize(0, 1)
+        trunk_run(1, 2, "SSSS")
+        hf_quantize(0, 2)
         h_interleave(0, 0, "V")
         h_interleave(1, 0, "V")
         b_run(0, "SS")
-        policy_run(0, 1)
+        policy_run(0, 0)
         hs_quantize(0, 0)
         hs_quantize(1, 0)
         b_run(1, "SS")
         b_quantize(0)
-        hf_quantize(1, 0)
-        trunk_run(1, 2, "SSSS")
-        b_quantize(1)
         h_interleave(0, 1, "V")
+        policy_run(0, 1)
+        b_quantize(1)
         h_interleave(1, 1, "V")
+        h_run(1, 0, "SS")
         h_run(1, 1, "SS")
-        value_run(0, range(2))
-        policy_run(0, 2)
         hs_quantize(0, 1)
+        value_run(0, range(2))
+        policy_mm(0, 2, 0)
+        policy_out(0, 2, 0, "S")
         hs_quantize(1, 1)
+        hf_quantize(1, 0)
         h_run(1, 2, "SS")
-        value_run(0, range(2, 4))
         hf_quantize(1, 1)
-        hf_quantize(1, 2)
-        h_interleave(0, 2, "V")
-        policy_run(0, 3)
-        value_run(1, range(2))
+        value_run(0, range(2, 4))
+        h_interleave(0, 2, "S")
         h_interleave(1, 2, "V")
-        hs_quantize(0, 2)
-        policy_run(1, 0)
+        policy_mm(0, 2, 1)
+        policy_out(0, 2, 1, "S")
+        hf_quantize(1, 2)
+        value_run(1, range(2))
+        policy_run(0, 3)
         hs_quantize(1, 2)
+        hs_quantize(0, 2)
         value_run(1, range(2, 4))
-        policy_run(1, 1)
+        policy_run(1, 0)
         value_run(2, range(2))
-        policy_run(1, 2)
+        policy_run(1, 1)
         value_run(2, range(2, 4))
-        policy_run(1, 3, "SV")
+        policy_run(1, 2)
+        policy_mm(1, 3, 0)
+        policy_out(1, 3, 0, "S")
+        policy_half(1, 3, 2, "V")
+        policy_half(1, 3, 3, "S")

@@ -49,7 +49,7 @@ def tile_policy_value_heads_s8_kernel(
         x_view = x.rearrange("(s q t) k -> s t q k", s=NS, t=4)
 
         def load_w(f, g):
-            w_raw[f, g] = keep.tile([P, 4, 512], BF16, name=f"w_raw{f}{g}", align_bytes=64)
+            w_raw[f, g] = stage.tile([P, 4, 512], BF16, name=f"w_raw{f}{g}", tag="plain", align_bytes=64, bufs=8)
             nc.sync.dma_start(
                 out=w_raw[f, g][:],
                 in_=w[512 * g : 512 * (g + 1), 512 * f : 512 * (f + 1)].rearrange("(p j) c -> p j c", j=4),
@@ -59,8 +59,6 @@ def tile_policy_value_heads_s8_kernel(
             x_raw[s, t] = persistent(f"x_raw{s}{t}", K, BF16)
             nc.sync.dma_start(out=x_raw[s, t][:], in_=x_view[s, t])
 
-        bcol = persistent("bcol", 8, F32)
-        nc.scalar.dma_start(out=bcol[:], in_=backup_scale.rearrange("o (p i) -> p (o i)", p=P))
         inv16 = keep.tile([P, NS, 4], BF16, name="inv16", align_bytes=64)
         nc.scalar.dma_start(out=inv16[:], in_=invtemp.rearrange("(s q t) -> q s t", s=NS, t=4))
 
@@ -68,6 +66,11 @@ def tile_policy_value_heads_s8_kernel(
         pw = keep.tile([P, NF, 2 * A], U8, name="pw", align_bytes=64)
 
         vg = persistent("vg", F, BF16)
+
+        bs = persistent("bs", M, F32)
+
+        def load_b_scale():
+            nc.sync.dma_start(out=bs[:], in_=backup_scale.rearrange("o k -> (o k)").partition_broadcast(P))
 
         def load_gain():
             nc.sync.dma_start(out=vg[:], in_=vgain.partition_broadcast(P))
@@ -96,6 +99,7 @@ def tile_policy_value_heads_s8_kernel(
         load_w(2, 0)
         load_w(2, 1)
         load_b()
+        load_b_scale()
         load_p()
         load_gain()
 
@@ -117,22 +121,9 @@ def tile_policy_value_heads_s8_kernel(
             copy(engine, out[:, lo // 4 : hi // 4], in_[:, lo // 4 : hi // 4])
 
         inv = persistent("inv", 8, F32)
-        bs = persistent("bs", M, F32)
 
         def widen_small():
             nc.scalar.activation(out=inv[:], in_=inv16[:].rearrange("p s t -> p (s t)"), func=ACT.Copy)
-
-        def spread(dst, cols, c, engine):
-            per = cols.shape[1]
-            bank = new_bank()
-            for i in range(4):
-                column = cols[:, 4 * c + i : 4 * c + i + 1].to_broadcast([P, P])
-                nc.tensor.transpose(bank[:, P * i : P * (i + 1)], column, ident[:])
-            copy(
-                engine,
-                dst[:].rearrange("p (q i) -> p q i", i=per)[:, :, 4 * c : 4 * c + 4],
-                bank[:].rearrange("p (i q) -> p q i", i=4),
-            )
 
         w_mx, w_grp = {}, {}
 
@@ -190,7 +181,9 @@ def tile_policy_value_heads_s8_kernel(
 
         def relu(s, t, f, engine):
             if (s, f) not in h_plain:
-                h_plain[s, f] = persistent(f"h_plain{s}{f}", 2048, BF16)
+                h_plain[s, f] = stage.tile(
+                    [P, 2048], BF16, name=f"h_plain{s}{f}", tag="plain", align_bytes=64, bufs=8
+                )
             out = h_plain[s, f][:, 512 * t : 512 * (t + 1)].rearrange("p (u m e) -> p u m e", u=2, e=2)
             in_ = h_bank[s, t, f][:].rearrange("p (m u e) -> p u m e", u=2, e=2)
             if engine == "S":
@@ -220,29 +213,18 @@ def tile_policy_value_heads_s8_kernel(
         def hs_quantize(s, f):
             hs_mx[s, f] = quantize(f"hs{s}{f}", hs_grp[s, f][:], 2048)
 
-        b16, b_flat, b_bank, b_mx = {}, {}, {}, {}
+        b16, b_bank, b_mx = {}, {}, {}
         b_grp = [persistent(f"b_grp{s}", 2048, BF16) for s in range(NS)]
 
         def b_scale(r):
             b16[r] = persistent(f"b16{r}", M, BF16)
             nc.vector.tensor_tensor(out=b16[r][:], in0=b_raw[:, r, :].bitcast(FP8), in1=bs[:], op=ALU.mult)
 
-        def b_flatten(r, engine):
-            b_flat[r] = persistent(f"b_flat{r}", 512, F32)
-            copy(
-                engine,
-                b_flat[r][:].rearrange("p (s u q) -> p s u q", s=2, u=2),
-                b16[r][:].bitcast(F32).rearrange("p (s q u) -> p s u q", s=2, u=2),
-            )
-
         def b_turn(s, a):
             sources = []
             for r in (2 * a, 2 * a + 1):
-                if r in b_flat:
-                    sources.extend(b_flat[r][:, 256 * s + P * u : 256 * s + P * (u + 1)] for u in range(2))
-                else:
-                    words = b16[r][:].bitcast(F32)
-                    sources.extend(words[:, 256 * s + u : 256 * (s + 1) : 2] for u in range(2))
+                words = b16[r][:].bitcast(F32)
+                sources.extend(words[:, 256 * s + u : 256 * (s + 1) : 2] for u in range(2))
             b_bank[s, a] = turn(sources)
 
         def b_copy(s, a, engine):
@@ -252,7 +234,7 @@ def tile_policy_value_heads_s8_kernel(
             b_mx[s] = quantize(f"b{s}", b_grp[s][:], 2048)
 
         p_view = policy.rearrange("(s q t) a -> s t q a", s=NS, t=4)
-        p_bank, v_bank = {}, {}
+        p_bank, p_rows, v_bank = {}, {}, {}
 
         def policy_mm(s, t, n):
             p_bank[s, t, n] = new_bank()
@@ -268,16 +250,21 @@ def tile_policy_value_heads_s8_kernel(
                     stop=(f == NF - 1),
                 )
 
-        def policy_out(s, t, n, engine):
-            result = ostage.tile([P, 512], F32, name="p_out")
+        def policy_out(s, t, n, engine, whole_rows=True):
+            if (s, t) not in p_rows:
+                p_rows[s, t] = ostage.tile([P, A], F32, name="p_out", bufs=3)
+            result = p_rows[s, t][:, 512 * n : 512 * (n + 1)]
             factor = inv[:, 4 * s + t : 4 * s + t + 1]
             if engine == "S":
-                nc.scalar.activation(out=result[:], in_=p_bank[s, t, n][:], func=ACT.Copy, scale=factor)
+                nc.scalar.activation(out=result, in_=p_bank[s, t, n][:], func=ACT.Copy, scale=factor)
             else:
                 nc.vector.tensor_scalar(
-                    out=result[:], in0=p_bank[s, t, n][:], scalar1=factor, scalar2=None, op0=ALU.mult
+                    out=result, in0=p_bank[s, t, n][:], scalar1=factor, scalar2=None, op0=ALU.mult
                 )
-            nc.sync.dma_start(out=p_view[s, t, :, 512 * n : 512 * (n + 1)], in_=result[:])
+            if not whole_rows:
+                nc.sync.dma_start(out=p_view[s, t, :, 512 * n : 512 * (n + 1)], in_=result)
+            elif n == 1:
+                nc.sync.dma_start(out=p_view[s, t], in_=p_rows[s, t][:])
 
         def policy_half(s, t, c, engine):
             bank = new_bank()
@@ -357,39 +344,42 @@ def tile_policy_value_heads_s8_kernel(
                 value_mm(r, f)
                 value_out(r, f)
 
+        def policy_one(s, t, n, whole_rows=True):
+            policy_mm(s, t, n)
+            policy_out(s, t, n, "S", whole_rows)
+
+        def w_shared(f, g):
+            w_interleave(f, g, "S", 352, 512)
+            w_interleave(f, g, "V", 0, 352)
+
         widen_small()
-        for c in range(2):
-            spread(bs, bcol, c, "S")
-        w_interleave(0, 0, "V")
+        w_shared(0, 0)
         x_run(0, range(4), "S")
         w_quantize(0, 0)
         for t in range(3):
             x_quantize(0, t)
-        w_interleave(0, 1, "S", 352, 512)
-        w_interleave(0, 1, "V", 0, 352)
+        w_shared(0, 1)
         x_quantize(0, 3)
         w_quantize(0, 1)
         for t in range(3):
             trunk(0, t, 0, [0])
         x_run(1, [0, 1], "S")
+        w_interleave(1, 0, "V")
         trunk(0, 3, 0, [0])
         for t in range(4):
             trunk(0, t, 0, [1])
-        for t in range(2):
+        for t in range(3):
             relu(0, t, 0, "S")
-        w_interleave(1, 0, "V")
         x_quantize(1, 0)
-        x_quantize(1, 1)
         w_quantize(1, 0)
+        x_quantize(1, 1)
         x_run(1, [2, 3], "S")
-        for t in range(2, 4):
-            relu(0, t, 0, "S")
+        relu(0, 3, 0, "S")
         trunk_run(1, 0, "SSSS", range(2))
         w_interleave(1, 1, "V")
         x_quantize(1, 2)
         x_quantize(1, 3)
         w_quantize(1, 1)
-        h_run(0, 0, "SS")
         trunk_run(1, 0, "SSSS", range(2, 4))
         w_interleave(2, 0, "V")
         w_interleave(2, 1, "V")
@@ -397,56 +387,60 @@ def tile_policy_value_heads_s8_kernel(
         w_quantize(2, 1)
         trunk_run(0, 1, "SSSS")
         trunk_run(1, 1, "SSSS", range(2))
-        hf_quantize(0, 0)
-        trunk_run(0, 2, "SSSS")
-        for r in range(3):
-            b_scale(r)
-        h_run(0, 1, "VV")
-        b_scale(3)
-        trunk_run(1, 1, "SSSS", range(2, 4))
-        h_run(0, 2, "VS")
-        hf_quantize(0, 1)
-        trunk_run(1, 2, "SSSS")
-        hf_quantize(0, 2)
         h_interleave(0, 0, "V")
-        h_interleave(1, 0, "V")
-        b_run(0, "SS")
+        h_run(0, 0, "VV")
+        h_run(0, 1, "VS")
+        trunk_run(0, 2, "SSSS")
+        b_scale(0)
+        hf_quantize(0, 0)
+        hf_quantize(0, 1)
+        trunk_run(1, 1, "SSSS", range(2, 4))
+        b_scale(1)
+        h_run(0, 2, "VS")
+        h_run(1, 0, "SS")
+        hf_quantize(0, 2)
+        trunk_run(1, 2, "SSSS", range(2))
+        b_scale(2)
+        b_scale(3)
         policy_run(0, 0)
+        h_interleave(1, 0, "V")
+        policy_one(0, 1, 0, False)
+        b_run(0, "SS")
         hs_quantize(0, 0)
         hs_quantize(1, 0)
-        b_run(1, "SS")
-        b_quantize(0)
+        policy_one(0, 1, 1, False)
+        trunk_run(1, 2, "SSSS", range(2, 4))
         h_interleave(0, 1, "V")
-        policy_run(0, 1)
-        b_quantize(1)
+        b_quantize(0)
+        b_run(1, "SS")
         h_interleave(1, 1, "V")
-        h_run(1, 0, "SS")
-        h_run(1, 1, "SS")
+        policy_run(0, 2)
+        b_quantize(1)
         hs_quantize(0, 1)
-        value_run(0, range(2))
-        policy_mm(0, 2, 0)
-        policy_out(0, 2, 0, "S")
+        h_run(1, 1, "SS")
+        h_run(1, 2, "SS")
         hs_quantize(1, 1)
         hf_quantize(1, 0)
-        h_run(1, 2, "SS")
+        value_run(0, range(2))
+        policy_one(0, 3, 0, False)
         hf_quantize(1, 1)
-        value_run(0, range(2, 4))
-        h_interleave(0, 2, "S")
-        h_interleave(1, 2, "V")
-        policy_mm(0, 2, 1)
-        policy_out(0, 2, 1, "S")
         hf_quantize(1, 2)
+        value_run(0, range(2, 4))
+        policy_one(0, 3, 1, False)
+        h_interleave(1, 2, "S")
+        h_interleave(0, 2, "V")
         value_run(1, range(2))
-        policy_run(0, 3)
-        hs_quantize(1, 2)
+        policy_one(1, 0, 0, False)
         hs_quantize(0, 2)
+        hs_quantize(1, 2)
         value_run(1, range(2, 4))
-        policy_run(1, 0)
+        policy_one(1, 0, 1, False)
+        policy_one(1, 1, 0, False)
+        policy_one(1, 1, 1, False)
         value_run(2, range(2))
-        policy_run(1, 1)
+        policy_one(1, 2, 0, False)
         value_run(2, range(2, 4))
-        policy_run(1, 2)
-        policy_mm(1, 3, 0)
-        policy_out(1, 3, 0, "S")
+        policy_one(1, 2, 1, False)
+        policy_one(1, 3, 0, False)
         policy_half(1, 3, 2, "V")
         policy_half(1, 3, 3, "S")

@@ -62,21 +62,20 @@ def tile_policy_value_heads_s8_kernel(
         inv16 = keep.tile([P, NS, 4], BF16, name="inv16", align_bytes=64)
         nc.scalar.dma_start(out=inv16[:], in_=invtemp.rearrange("(s q t) -> q s t", s=NS, t=4))
 
-        b_raw = keep.tile([P, 4, M], U8, name="b_raw", align_bytes=64)
+        bscale = keep.tile([P, NS, 4], F32, name="bscale", align_bytes=64)
+        nc.scalar.dma_start(out=bscale[:], in_=backup_scale.rearrange("o (s q t) -> q (o s) t", s=NS, t=4))
+
+        b_raw = {}
         pw = keep.tile([P, NF, 2 * A], U8, name="pw", align_bytes=64)
 
         vg = persistent("vg", F, BF16)
 
-        bs = persistent("bs", M, F32)
-
-        def load_b_scale():
-            nc.sync.dma_start(out=bs[:], in_=backup_scale.rearrange("o k -> (o k)").partition_broadcast(P))
-
         def load_gain():
             nc.sync.dma_start(out=vg[:], in_=vgain.partition_broadcast(P))
 
-        def load_b():
-            nc.sync.dma_start(out=b_raw[:], in_=backup_bytes.rearrange("(t r) k -> r t k", r=P))
+        def load_b(r):
+            b_raw[r] = persistent(f"b_raw{r}", M, U8)
+            nc.sync.dma_start(out=b_raw[r][:], in_=backup_bytes[P * r : P * (r + 1), :])
 
         def load_p():
             for c in range(4):
@@ -86,6 +85,8 @@ def tile_policy_value_heads_s8_kernel(
                 )
             nc.sync.dma_start(out=pw[:].bitcast(I32), in_=p_words.rearrange("g p n -> p g n").bitcast(I32))
 
+        for r in range(4):
+            load_b(r)
         load_w(0, 0)
         for t in range(4):
             load_x(0, t)
@@ -98,8 +99,6 @@ def tile_policy_value_heads_s8_kernel(
         load_w(1, 1)
         load_w(2, 0)
         load_w(2, 1)
-        load_b()
-        load_b_scale()
         load_p()
         load_gain()
 
@@ -213,22 +212,32 @@ def tile_policy_value_heads_s8_kernel(
         def hs_quantize(s, f):
             hs_mx[s, f] = quantize(f"hs{s}{f}", hs_grp[s, f][:], 2048)
 
-        b16, b_bank, b_mx = {}, {}, {}
-        b_grp = [persistent(f"b_grp{s}", 2048, BF16) for s in range(NS)]
+        b_wide, b_bank, b_grp, b_mx = {}, {}, {}, {}
+        b_turned = persistent("b_turned", NS * 2048, BF16)
 
-        def b_scale(r):
-            b16[r] = persistent(f"b16{r}", M, BF16)
-            nc.vector.tensor_tensor(out=b16[r][:], in0=b_raw[:, r, :].bitcast(FP8), in1=bs[:], op=ALU.mult)
+        def b_widen(r):
+            b_wide[r] = persistent(f"b_wide{r}", M, BF16)
+            nc.vector.tensor_copy(out=b_wide[r][:], in_=b_raw[r][:].bitcast(FP8))
 
-        def b_turn(s, a):
-            sources = []
-            for r in (2 * a, 2 * a + 1):
-                words = b16[r][:].bitcast(F32)
-                sources.extend(words[:, 256 * s + u : 256 * (s + 1) : 2] for u in range(2))
-            b_bank[s, a] = turn(sources)
+        def b_turn(r):
+            words = b_wide[r][:].bitcast(F32)
+            b_bank[r] = turn([words[:, 256 * s + u : 256 * (s + 1) : 2] for s in range(NS) for u in range(2)])
 
-        def b_copy(s, a, engine):
-            pair_up(engine, b_grp[s][:, 1024 * a : 1024 * (a + 1)], b_bank[s, a])
+        def b_copy(r, engine):
+            copy(
+                engine,
+                b_turned[:].bitcast(F32).rearrange("p (s r q u) -> p r s q u", s=NS, r=4, u=2)[:, r],
+                b_bank[r][:].rearrange("p (s u q) -> p s q u", s=NS, u=2),
+            )
+
+        def b_scale(s):
+            b_grp[s] = persistent(f"b_grp{s}", 2048, BF16)
+            nc.vector.tensor_tensor(
+                out=b_grp[s][:].rearrange("p (r t) -> p r t", t=4),
+                in0=b_turned[:, 2048 * s : 2048 * (s + 1)].rearrange("p (r t) -> p r t", t=4),
+                in1=bscale[:, s, :].unsqueeze(1).to_broadcast([P, 512, 4]),
+                op=ALU.mult,
+            )
 
         def b_quantize(s):
             b_mx[s] = quantize(f"b{s}", b_grp[s][:], 2048)
@@ -324,11 +333,6 @@ def tile_policy_value_heads_s8_kernel(
                 h_turn(s, f, a)
                 h_copy(s, f, a, engines[a])
 
-        def b_run(s, engines):
-            for a in range(2):
-                b_turn(s, a)
-                b_copy(s, a, engines[a])
-
         def x_run(s, tiles, engine):
             for t in tiles:
                 x_turn(s, t)
@@ -348,33 +352,40 @@ def tile_policy_value_heads_s8_kernel(
             policy_mm(s, t, n)
             policy_out(s, t, n, "S", whole_rows)
 
-        def w_shared(f, g):
-            w_interleave(f, g, "S", 352, 512)
-            w_interleave(f, g, "V", 0, 352)
+        def w_shared(f, g, cut):
+            w_interleave(f, g, "S", cut, 512)
+            w_interleave(f, g, "V", 0, cut)
 
         widen_small()
-        w_shared(0, 0)
+        for r in range(4):
+            b_widen(r)
+            b_turn(r)
+            b_copy(r, "S")
+        w_interleave(0, 0, "V")
         x_run(0, range(4), "S")
         w_quantize(0, 0)
-        for t in range(3):
+        for t in range(2):
             x_quantize(0, t)
-        w_shared(0, 1)
-        x_quantize(0, 3)
+        w_shared(0, 1, 384)
+        for t in range(2, 4):
+            x_quantize(0, t)
         w_quantize(0, 1)
-        for t in range(3):
+        for t in range(2):
             trunk(0, t, 0, [0])
         x_run(1, [0, 1], "S")
-        w_interleave(1, 0, "V")
-        trunk(0, 3, 0, [0])
+        w_shared(1, 0, 384)
+        for t in range(2, 4):
+            trunk(0, t, 0, [0])
         for t in range(4):
             trunk(0, t, 0, [1])
-        for t in range(3):
+        for t in range(2):
             relu(0, t, 0, "S")
         x_quantize(1, 0)
-        w_quantize(1, 0)
         x_quantize(1, 1)
+        w_quantize(1, 0)
         x_run(1, [2, 3], "S")
-        relu(0, 3, 0, "S")
+        for t in range(2, 4):
+            relu(0, t, 0, "S")
         trunk_run(1, 0, "SSSS", range(2))
         w_interleave(1, 1, "V")
         x_quantize(1, 2)
@@ -391,31 +402,26 @@ def tile_policy_value_heads_s8_kernel(
         h_run(0, 0, "VV")
         h_run(0, 1, "VS")
         trunk_run(0, 2, "SSSS")
-        b_scale(0)
         hf_quantize(0, 0)
         hf_quantize(0, 1)
         trunk_run(1, 1, "SSSS", range(2, 4))
-        b_scale(1)
+        b_scale(0)
         h_run(0, 2, "VS")
         h_run(1, 0, "SS")
         hf_quantize(0, 2)
-        trunk_run(1, 2, "SSSS", range(2))
-        b_scale(2)
-        b_scale(3)
-        policy_run(0, 0)
+        trunk_run(1, 2, "SSSS")
         h_interleave(1, 0, "V")
-        policy_one(0, 1, 0, False)
-        b_run(0, "SS")
+        b_scale(1)
+        policy_run(0, 0)
+        h_interleave(0, 1, "S", 0, 256)
         hs_quantize(0, 0)
         hs_quantize(1, 0)
-        policy_one(0, 1, 1, False)
-        trunk_run(1, 2, "SSSS", range(2, 4))
-        h_interleave(0, 1, "V")
         b_quantize(0)
-        b_run(1, "SS")
+        b_quantize(1)
+        policy_run(0, 1)
+        h_interleave(0, 1, "S", 256, 512)
         h_interleave(1, 1, "V")
         policy_run(0, 2)
-        b_quantize(1)
         hs_quantize(0, 1)
         h_run(1, 1, "SS")
         h_run(1, 2, "SS")
@@ -424,23 +430,24 @@ def tile_policy_value_heads_s8_kernel(
         value_run(0, range(2))
         policy_one(0, 3, 0, False)
         hf_quantize(1, 1)
-        hf_quantize(1, 2)
         value_run(0, range(2, 4))
+        hf_quantize(1, 2)
         policy_one(0, 3, 1, False)
-        h_interleave(1, 2, "S")
-        h_interleave(0, 2, "V")
+        h_interleave(1, 2, "S", 0, 256)
         value_run(1, range(2))
+        h_interleave(0, 2, "V")
         policy_one(1, 0, 0, False)
+        h_interleave(1, 2, "S", 256, 512)
+        value_run(1, range(2, 4))
         hs_quantize(0, 2)
         hs_quantize(1, 2)
-        value_run(1, range(2, 4))
         policy_one(1, 0, 1, False)
         policy_one(1, 1, 0, False)
         policy_one(1, 1, 1, False)
-        value_run(2, range(2))
         policy_one(1, 2, 0, False)
-        value_run(2, range(2, 4))
+        value_run(2, range(2))
         policy_one(1, 2, 1, False)
+        value_run(2, range(2, 4))
         policy_one(1, 3, 0, False)
         policy_half(1, 3, 2, "V")
         policy_half(1, 3, 3, "S")

@@ -60,10 +60,12 @@ def tile_policy_value_heads_s8_kernel(
             nc.sync.dma_start(out=x_raw[s, t][:], in_=x_view[s, t])
 
         inv16 = keep.tile([P, NS, 4], BF16, name="inv16", align_bytes=64)
-        nc.scalar.dma_start(out=inv16[:], in_=invtemp.rearrange("(s q t) -> q s t", s=NS, t=4))
 
         bscale = keep.tile([P, NS, 4], F32, name="bscale", align_bytes=64)
-        nc.scalar.dma_start(out=bscale[:], in_=backup_scale.rearrange("o (s q t) -> q (o s) t", s=NS, t=4))
+
+        def load_factors():
+            nc.sync.dma_start(out=bscale[:], in_=backup_scale.rearrange("o (s q t) -> q (o s) t", s=NS, t=4))
+            nc.sync.dma_start(out=inv16[:], in_=invtemp.rearrange("(s q t) -> q s t", s=NS, t=4))
 
         b_raw = {}
         pw = keep.tile([P, NF, 2 * A], U8, name="pw", align_bytes=64)
@@ -99,6 +101,7 @@ def tile_policy_value_heads_s8_kernel(
         load_w(1, 1)
         load_w(2, 0)
         load_w(2, 1)
+        load_factors()
         load_p()
         load_gain()
 
@@ -108,11 +111,18 @@ def tile_policy_value_heads_s8_kernel(
             else:
                 nc.vector.tensor_copy(out=out, in_=in_)
 
-        def quantize(name, grouped, width):
-            codes = persistent(name + "_codes", width // 4, U32)
-            scales = persistent(name + "_scales", width // 4, U8)
-            nc.vector.quantize_mx(out=codes[:].bitcast(FP8X4), scales=scales[:], in_=grouped)
-            return codes, scales
+        def mx_tiles(name, columns):
+            return persistent(name + "_codes", columns, U32), persistent(name + "_scales", columns, U8)
+
+        def quantize(mx, grouped, lo, hi):
+            codes, scales = mx
+            nc.vector.quantize_mx(
+                out=codes[:, lo:hi].bitcast(FP8X4), scales=scales[:, lo:hi], in_=grouped[:, 4 * lo : 4 * hi]
+            )
+
+        def operand(mx, lo, width):
+            codes, scales = mx
+            return codes[:, lo : lo + width].bitcast(FP8X4), scales[:, lo : lo + width]
 
         def interleave(engine, grouped, planes, lo, hi):
             out = grouped.rearrange("p (c i t) -> p c t i", i=4, t=4)
@@ -121,18 +131,19 @@ def tile_policy_value_heads_s8_kernel(
 
         inv = persistent("inv", 8, F32)
 
-        def widen_small():
-            nc.scalar.activation(out=inv[:], in_=inv16[:].rearrange("p s t -> p (s t)"), func=ACT.Copy)
+        def widen_inv():
+            nc.scalar.copy(out=inv[:], in_=inv16[:].rearrange("p s t -> p (s t)"))
 
         w_mx, w_grp = {}, {}
 
         def w_interleave(f, g, engine, lo=0, hi=512):
-            if (f, g) not in w_grp:
-                w_grp[f, g] = stage.tile([P, 2048], BF16, name="w_grp", align_bytes=64)
-            interleave(engine, w_grp[f, g][:], w_raw[f, g][:], lo, hi)
+            if f not in w_grp:
+                w_grp[f] = stage.tile([P, 4096], BF16, name="w_grp", align_bytes=64, bufs=2)
+                w_mx[f] = mx_tiles(f"w{f}", 1024)
+            interleave(engine, w_grp[f][:, 2048 * g : 2048 * (g + 1)], w_raw[f, g][:], lo, hi)
 
-        def w_quantize(f, g):
-            w_mx[f, g] = quantize(f"w{f}{g}", w_grp[f, g][:], 2048)
+        def w_quantize(f, first, last):
+            quantize(w_mx[f], w_grp[f], 512 * first, 512 * (last + 1))
 
         def turn(sources):
             bank = new_bank()
@@ -158,25 +169,27 @@ def tile_policy_value_heads_s8_kernel(
             pair_up(engine, x_grp[s, t][:], x_bank[s, t])
 
         def x_quantize(s, t):
-            x_mx[s, t] = quantize(f"x{s}{t}", x_grp[s, t][:], 1024)
+            x_mx[s, t] = mx_tiles(f"x{s}{t}", 256)
+            quantize(x_mx[s, t], x_grp[s, t], 0, 256)
+
+        def product(out, stationary, moving, index, count):
+            nc.tensor.matmul_mx(
+                out=out,
+                lhsT=stationary[0],
+                lhsT_scale=stationary[1],
+                rhs=moving[0],
+                rhs_scale=moving[1],
+                start=(index == 0),
+                stop=(index == count - 1),
+            )
 
         h_bank, h_plain = {}, {}
 
         def trunk(s, t, f, passes=range(2)):
             if (s, t, f) not in h_bank:
                 h_bank[s, t, f] = new_bank()
-            codes, scales = x_mx[s, t]
             for g in passes:
-                cols = slice(P * g, P * (g + 1))
-                nc.tensor.matmul_mx(
-                    out=h_bank[s, t, f][:],
-                    lhsT=codes[:, cols].bitcast(FP8X4),
-                    lhsT_scale=scales[:, cols],
-                    rhs=w_mx[f, g][0][:].bitcast(FP8X4),
-                    rhs_scale=w_mx[f, g][1][:],
-                    start=(g == 0),
-                    stop=(g == 1),
-                )
+                product(h_bank[s, t, f][:], operand(x_mx[s, t], P * g, P), operand(w_mx[f], 512 * g, 512), g, 2)
 
         def relu(s, t, f, engine):
             if (s, f) not in h_plain:
@@ -197,27 +210,42 @@ def tile_policy_value_heads_s8_kernel(
             ht_bank[s, f, a] = turn([words[:, P * i : P * (i + 1)] for i in range(4 * a, 4 * a + 4)])
 
         def h_copy(s, f, a, engine):
-            if (s, f) not in hf_grp:
-                hf_grp[s, f] = stage.tile([P, 2048], BF16, name="hf_grp", align_bytes=64)
-            pair_up(engine, hf_grp[s, f][:, 1024 * a : 1024 * (a + 1)], ht_bank[s, f, a])
+            pair, half = divmod(NF * s + f, 2)
+            if pair not in hf_grp:
+                hf_grp[pair] = stage.tile([P, 4096], BF16, name="hf_grp", align_bytes=64, bufs=2)
+                hf_mx[pair] = mx_tiles(f"hf{pair}", 1024)
+            first = 2048 * half + 1024 * a
+            pair_up(engine, hf_grp[pair][:, first : first + 1024], ht_bank[s, f, a])
 
-        def hf_quantize(s, f):
-            hf_mx[s, f] = quantize(f"hf{s}{f}", hf_grp[s, f][:], 2048)
+        def hf_quantize(s, f, count=1):
+            pair, half = divmod(NF * s + f, 2)
+            quantize(hf_mx[pair], hf_grp[pair], 512 * half, 512 * (half + count))
+
+        def hf_operand(s, f, t):
+            pair, half = divmod(NF * s + f, 2)
+            return operand(hf_mx[pair], 512 * half + P * t, P)
 
         def h_interleave(s, f, engine, lo=0, hi=512):
-            if (s, f) not in hs_grp:
-                hs_grp[s, f] = stage.tile([P, 2048], BF16, name="hs_grp", align_bytes=64)
-            interleave(engine, hs_grp[s, f][:], h_plain[s, f][:].rearrange("p (t c) -> p t c", t=4), lo, hi)
+            if f not in hs_grp:
+                hs_grp[f] = stage.tile([P, 4096], BF16, name="hs_grp", align_bytes=64, bufs=2)
+                hs_mx[f] = mx_tiles(f"hs{f}", 1024)
+            planes = h_plain[s, f][:].rearrange("p (t c) -> p t c", t=4)
+            interleave(engine, hs_grp[f][:, 2048 * s : 2048 * (s + 1)], planes, lo, hi)
 
-        def hs_quantize(s, f):
-            hs_mx[s, f] = quantize(f"hs{s}{f}", hs_grp[s, f][:], 2048)
+        def hs_quantize(f):
+            quantize(hs_mx[f], hs_grp[f], 0, 1024)
 
-        b_wide, b_bank, b_grp, b_mx = {}, {}, {}, {}
+        b_wide, b_bank = {}, {}
+        b_grp = persistent("b_grp", NS * 2048, BF16)
+        b_mx = mx_tiles("b", 1024)
         b_turned = persistent("b_turned", NS * 2048, BF16)
 
-        def b_widen(r):
+        def b_widen(r, engine):
             b_wide[r] = persistent(f"b_wide{r}", M, BF16)
-            nc.vector.tensor_copy(out=b_wide[r][:], in_=b_raw[r][:].bitcast(FP8))
+            if engine == "S":
+                nc.scalar.activation(out=b_wide[r][:], in_=b_raw[r][:].bitcast(FP8), func=ACT.Copy)
+            else:
+                nc.vector.tensor_copy(out=b_wide[r][:], in_=b_raw[r][:].bitcast(FP8))
 
         def b_turn(r):
             words = b_wide[r][:].bitcast(F32)
@@ -230,34 +258,28 @@ def tile_policy_value_heads_s8_kernel(
                 b_bank[r][:].rearrange("p (s u q) -> p s q u", s=NS, u=2),
             )
 
-        def b_scale(s):
-            b_grp[s] = persistent(f"b_grp{s}", 2048, BF16)
+        def b_scale(s, a):
+            cols = slice(2048 * s + 1024 * a, 2048 * s + 1024 * (a + 1))
             nc.vector.tensor_tensor(
-                out=b_grp[s][:].rearrange("p (r t) -> p r t", t=4),
-                in0=b_turned[:, 2048 * s : 2048 * (s + 1)].rearrange("p (r t) -> p r t", t=4),
-                in1=bscale[:, s, :].unsqueeze(1).to_broadcast([P, 512, 4]),
+                out=b_grp[:, cols].rearrange("p (r t) -> p r t", t=4),
+                in0=b_turned[:, cols].rearrange("p (r t) -> p r t", t=4),
+                in1=bscale[:, s, :].unsqueeze(1).to_broadcast([P, 256, 4]),
                 op=ALU.mult,
             )
 
-        def b_quantize(s):
-            b_mx[s] = quantize(f"b{s}", b_grp[s][:], 2048)
+        def b_quantize():
+            quantize(b_mx, b_grp, 0, 1024)
 
         p_view = policy.rearrange("(s q t) a -> s t q a", s=NS, t=4)
         p_bank, p_rows, v_bank = {}, {}, {}
 
+        def p_operand(f, lo, width):
+            return pw[:, f, 2 * lo : 2 * (lo + width)].bitcast(FP4X4), ps[:, f, lo : lo + width]
+
         def policy_mm(s, t, n):
             p_bank[s, t, n] = new_bank()
-            rows = slice(P * t, P * (t + 1))
             for f in range(NF):
-                nc.tensor.matmul_mx(
-                    out=p_bank[s, t, n][:],
-                    lhsT=hf_mx[s, f][0][:, rows].bitcast(FP8X4),
-                    lhsT_scale=hf_mx[s, f][1][:, rows],
-                    rhs=pw[:, f, 1024 * n : 1024 * (n + 1)].bitcast(FP4X4),
-                    rhs_scale=ps[:, f, 512 * n : 512 * (n + 1)],
-                    start=(f == 0),
-                    stop=(f == NF - 1),
-                )
+                product(p_bank[s, t, n][:], hf_operand(s, f, t), p_operand(f, 512 * n, 512), f, NF)
 
         def policy_out(s, t, n, engine, whole_rows=True):
             if (s, t) not in p_rows:
@@ -277,19 +299,10 @@ def tile_policy_value_heads_s8_kernel(
 
         def policy_half(s, t, c, engine):
             bank = new_bank()
-            rows = slice(P * t, P * (t + 1))
             for j in range(2):
-                n0 = 256 * c + P * j
                 for f in range(NF):
-                    nc.tensor.matmul_mx(
-                        out=bank[:, P * j : P * (j + 1)],
-                        lhsT=hf_mx[s, f][0][:, rows].bitcast(FP8X4),
-                        lhsT_scale=hf_mx[s, f][1][:, rows],
-                        rhs=pw[:, f, 2 * n0 : 2 * (n0 + P)].bitcast(FP4X4),
-                        rhs_scale=ps[:, f, n0 : n0 + P],
-                        start=(f == 0),
-                        stop=(f == NF - 1),
-                    )
+                    moving = p_operand(f, 256 * c + P * j, P)
+                    product(bank[:, P * j : P * (j + 1)], hf_operand(s, f, t), moving, f, NF)
             result = ostage.tile([P, 256], F32, name="p_half", bufs=2)
             factor = inv[:, 4 * s + t : 4 * s + t + 1]
             if engine == "S":
@@ -300,17 +313,8 @@ def tile_policy_value_heads_s8_kernel(
 
         def value_mm(r, f):
             v_bank[r, f] = new_bank()
-            rows = slice(P * r, P * (r + 1))
             for s in range(NS):
-                nc.tensor.matmul_mx(
-                    out=v_bank[r, f][:],
-                    lhsT=b_mx[s][0][:, rows].bitcast(FP8X4),
-                    lhsT_scale=b_mx[s][1][:, rows],
-                    rhs=hs_mx[s, f][0][:].bitcast(FP8X4),
-                    rhs_scale=hs_mx[s, f][1][:],
-                    start=(s == 0),
-                    stop=(s == NS - 1),
-                )
+                product(v_bank[r, f][:], operand(b_mx, 512 * s + P * r, P), operand(hs_mx[f], 512 * s, 512), s, NS)
 
         def value_out(r, f):
             cols = slice(512 * f, 512 * (f + 1))
@@ -352,24 +356,28 @@ def tile_policy_value_heads_s8_kernel(
             policy_mm(s, t, n)
             policy_out(s, t, n, "S", whole_rows)
 
+        def value_one(r, f):
+            value_mm(r, f)
+            value_out(r, f)
+
         def w_shared(f, g, cut):
             w_interleave(f, g, "S", cut, 512)
             w_interleave(f, g, "V", 0, cut)
 
-        widen_small()
         for r in range(4):
-            b_widen(r)
+            b_widen(r, "VVVS"[r])
+        for r in range(4):
             b_turn(r)
-            b_copy(r, "S")
+            b_copy(r, "VSSS"[r])
         w_interleave(0, 0, "V")
         x_run(0, range(4), "S")
-        w_quantize(0, 0)
+        w_quantize(0, 0, 0)
         for t in range(2):
             x_quantize(0, t)
         w_shared(0, 1, 384)
         for t in range(2, 4):
             x_quantize(0, t)
-        w_quantize(0, 1)
+        w_quantize(0, 1, 1)
         for t in range(2):
             trunk(0, t, 0, [0])
         x_run(1, [0, 1], "S")
@@ -382,68 +390,73 @@ def tile_policy_value_heads_s8_kernel(
             relu(0, t, 0, "S")
         x_quantize(1, 0)
         x_quantize(1, 1)
-        w_quantize(1, 0)
+        w_quantize(1, 0, 0)
         x_run(1, [2, 3], "S")
         for t in range(2, 4):
             relu(0, t, 0, "S")
         trunk_run(1, 0, "SSSS", range(2))
-        w_interleave(1, 1, "V")
+        w_interleave(1, 1, "V", 0, 256)
         x_quantize(1, 2)
         x_quantize(1, 3)
-        w_quantize(1, 1)
+        w_interleave(1, 1, "V", 256, 512)
         trunk_run(1, 0, "SSSS", range(2, 4))
-        w_interleave(2, 0, "V")
+        w_interleave(2, 0, "V", 0, 128)
+        w_quantize(1, 1, 1)
+        w_interleave(2, 0, "V", 128, 512)
         w_interleave(2, 1, "V")
-        w_quantize(2, 0)
-        w_quantize(2, 1)
-        trunk_run(0, 1, "SSSS")
+        w_quantize(2, 0, 0)
+        w_quantize(2, 1, 1)
+        for t in range(4):
+            trunk(0, t, 1, [0])
+        for t in range(4):
+            trunk(0, t, 1, [1])
+            relu(0, t, 1, "S")
         trunk_run(1, 1, "SSSS", range(2))
         h_interleave(0, 0, "V")
         h_run(0, 0, "VV")
         h_run(0, 1, "VS")
         trunk_run(0, 2, "SSSS")
-        hf_quantize(0, 0)
-        hf_quantize(0, 1)
+        b_scale(0, 0)
+        hf_quantize(0, 0, 2)
         trunk_run(1, 1, "SSSS", range(2, 4))
-        b_scale(0)
         h_run(0, 2, "VS")
         h_run(1, 0, "SS")
+        b_scale(0, 1)
         hf_quantize(0, 2)
+        widen_inv()
         trunk_run(1, 2, "SSSS")
         h_interleave(1, 0, "V")
-        b_scale(1)
-        policy_run(0, 0)
-        h_interleave(0, 1, "S", 0, 256)
-        hs_quantize(0, 0)
-        hs_quantize(1, 0)
-        b_quantize(0)
-        b_quantize(1)
-        policy_run(0, 1)
-        h_interleave(0, 1, "S", 256, 512)
-        h_interleave(1, 1, "V")
-        policy_run(0, 2)
-        hs_quantize(0, 1)
+        b_scale(1, 0)
+        b_scale(1, 1)
+        for n in range(2):
+            policy_one(0, 0, n, False)
+        hs_quantize(0)
+        b_quantize()
+        for t in range(1, 3):
+            for n in range(2):
+                policy_one(0, t, n, False)
+        hf_quantize(1, 0)
+        h_interleave(0, 1, "V")
         h_run(1, 1, "SS")
         h_run(1, 2, "SS")
-        hs_quantize(1, 1)
-        hf_quantize(1, 0)
+        h_interleave(1, 1, "S", 0, 256)
         value_run(0, range(2))
+        hf_quantize(1, 1, 2)
         policy_one(0, 3, 0, False)
-        hf_quantize(1, 1)
+        h_interleave(1, 1, "S", 256, 512)
         value_run(0, range(2, 4))
-        hf_quantize(1, 2)
-        policy_one(0, 3, 1, False)
-        h_interleave(1, 2, "S", 0, 256)
-        value_run(1, range(2))
+        h_interleave(1, 2, "V", 256, 512)
+        hs_quantize(1)
         h_interleave(0, 2, "V")
+        policy_one(0, 3, 1, False)
         policy_one(1, 0, 0, False)
-        h_interleave(1, 2, "S", 256, 512)
-        value_run(1, range(2, 4))
-        hs_quantize(0, 2)
-        hs_quantize(1, 2)
         policy_one(1, 0, 1, False)
         policy_one(1, 1, 0, False)
+        h_interleave(1, 2, "S", 0, 256)
+        value_run(1, range(2))
+        hs_quantize(2)
         policy_one(1, 1, 1, False)
+        value_run(1, range(2, 4))
         policy_one(1, 2, 0, False)
         value_run(2, range(2))
         policy_one(1, 2, 1, False)

@@ -20,6 +20,7 @@ ALU = mybir.AluOpType
 P = 128
 NF = F // 512
 NS = M // 512
+RESULT_BUFS = {1024: 5, 512: 7, 256: 4}
 
 
 def tile_policy_value_heads_s8_kernel(
@@ -29,14 +30,17 @@ def tile_policy_value_heads_s8_kernel(
     with ExitStack() as ctx:
         keep = ctx.enter_context(tc.tile_pool(name="keep", bufs=1))
         stage = ctx.enter_context(tc.tile_pool(name="stage", bufs=3))
-        ostage = ctx.enter_context(tc.tile_pool(name="ostage", bufs=6))
-        psum = ctx.enter_context(tc.psum_pool(name="psum", bufs=8))
+        psum = ctx.enter_context(tc.psum_pool(name="psum", bufs=1))
 
         def persistent(name, width, dtype):
             return keep.tile([P, width], dtype, name=name, align_bytes=64)
 
+        banks_taken = []
+
         def new_bank():
-            return psum.tile([P, 512], F32, name="bank")
+            bank = psum.tile([P, 512], F32, name=f"bank{len(banks_taken) % 8}")
+            banks_taken.append(bank)
+            return bank
 
         ctx.enter_context(tc.manual_schedule())
 
@@ -45,8 +49,12 @@ def tile_policy_value_heads_s8_kernel(
         ps = keep.tile([P, NF, A], U8, name="ps", align_bytes=64)
         nc.gpsimd.memset(ps[:].rearrange("p g n -> p (g n)").bitcast(I32), 0)
 
+        one_set = persistent("one_set", 1, F32)
+        nc.vector.memset(one_set[:], 1.0)
+        one = persistent("one", 1, F32)
+        nc.scalar.activation(out=one[:], in_=one_set[:], func=ACT.Copy)
         w_raw, x_raw = {}, {}
-        x_view = x.rearrange("(s q t) k -> s t q k", s=NS, t=4)
+        x_view = x.rearrange("(s q t) k -> s q t k", s=NS, t=4)
 
         def load_w(f, g):
             w_raw[f, g] = stage.tile([P, 4, 512], BF16, name=f"w_raw{f}{g}", tag="plain", align_bytes=64, bufs=8)
@@ -55,29 +63,40 @@ def tile_policy_value_heads_s8_kernel(
                 in_=w[512 * g : 512 * (g + 1), 512 * f : 512 * (f + 1)].rearrange("(p j) c -> p j c", j=4),
             )
 
-        def load_x(s, t):
-            x_raw[s, t] = persistent(f"x_raw{s}{t}", K, BF16)
-            nc.sync.dma_start(out=x_raw[s, t][:], in_=x_view[s, t])
+        x_pair = {}
+
+        def load_x(s, t, count=1):
+            if t % 2 == 0:
+                x_pair[s, t // 2] = stage.tile(
+                    [P, 2 * K], BF16, name=f"x_raw{s}{t}", tag="rows1024", align_bytes=64, bufs=RESULT_BUFS[1024]
+                )
+            rows = x_pair[s, t // 2][:, K * (t % 2) : K * (t % 2 + count)]
+            nc.sync.dma_start(out=rows, in_=x_view[s, :, t : t + count].rearrange("q t k -> q (t k)"))
+            for i in range(count):
+                x_raw[s, t + i] = rows[:, K * i : K * (i + 1)]
 
         inv16 = keep.tile([P, NS, 4], BF16, name="inv16", align_bytes=64)
-
         bscale = keep.tile([P, NS, 4], F32, name="bscale", align_bytes=64)
 
-        def load_factors():
+        def load_bscale():
             nc.sync.dma_start(out=bscale[:], in_=backup_scale.rearrange("o (s q t) -> q (o s) t", s=NS, t=4))
+
+        def load_inv():
             nc.sync.dma_start(out=inv16[:], in_=invtemp.rearrange("(s q t) -> q s t", s=NS, t=4))
 
-        b_raw = {}
         pw = keep.tile([P, NF, 2 * A], U8, name="pw", align_bytes=64)
-
         vg = persistent("vg", F, BF16)
+        b_raw = {}
+        b_view = backup_bytes.rearrange("(p j) m -> p j m", j=4)
 
         def load_gain():
             nc.sync.dma_start(out=vg[:], in_=vgain.partition_broadcast(P))
 
-        def load_b(r):
-            b_raw[r] = persistent(f"b_raw{r}", M, U8)
-            nc.sync.dma_start(out=b_raw[r][:], in_=backup_bytes[P * r : P * (r + 1), :])
+        def load_b(j, count):
+            rows = persistent(f"b_raw{j}", count * M, U8)
+            nc.sync.dma_start(out=rows[:], in_=b_view[:, j : j + count].rearrange("p j m -> p (j m)"))
+            for i in range(count):
+                b_raw[j + i] = rows[:, M * i : M * (i + 1)]
 
         def load_p():
             for c in range(4):
@@ -87,9 +106,10 @@ def tile_policy_value_heads_s8_kernel(
                 )
             nc.sync.dma_start(out=pw[:].bitcast(I32), in_=p_words.rearrange("g p n -> p g n").bitcast(I32))
 
-        for r in range(4):
-            load_b(r)
+        for j in range(4):
+            load_b(j, 1)
         load_w(0, 0)
+        load_bscale()
         for t in range(4):
             load_x(0, t)
         load_w(0, 1)
@@ -101,7 +121,7 @@ def tile_policy_value_heads_s8_kernel(
         load_w(1, 1)
         load_w(2, 0)
         load_w(2, 1)
-        load_factors()
+        load_inv()
         load_p()
         load_gain()
 
@@ -114,10 +134,12 @@ def tile_policy_value_heads_s8_kernel(
         def mx_tiles(name, columns):
             return persistent(name + "_codes", columns, U32), persistent(name + "_scales", columns, U8)
 
-        def quantize(mx, grouped, lo, hi):
+        def quantize(mx, grouped, lo, hi, shift=0):
             codes, scales = mx
             nc.vector.quantize_mx(
-                out=codes[:, lo:hi].bitcast(FP8X4), scales=scales[:, lo:hi], in_=grouped[:, 4 * lo : 4 * hi]
+                out=codes[:, lo:hi].bitcast(FP8X4),
+                scales=scales[:, lo:hi],
+                in_=grouped[:, 4 * (lo - shift) : 4 * (hi - shift)],
             )
 
         def operand(mx, lo, width):
@@ -138,7 +160,7 @@ def tile_policy_value_heads_s8_kernel(
 
         def w_interleave(f, g, engine, lo=0, hi=512):
             if f not in w_grp:
-                w_grp[f] = stage.tile([P, 4096], BF16, name="w_grp", align_bytes=64, bufs=2)
+                w_grp[f] = stage.tile([P, 4096], BF16, name="w_grp", tag="grp", align_bytes=64, bufs=4)
                 w_mx[f] = mx_tiles(f"w{f}", 1024)
             interleave(engine, w_grp[f][:, 2048 * g : 2048 * (g + 1)], w_raw[f, g][:], lo, hi)
 
@@ -158,19 +180,19 @@ def tile_policy_value_heads_s8_kernel(
                 bank[:].rearrange("p (a u q) -> p a q u", a=2, u=2),
             )
 
-        x_bank, x_grp, x_mx = {}, {}, {}
+        x_bank = {}
+        x_grp = persistent("x_grp", 4096, BF16)
+        x_mx = [mx_tiles(f"x{s}", 1024) for s in range(NS)]
 
         def x_turn(s, t):
-            words = x_raw[s, t][:].bitcast(F32)
+            words = x_raw[s, t].bitcast(F32)
             x_bank[s, t] = turn([words[:, 256 * g + u : 256 * (g + 1) : 2] for g in range(2) for u in range(2)])
 
         def x_copy(s, t, engine):
-            x_grp[s, t] = stage.tile([P, 1024], BF16, name="x_grp", align_bytes=64, bufs=4)
-            pair_up(engine, x_grp[s, t][:], x_bank[s, t])
+            pair_up(engine, x_grp[:, 1024 * t : 1024 * (t + 1)], x_bank[s, t])
 
-        def x_quantize(s, t):
-            x_mx[s, t] = mx_tiles(f"x{s}{t}", 256)
-            quantize(x_mx[s, t], x_grp[s, t], 0, 256)
+        def x_quantize(s, t, count=1):
+            quantize(x_mx[s], x_grp, 256 * t, 256 * (t + count))
 
         def product(out, stationary, moving, index, count):
             nc.tensor.matmul_mx(
@@ -189,7 +211,9 @@ def tile_policy_value_heads_s8_kernel(
             if (s, t, f) not in h_bank:
                 h_bank[s, t, f] = new_bank()
             for g in passes:
-                product(h_bank[s, t, f][:], operand(x_mx[s, t], P * g, P), operand(w_mx[f], 512 * g, 512), g, 2)
+                product(
+                    h_bank[s, t, f][:], operand(x_mx[s], 256 * t + P * g, P), operand(w_mx[f], 512 * g, 512), g, 2
+                )
 
         def relu(s, t, f, engine):
             if (s, f) not in h_plain:
@@ -203,264 +227,386 @@ def tile_policy_value_heads_s8_kernel(
             else:
                 nc.vector.tensor_relu(out=out, in_=in_)
 
-        ht_bank, hf_grp, hf_mx, hs_grp, hs_mx = {}, {}, {}, {}, {}
+        ht_bank, hf_place, hs_grp, hs_mx = {}, {}, {}, {}
+        hf_grp = persistent("hf_grp", 8 * 1024, BF16)
+        hf_mx = mx_tiles("hf", 12 * 256)
 
         def h_turn(s, f, a):
+            hf_place[s, f, a] = len(hf_place)
             words = h_plain[s, f][:].bitcast(F32)
             ht_bank[s, f, a] = turn([words[:, P * i : P * (i + 1)] for i in range(4 * a, 4 * a + 4)])
 
         def h_copy(s, f, a, engine):
-            pair, half = divmod(NF * s + f, 2)
-            if pair not in hf_grp:
-                hf_grp[pair] = stage.tile([P, 4096], BF16, name="hf_grp", align_bytes=64, bufs=2)
-                hf_mx[pair] = mx_tiles(f"hf{pair}", 1024)
-            first = 2048 * half + 1024 * a
-            pair_up(engine, hf_grp[pair][:, first : first + 1024], ht_bank[s, f, a])
+            first = 1024 * (hf_place[s, f, a] % 8)
+            pair_up(engine, hf_grp[:, first : first + 1024], ht_bank[s, f, a])
 
-        def hf_quantize(s, f, count=1):
-            pair, half = divmod(NF * s + f, 2)
-            quantize(hf_mx[pair], hf_grp[pair], 512 * half, 512 * (half + count))
+        def hf_quantize(s, f, a, count):
+            place = hf_place[s, f, a]
+            quantize(hf_mx, hf_grp, 256 * place, 256 * (place + count), 256 * (place - place % 8))
 
         def hf_operand(s, f, t):
-            pair, half = divmod(NF * s + f, 2)
-            return operand(hf_mx[pair], 512 * half + P * t, P)
+            return operand(hf_mx, 256 * hf_place[s, f, t // 2] + P * (t % 2), P)
 
         def h_interleave(s, f, engine, lo=0, hi=512):
             if f not in hs_grp:
-                hs_grp[f] = stage.tile([P, 4096], BF16, name="hs_grp", align_bytes=64, bufs=2)
+                hs_grp[f] = stage.tile([P, 4096], BF16, name="hs_grp", tag="grp", align_bytes=64, bufs=4)
                 hs_mx[f] = mx_tiles(f"hs{f}", 1024)
             planes = h_plain[s, f][:].rearrange("p (t c) -> p t c", t=4)
             interleave(engine, hs_grp[f][:, 2048 * s : 2048 * (s + 1)], planes, lo, hi)
 
-        def hs_quantize(f):
-            quantize(hs_mx[f], hs_grp[f], 0, 1024)
-
-        b_wide, b_bank = {}, {}
-        b_grp = persistent("b_grp", NS * 2048, BF16)
-        b_mx = mx_tiles("b", 1024)
-        b_turned = persistent("b_turned", NS * 2048, BF16)
-
-        def b_widen(r, engine):
-            b_wide[r] = persistent(f"b_wide{r}", M, BF16)
-            if engine == "S":
-                nc.scalar.activation(out=b_wide[r][:], in_=b_raw[r][:].bitcast(FP8), func=ACT.Copy)
-            else:
-                nc.vector.tensor_copy(out=b_wide[r][:], in_=b_raw[r][:].bitcast(FP8))
-
-        def b_turn(r):
-            words = b_wide[r][:].bitcast(F32)
-            b_bank[r] = turn([words[:, 256 * s + u : 256 * (s + 1) : 2] for s in range(NS) for u in range(2)])
-
-        def b_copy(r, engine):
-            copy(
-                engine,
-                b_turned[:].bitcast(F32).rearrange("p (s r q u) -> p r s q u", s=NS, r=4, u=2)[:, r],
-                b_bank[r][:].rearrange("p (s u q) -> p s q u", s=NS, u=2),
+        def h_interleave_pool(s, f, lo, hi):
+            if f not in hs_grp:
+                hs_grp[f] = stage.tile([P, 4096], BF16, name="hs_grp", tag="grp", align_bytes=64, bufs=4)
+                hs_mx[f] = mx_tiles(f"hs{f}", 1024)
+            nc.gpsimd.tensor_scalar(
+                out=hs_grp[f][:, 2048 * s : 2048 * (s + 1)].rearrange("p (c t) -> p c t", t=4)[:, lo:hi],
+                in0=h_plain[s, f][:].rearrange("p (t c) -> p c t", t=4)[:, lo:hi],
+                scalar1=1.0,
+                scalar2=0.0,
+                op0=ALU.mult,
+                op1=ALU.add,
             )
 
-        def b_scale(s, a):
-            cols = slice(2048 * s + 1024 * a, 2048 * s + 1024 * (a + 1))
+        def hs_quantize(f, first=0, last=1):
+            quantize(hs_mx[f], hs_grp[f], 512 * first, 512 * (last + 1))
+
+        b_wide, b_bank = {}, {}
+        b_turned = persistent("b_turned", NS * 2048, BF16)
+        b_grp = persistent("b_grp", NS * 2048, BF16)
+        b_mx = mx_tiles("b", 1024)
+
+        def b_widen(j):
+            b_wide[j] = persistent(f"b_wide{j}", M, BF16)
+            nc.vector.tensor_scalar(
+                out=b_wide[j][:].rearrange("p (u q e) -> p q u e", u=2, e=2),
+                in0=b_raw[j].bitcast(FP8).rearrange("p (q u e) -> p q u e", u=2, e=2),
+                scalar1=one[:],
+                scalar2=None,
+                op0=ALU.mult,
+            )
+
+        def b_turn(j):
+            words = b_wide[j][:].bitcast(F32)
+            starts = [256 * u + P * s for s in range(NS) for u in range(2)]
+            b_bank[j] = turn([words[:, c : c + P] for c in starts])
+
+        def b_copy(j, engine):
+            copy(
+                engine,
+                b_turned[:].bitcast(F32).rearrange("p (s j q u) -> p j s q u", s=NS, j=4, u=2)[:, j],
+                b_bank[j][:].rearrange("p (s u q) -> p s q u", s=NS, u=2),
+            )
+
+        def b_scale(s, j, count):
+            cols = slice(2048 * s + 512 * j, 2048 * s + 512 * (j + count))
             nc.vector.tensor_tensor(
                 out=b_grp[:, cols].rearrange("p (r t) -> p r t", t=4),
                 in0=b_turned[:, cols].rearrange("p (r t) -> p r t", t=4),
-                in1=bscale[:, s, :].unsqueeze(1).to_broadcast([P, 256, 4]),
+                in1=bscale[:, s, :].unsqueeze(1).to_broadcast([P, P * count, 4]),
                 op=ALU.mult,
             )
 
-        def b_quantize():
-            quantize(b_mx, b_grp, 0, 1024)
+        def b_scale_out(j, s):
+            first = 2048 * s + 512 * j
+            nc.vector.tensor_tensor(
+                out=b_grp[:, first : first + 512].rearrange("p (r u e) -> p r u e", u=2, e=2),
+                in0=b_bank[j][:, 256 * s : 256 * (s + 1)].bitcast(BF16).rearrange("p (u r e) -> p r u e", u=2, e=2),
+                in1=bscale[:, s, :].rearrange("p (u e) -> p u e", u=2).unsqueeze(1).to_broadcast([P, P, 2, 2]),
+                op=ALU.mult,
+            )
+
+        def b_quantize(first=0, last=1):
+            quantize(b_mx, b_grp, 512 * first, 512 * (last + 1))
 
         p_view = policy.rearrange("(s q t) a -> s t q a", s=NS, t=4)
-        p_bank, p_rows, v_bank = {}, {}, {}
+        v_view = value.rearrange("(p j) f -> p j f", j=4)
+        p_bank, p_rows, v_bank, v_rows = {}, {}, {}, {}
 
         def p_operand(f, lo, width):
             return pw[:, f, 2 * lo : 2 * (lo + width)].bitcast(FP4X4), ps[:, f, lo : lo + width]
+
+        def result_tile(width):
+            return stage.tile([P, width], F32, name="result", tag=f"rows{width}", align_bytes=64, bufs=RESULT_BUFS[width])
+
+        def scaled_copy(engine, out, in_, factor):
+            if engine == "S":
+                nc.scalar.activation(out=out, in_=in_, func=ACT.Copy, scale=factor)
+            else:
+                nc.vector.tensor_scalar(out=out, in0=in_, scalar1=factor, scalar2=None, op0=ALU.mult)
 
         def policy_mm(s, t, n):
             p_bank[s, t, n] = new_bank()
             for f in range(NF):
                 product(p_bank[s, t, n][:], hf_operand(s, f, t), p_operand(f, 512 * n, 512), f, NF)
 
-        def policy_out(s, t, n, engine, whole_rows=True):
-            if (s, t) not in p_rows:
-                p_rows[s, t] = ostage.tile([P, A], F32, name="p_out", bufs=3)
-            result = p_rows[s, t][:, 512 * n : 512 * (n + 1)]
+        def policy_out(s, t, n, engine, whole_rows):
             factor = inv[:, 4 * s + t : 4 * s + t + 1]
-            if engine == "S":
-                nc.scalar.activation(out=result, in_=p_bank[s, t, n][:], func=ACT.Copy, scale=factor)
+            if whole_rows:
+                if n == 0:
+                    p_rows[s, t] = result_tile(1024)
+                scaled_copy(engine, p_rows[s, t][:, 512 * n : 512 * (n + 1)], p_bank[s, t, n][:], factor)
+                if n == 1:
+                    nc.sync.dma_start(out=p_view[s, t], in_=p_rows[s, t][:])
             else:
-                nc.vector.tensor_scalar(
-                    out=result, in0=p_bank[s, t, n][:], scalar1=factor, scalar2=None, op0=ALU.mult
-                )
-            if not whole_rows:
-                nc.sync.dma_start(out=p_view[s, t, :, 512 * n : 512 * (n + 1)], in_=result)
-            elif n == 1:
-                nc.sync.dma_start(out=p_view[s, t], in_=p_rows[s, t][:])
+                result = result_tile(512)
+                scaled_copy(engine, result[:], p_bank[s, t, n][:], factor)
+                nc.sync.dma_start(out=p_view[s, t, :, 512 * n : 512 * (n + 1)], in_=result[:])
 
-        def policy_half(s, t, c, engine):
-            bank = new_bank()
-            for j in range(2):
+        def piece_mm(s, t, first, count):
+            p_bank[s, t, 2 + first] = new_bank()
+            for j in range(count):
                 for f in range(NF):
-                    moving = p_operand(f, 256 * c + P * j, P)
-                    product(bank[:, P * j : P * (j + 1)], hf_operand(s, f, t), moving, f, NF)
-            result = ostage.tile([P, 256], F32, name="p_half", bufs=2)
+                    moving = p_operand(f, P * (first + j), P)
+                    product(p_bank[s, t, 2 + first][:, P * j : P * (j + 1)], hf_operand(s, f, t), moving, f, NF)
+
+        def piece_out(s, t, first, count, engine):
+            result = result_tile(256)
+            width = P * count
             factor = inv[:, 4 * s + t : 4 * s + t + 1]
-            if engine == "S":
-                nc.scalar.activation(out=result[:], in_=bank[:, 0:256], func=ACT.Copy, scale=factor)
-            else:
-                nc.vector.tensor_scalar(out=result[:], in0=bank[:, 0:256], scalar1=factor, scalar2=None, op0=ALU.mult)
-            nc.sync.dma_start(out=p_view[s, t, :, 256 * c : 256 * (c + 1)], in_=result[:])
+            scaled_copy(engine, result[:, 0:width], p_bank[s, t, 2 + first][:, 0:width], factor)
+            nc.sync.dma_start(out=p_view[s, t, :, P * first : P * first + width], in_=result[:, 0:width])
 
-        def value_mm(r, f):
-            v_bank[r, f] = new_bank()
+        def value_mm(j, f):
+            v_bank[j, f] = new_bank()
             for s in range(NS):
-                product(v_bank[r, f][:], operand(b_mx, 512 * s + P * r, P), operand(hs_mx[f], 512 * s, 512), s, NS)
+                product(v_bank[j, f][:], operand(b_mx, 512 * s + P * j, P), operand(hs_mx[f], 512 * s, 512), s, NS)
 
-        def value_out(r, f):
+        def value_out(j, f, paired):
             cols = slice(512 * f, 512 * (f + 1))
-            result = ostage.tile([P, 512], F32, name="v_out")
+            if paired:
+                if j % 2 == 0:
+                    v_rows[f] = result_tile(1024)
+                result = v_rows[f][:, 512 * (j % 2) : 512 * (j % 2 + 1)]
+            else:
+                single = result_tile(512)
+                result = single[:]
             nc.vector.tensor_tensor(
-                out=result[:].rearrange("p (m u e) -> p m u e", u=2, e=2),
-                in0=v_bank[r, f][:].rearrange("p (u m e) -> p m u e", u=2, e=2),
+                out=result.rearrange("p (m u e) -> p m u e", u=2, e=2),
+                in0=v_bank[j, f][:].rearrange("p (u m e) -> p m u e", u=2, e=2),
                 in1=vg[:, cols].rearrange("p (m u e) -> p m u e", u=2, e=2),
                 op=ALU.mult,
             )
-            nc.sync.dma_start(out=value[P * r : P * (r + 1), cols], in_=result[:])
+            if not paired:
+                nc.sync.dma_start(out=v_view[:, j, cols], in_=result)
+            elif j % 2 == 1:
+                nc.sync.dma_start(
+                    out=v_view[:, j - 1 : j + 1, cols], in_=v_rows[f][:].rearrange("p (j c) -> p j c", j=2)
+                )
 
-        def trunk_run(s, f, engines, tiles=range(4)):
-            for t in tiles:
-                trunk(s, t, f)
-                relu(s, t, f, engines[t])
-
-        def h_run(s, f, engines):
-            for a in range(2):
-                h_turn(s, f, a)
-                h_copy(s, f, a, engines[a])
-
-        def x_run(s, tiles, engine):
-            for t in tiles:
-                x_turn(s, t)
-                x_copy(s, t, engine)
-
-        def policy_run(s, t, engines="SS"):
-            for n in range(2):
-                policy_mm(s, t, n)
-                policy_out(s, t, n, engines[n])
-
-        def value_run(f, rows):
-            for r in rows:
-                value_mm(r, f)
-                value_out(r, f)
-
-        def policy_one(s, t, n, whole_rows=True):
-            policy_mm(s, t, n)
-            policy_out(s, t, n, "S", whole_rows)
-
-        def value_one(r, f):
-            value_mm(r, f)
-            value_out(r, f)
-
-        def w_shared(f, g, cut):
-            w_interleave(f, g, "S", cut, 512)
-            w_interleave(f, g, "V", 0, cut)
-
-        for r in range(4):
-            b_widen(r, "VVVS"[r])
-        for r in range(4):
-            b_turn(r)
-            b_copy(r, "VSSS"[r])
-        w_interleave(0, 0, "V")
-        x_run(0, range(4), "S")
+        b_widen(0)
+        b_widen(1)
+        b_turn(0)
+        b_widen(2)
+        b_turn(1)
+        b_widen(3)
+        b_copy(0, "S")
+        b_turn(2)
+        w_interleave(0, 0, "V", 0, 512)
+        b_copy(1, "S")
+        b_turn(3)
+        b_copy(2, "S")
+        x_turn(0, 0)
+        b_copy(3, "S")
+        b_scale(0, 0, 1)
+        x_turn(0, 1)
         w_quantize(0, 0, 0)
-        for t in range(2):
-            x_quantize(0, t)
-        w_shared(0, 1, 384)
-        for t in range(2, 4):
-            x_quantize(0, t)
+        x_copy(0, 0, "S")
+        x_turn(0, 2)
+        b_scale(1, 0, 1)
+        x_copy(0, 1, "S")
+        x_turn(0, 3)
+        x_quantize(0, 0, 1)
+        x_copy(0, 2, "S")
+        x_quantize(0, 1, 1)
+        trunk(0, 0, 0, [0])
+        x_copy(0, 3, "S")
+        w_interleave(0, 1, "V", 0, 384)
+        trunk(0, 1, 0, [0])
+        w_interleave(0, 1, "S", 384, 512)
+        x_quantize(0, 2, 1)
+        x_turn(1, 0)
+        x_quantize(0, 3, 1)
         w_quantize(0, 1, 1)
-        for t in range(2):
-            trunk(0, t, 0, [0])
-        x_run(1, [0, 1], "S")
-        w_shared(1, 0, 384)
-        for t in range(2, 4):
-            trunk(0, t, 0, [0])
-        for t in range(4):
-            trunk(0, t, 0, [1])
-        for t in range(2):
-            relu(0, t, 0, "S")
-        x_quantize(1, 0)
-        x_quantize(1, 1)
+        x_turn(1, 1)
+        x_copy(1, 0, "S")
+        trunk(0, 2, 0, [0])
+        w_interleave(1, 0, "V", 0, 384)
+        x_copy(1, 1, "S")
+        trunk(0, 3, 0, [0])
+        trunk(0, 0, 0, [1])
+        w_interleave(1, 0, "S", 384, 512)
+        trunk(0, 1, 0, [1])
+        trunk(0, 2, 0, [1])
+        x_quantize(1, 0, 1)
+        trunk(0, 3, 0, [1])
+        relu(0, 0, 0, "S")
+        x_quantize(1, 1, 1)
         w_quantize(1, 0, 0)
-        x_run(1, [2, 3], "S")
-        for t in range(2, 4):
-            relu(0, t, 0, "S")
-        trunk_run(1, 0, "SSSS", range(2))
+        x_turn(1, 2)
+        relu(0, 1, 0, "S")
+        x_turn(1, 3)
         w_interleave(1, 1, "V", 0, 256)
-        x_quantize(1, 2)
-        x_quantize(1, 3)
+        x_copy(1, 2, "S")
+        trunk(1, 0, 0)
+        x_copy(1, 3, "S")
+        b_scale(0, 1, 1)
+        trunk(1, 1, 0)
+        relu(0, 2, 0, "S")
+        x_quantize(1, 2, 1)
+        trunk(0, 0, 1, [0])
+        x_quantize(1, 3, 1)
+        trunk(0, 1, 1, [0])
+        relu(0, 3, 0, "S")
         w_interleave(1, 1, "V", 256, 512)
-        trunk_run(1, 0, "SSSS", range(2, 4))
+        trunk(1, 2, 0)
+        relu(1, 0, 0, "S")
         w_interleave(2, 0, "V", 0, 128)
+        trunk(1, 3, 0)
         w_quantize(1, 1, 1)
+        relu(1, 1, 0, "S")
+        trunk(0, 2, 1, [0])
         w_interleave(2, 0, "V", 128, 512)
-        w_interleave(2, 1, "V")
+        relu(1, 2, 0, "S")
+        trunk(0, 3, 1, [0])
+        trunk(0, 0, 1, [1])
+        relu(1, 3, 0, "S")
+        trunk(0, 1, 1, [1])
+        trunk(0, 2, 1, [1])
+        w_interleave(2, 1, "V", 0, 512)
+        relu(0, 0, 1, "S")
+        trunk(0, 3, 1, [1])
+        trunk(1, 0, 1)
+        relu(0, 1, 1, "S")
+        trunk(1, 1, 1)
         w_quantize(2, 0, 0)
+        relu(0, 2, 1, "S")
+        h_turn(0, 0, 0)
         w_quantize(2, 1, 1)
-        for t in range(4):
-            trunk(0, t, 1, [0])
-        for t in range(4):
-            trunk(0, t, 1, [1])
-            relu(0, t, 1, "S")
-        trunk_run(1, 1, "SSSS", range(2))
-        h_interleave(0, 0, "V")
-        h_run(0, 0, "VV")
-        h_run(0, 1, "VS")
-        trunk_run(0, 2, "SSSS")
-        b_scale(0, 0)
-        hf_quantize(0, 0, 2)
-        trunk_run(1, 1, "SSSS", range(2, 4))
-        h_run(0, 2, "VS")
-        h_run(1, 0, "SS")
-        b_scale(0, 1)
-        hf_quantize(0, 2)
+        relu(0, 3, 1, "S")
+        h_turn(0, 0, 1)
+        h_turn(0, 1, 0)
+        relu(1, 0, 1, "S")
+        h_interleave(0, 0, "V", 0, 512)
+        h_turn(0, 1, 1)
+        relu(1, 1, 1, "S")
+        trunk(0, 0, 2)
+        h_copy(0, 1, 1, "S")
+        trunk(0, 1, 2)
+        h_copy(0, 0, 0, "V")
+        relu(0, 0, 2, "S")
+        trunk(0, 2, 2)
+        h_copy(0, 0, 1, "V")
+        relu(0, 1, 2, "S")
+        trunk(0, 3, 2)
+        h_copy(0, 1, 0, "V")
+        relu(0, 2, 2, "S")
+        trunk(1, 2, 1)
+        b_scale(0, 2, 2)
+        relu(0, 3, 2, "S")
+        trunk(1, 3, 1)
+        relu(1, 2, 1, "S")
+        hf_quantize(0, 0, 0, 4)
+        h_turn(0, 2, 0)
+        h_turn(0, 2, 1)
+        relu(1, 3, 1, "S")
+        h_turn(1, 0, 0)
+        h_turn(1, 0, 1)
+        h_copy(0, 2, 1, "S")
+        h_copy(0, 2, 0, "V")
+        trunk(1, 0, 2)
+        h_copy(1, 0, 0, "S")
+        b_scale(1, 1, 1)
+        trunk(1, 1, 2)
+        h_copy(1, 0, 1, "S")
+        hf_quantize(0, 2, 0, 2)
+        trunk(1, 2, 2)
         widen_inv()
-        trunk_run(1, 2, "SSSS")
-        h_interleave(1, 0, "V")
-        b_scale(1, 0)
-        b_scale(1, 1)
-        for n in range(2):
-            policy_one(0, 0, n, False)
+        relu(1, 0, 2, "S")
+        h_interleave(1, 0, "V", 0, 512)
+        trunk(1, 3, 2)
+        relu(1, 1, 2, "S")
+        policy_mm(0, 0, 0)
+        relu(1, 2, 2, "S")
+        b_scale(1, 2, 2)
+        relu(1, 3, 2, "S")
+        policy_mm(0, 0, 1)
         hs_quantize(0)
+        policy_mm(0, 1, 0)
+        policy_out(0, 0, 0, "S", True)
+        policy_mm(0, 1, 1)
+        policy_out(0, 0, 1, "S", True)
         b_quantize()
-        for t in range(1, 3):
-            for n in range(2):
-                policy_one(0, t, n, False)
-        hf_quantize(1, 0)
-        h_interleave(0, 1, "V")
-        h_run(1, 1, "SS")
-        h_run(1, 2, "SS")
+        policy_mm(0, 2, 0)
+        policy_out(0, 1, 0, "S", True)
+        h_interleave(0, 1, "V", 0, 512)
+        policy_mm(0, 2, 1)
+        policy_out(0, 1, 1, "S", True)
         h_interleave(1, 1, "S", 0, 256)
-        value_run(0, range(2))
-        hf_quantize(1, 1, 2)
-        policy_one(0, 3, 0, False)
+        value_mm(0, 0)
+        hf_quantize(1, 0, 0, 2)
+        value_mm(1, 0)
+        value_mm(2, 0)
+        policy_out(0, 2, 0, "S", True)
+        value_out(0, 0, True)
+        value_mm(3, 0)
+        policy_out(0, 2, 1, "S", True)
         h_interleave(1, 1, "S", 256, 512)
-        value_run(0, range(2, 4))
-        h_interleave(1, 2, "V", 256, 512)
+        value_out(1, 0, True)
+        h_turn(1, 1, 0)
+        value_out(2, 0, True)
+        h_turn(1, 2, 0)
+        h_copy(1, 1, 0, "S")
+        h_turn(1, 1, 1)
+        value_out(3, 0, True)
         hs_quantize(1)
-        h_interleave(0, 2, "V")
-        policy_one(0, 3, 1, False)
-        policy_one(1, 0, 0, False)
-        policy_one(1, 0, 1, False)
-        policy_one(1, 1, 0, False)
-        h_interleave(1, 2, "S", 0, 256)
-        value_run(1, range(2))
+        h_turn(1, 2, 1)
+        h_copy(1, 2, 0, "S")
+        policy_mm(0, 3, 0)
+        h_copy(1, 1, 1, "S")
+        h_interleave(1, 2, "V", 0, 256)
+        policy_mm(0, 3, 1)
+        h_copy(1, 2, 1, "S")
+        hf_quantize(1, 1, 0, 2)
+        value_mm(0, 1)
+        policy_out(0, 3, 0, "S", True)
+        h_interleave(1, 2, "V", 256, 512)
+        value_mm(1, 1)
+        policy_out(0, 3, 1, "S", True)
+        h_interleave(0, 2, "S", 0, 256)
+        policy_mm(1, 0, 0)
+        value_out(0, 1, True)
+        value_mm(2, 1)
+        value_out(1, 1, True)
+        h_interleave(0, 2, "V", 256, 512)
+        value_mm(3, 1)
+        policy_out(1, 0, 0, "S", True)
+        policy_mm(1, 0, 1)
+        value_out(2, 1, True)
+        policy_mm(1, 1, 0)
+        value_out(3, 1, True)
         hs_quantize(2)
-        policy_one(1, 1, 1, False)
-        value_run(1, range(2, 4))
-        policy_one(1, 2, 0, False)
-        value_run(2, range(2))
-        policy_one(1, 2, 1, False)
-        value_run(2, range(2, 4))
-        policy_one(1, 3, 0, False)
-        policy_half(1, 3, 2, "V")
-        policy_half(1, 3, 3, "S")
+        policy_mm(1, 1, 1)
+        policy_out(1, 0, 1, "S", True)
+        hf_quantize(1, 1, 1, 2)
+        value_mm(0, 2)
+        policy_out(1, 1, 0, "S", True)
+        value_mm(1, 2)
+        policy_out(1, 1, 1, "S", True)
+        policy_mm(1, 2, 0)
+        value_out(0, 2, False)
+        value_mm(2, 2)
+        value_out(1, 2, False)
+        value_mm(3, 2)
+        policy_out(1, 2, 0, "S", False)
+        policy_mm(1, 2, 1)
+        value_out(2, 2, False)
+        piece_mm(1, 3, 0, 2)
+        value_out(3, 2, False)
+        piece_mm(1, 3, 2, 2)
+        piece_mm(1, 3, 4, 2)
+        policy_out(1, 2, 1, "S", False)
+        piece_out(1, 3, 0, 2, "V")
+        piece_mm(1, 3, 6, 2)
+        piece_out(1, 3, 2, 2, "S")
+        piece_out(1, 3, 4, 2, "V")
+        piece_out(1, 3, 6, 2, "S")

@@ -20,7 +20,7 @@ ALU = mybir.AluOpType
 P = 128
 NF = F // 512
 NS = M // 512
-RESULT_BUFS = {1024: 5, 512: 7, 256: 4}
+RESULT_BUFS = {1024: 10, 512: 8, 256: 4}
 
 
 def tile_policy_value_heads_s8_kernel(
@@ -47,12 +47,10 @@ def tile_policy_value_heads_s8_kernel(
         ident = persistent("ident", P, F32)
         make_identity(nc, ident[:])
         ps = keep.tile([P, NF, A], U8, name="ps", align_bytes=64)
-        nc.gpsimd.memset(ps[:].rearrange("p g n -> p (g n)").bitcast(I32), 0)
+        nc.vector.memset(ps[:].rearrange("p g n -> p (g n)").bitcast(I32), 0)
 
-        one_set = persistent("one_set", 1, F32)
-        nc.vector.memset(one_set[:], 1.0)
         one = persistent("one", 1, F32)
-        nc.scalar.activation(out=one[:], in_=one_set[:], func=ACT.Copy)
+        nc.vector.memset(one[:], 1.0)
         w_raw, x_raw = {}, {}
         x_view = x.rearrange("(s q t) k -> s q t k", s=NS, t=4)
 
@@ -63,13 +61,15 @@ def tile_policy_value_heads_s8_kernel(
                 in_=w[512 * g : 512 * (g + 1), 512 * f : 512 * (f + 1)].rearrange("(p j) c -> p j c", j=4),
             )
 
+        def wide_tile(name, dtype):
+            width = 1024 if dtype == F32 else 2048
+            return stage.tile([P, width], dtype, name=name, tag="rows1024", align_bytes=64, bufs=RESULT_BUFS[1024])
+
         x_pair = {}
 
         def load_x(s, t, count=1):
             if t % 2 == 0:
-                x_pair[s, t // 2] = stage.tile(
-                    [P, 2 * K], BF16, name=f"x_raw{s}{t}", tag="rows1024", align_bytes=64, bufs=RESULT_BUFS[1024]
-                )
+                x_pair[s, t // 2] = wide_tile(f"x_raw{s}{t}", BF16)
             rows = x_pair[s, t // 2][:, K * (t % 2) : K * (t % 2 + count)]
             nc.sync.dma_start(out=rows, in_=x_view[s, :, t : t + count].rearrange("q t k -> q (t k)"))
             for i in range(count):
@@ -181,18 +181,32 @@ def tile_policy_value_heads_s8_kernel(
             )
 
         x_bank = {}
-        x_grp = persistent("x_grp", 4096, BF16)
+        x_grp = [wide_tile(f"x_grp{a}", BF16) for a in range(2)]
         x_mx = [mx_tiles(f"x{s}", 1024) for s in range(NS)]
 
+        x_sorted = {}
+
+        def x_sort(s, t, engine):
+            x_sorted[s, t] = stage.tile([P, 512], F32, name="x_sorted", align_bytes=64, bufs=2)
+            copy(
+                engine,
+                x_sorted[s, t][:].rearrange("p (g u q) -> p g u q", g=2, u=2),
+                x_raw[s, t].bitcast(F32).rearrange("p (g q u) -> p g u q", g=2, u=2),
+            )
+
         def x_turn(s, t):
-            words = x_raw[s, t].bitcast(F32)
-            x_bank[s, t] = turn([words[:, 256 * g + u : 256 * (g + 1) : 2] for g in range(2) for u in range(2)])
+            if (s, t) in x_sorted:
+                sources = [x_sorted[s, t][:, P * i : P * (i + 1)] for i in range(4)]
+            else:
+                words = x_raw[s, t].bitcast(F32)
+                sources = [words[:, 256 * g + u : 256 * (g + 1) : 2] for g in range(2) for u in range(2)]
+            x_bank[s, t] = turn(sources)
 
         def x_copy(s, t, engine):
-            pair_up(engine, x_grp[:, 1024 * t : 1024 * (t + 1)], x_bank[s, t])
+            pair_up(engine, x_grp[t // 2][:, 1024 * (t % 2) : 1024 * (t % 2 + 1)], x_bank[s, t])
 
         def x_quantize(s, t, count=1):
-            quantize(x_mx[s], x_grp, 256 * t, 256 * (t + count))
+            quantize(x_mx[s], x_grp[t // 2], 256 * t, 256 * (t + count), 512 * (t // 2))
 
         def product(out, stationary, moving, index, count):
             nc.tensor.matmul_mx(
@@ -270,15 +284,16 @@ def tile_policy_value_heads_s8_kernel(
         def hs_quantize(f, first=0, last=1):
             quantize(hs_mx[f], hs_grp[f], 512 * first, 512 * (last + 1))
 
-        b_wide, b_bank = {}, {}
-        b_turned = persistent("b_turned", NS * 2048, BF16)
+        b_bank = {}
+        b_pair = [wide_tile(f"b_wide{a}", BF16) for a in range(2)]
+        b_wide = [b_pair[j // 2][:, M * (j % 2) : M * (j % 2 + 1)] for j in range(4)]
+        b_turned = [wide_tile(f"b_turned{a}", BF16) for a in range(2)]
         b_grp = persistent("b_grp", NS * 2048, BF16)
         b_mx = mx_tiles("b", 1024)
 
         def b_widen(j):
-            b_wide[j] = persistent(f"b_wide{j}", M, BF16)
             nc.vector.tensor_scalar(
-                out=b_wide[j][:].rearrange("p (u q e) -> p q u e", u=2, e=2),
+                out=b_wide[j].rearrange("p (u q e) -> p q u e", u=2, e=2),
                 in0=b_raw[j].bitcast(FP8).rearrange("p (q u e) -> p q u e", u=2, e=2),
                 scalar1=one[:],
                 scalar2=None,
@@ -286,22 +301,23 @@ def tile_policy_value_heads_s8_kernel(
             )
 
         def b_turn(j):
-            words = b_wide[j][:].bitcast(F32)
+            words = b_wide[j].bitcast(F32)
             starts = [256 * u + P * s for s in range(NS) for u in range(2)]
             b_bank[j] = turn([words[:, c : c + P] for c in starts])
 
         def b_copy(j, engine):
             copy(
                 engine,
-                b_turned[:].bitcast(F32).rearrange("p (s j q u) -> p j s q u", s=NS, j=4, u=2)[:, j],
+                b_turned[j // 2][:].bitcast(F32).rearrange("p (s j q u) -> p j s q u", s=NS, j=2, u=2)[:, j % 2],
                 b_bank[j][:].rearrange("p (s u q) -> p s q u", s=NS, u=2),
             )
 
         def b_scale(s, j, count):
             cols = slice(2048 * s + 512 * j, 2048 * s + 512 * (j + count))
+            first = 1024 * s + 512 * (j % 2)
             nc.vector.tensor_tensor(
                 out=b_grp[:, cols].rearrange("p (r t) -> p r t", t=4),
-                in0=b_turned[:, cols].rearrange("p (r t) -> p r t", t=4),
+                in0=b_turned[j // 2][:, first : first + 512 * count].rearrange("p (r t) -> p r t", t=4),
                 in1=bscale[:, s, :].unsqueeze(1).to_broadcast([P, P * count, 4]),
                 op=ALU.mult,
             )
@@ -406,11 +422,11 @@ def tile_policy_value_heads_s8_kernel(
         b_turn(3)
         b_copy(2, "S")
         x_turn(0, 0)
-        b_copy(3, "S")
         b_scale(0, 0, 1)
+        b_copy(3, "S")
         x_turn(0, 1)
-        w_quantize(0, 0, 0)
         x_copy(0, 0, "S")
+        w_quantize(0, 0, 0)
         x_turn(0, 2)
         b_scale(1, 0, 1)
         x_copy(0, 1, "S")
@@ -419,8 +435,8 @@ def tile_policy_value_heads_s8_kernel(
         x_copy(0, 2, "S")
         x_quantize(0, 1, 1)
         trunk(0, 0, 0, [0])
-        x_copy(0, 3, "S")
         w_interleave(0, 1, "V", 0, 384)
+        x_copy(0, 3, "S")
         trunk(0, 1, 0, [0])
         w_interleave(0, 1, "S", 384, 512)
         x_quantize(0, 2, 1)
@@ -429,33 +445,33 @@ def tile_policy_value_heads_s8_kernel(
         w_quantize(0, 1, 1)
         x_turn(1, 1)
         x_copy(1, 0, "S")
-        trunk(0, 2, 0, [0])
         w_interleave(1, 0, "V", 0, 384)
-        x_copy(1, 1, "S")
+        trunk(0, 2, 0, [0])
         trunk(0, 3, 0, [0])
+        x_copy(1, 1, "S")
         trunk(0, 0, 0, [1])
-        w_interleave(1, 0, "S", 384, 512)
-        trunk(0, 1, 0, [1])
-        trunk(0, 2, 0, [1])
         x_quantize(1, 0, 1)
-        trunk(0, 3, 0, [1])
-        relu(0, 0, 0, "S")
+        trunk(0, 1, 0, [1])
+        w_interleave(1, 0, "S", 384, 512)
+        trunk(0, 2, 0, [1])
         x_quantize(1, 1, 1)
-        w_quantize(1, 0, 0)
+        trunk(0, 3, 0, [1])
         x_turn(1, 2)
-        relu(0, 1, 0, "S")
+        w_quantize(1, 0, 0)
         x_turn(1, 3)
         w_interleave(1, 1, "V", 0, 256)
-        x_copy(1, 2, "S")
-        trunk(1, 0, 0)
-        x_copy(1, 3, "S")
+        relu(0, 0, 0, "S")
         b_scale(0, 1, 1)
+        relu(0, 1, 0, "S")
+        trunk(1, 0, 0)
+        x_copy(1, 2, "S")
         trunk(1, 1, 0)
-        relu(0, 2, 0, "S")
+        x_copy(1, 3, "S")
         x_quantize(1, 2, 1)
         trunk(0, 0, 1, [0])
-        x_quantize(1, 3, 1)
+        relu(0, 2, 0, "S")
         trunk(0, 1, 1, [0])
+        x_quantize(1, 3, 1)
         relu(0, 3, 0, "S")
         w_interleave(1, 1, "V", 256, 512)
         trunk(1, 2, 0)
@@ -469,12 +485,12 @@ def tile_policy_value_heads_s8_kernel(
         relu(1, 2, 0, "S")
         trunk(0, 3, 1, [0])
         trunk(0, 0, 1, [1])
-        relu(1, 3, 0, "S")
         trunk(0, 1, 1, [1])
+        relu(1, 3, 0, "S")
         trunk(0, 2, 1, [1])
         w_interleave(2, 1, "V", 0, 512)
-        relu(0, 0, 1, "S")
         trunk(0, 3, 1, [1])
+        relu(0, 0, 1, "S")
         trunk(1, 0, 1)
         relu(0, 1, 1, "S")
         trunk(1, 1, 1)
@@ -482,64 +498,64 @@ def tile_policy_value_heads_s8_kernel(
         relu(0, 2, 1, "S")
         h_turn(0, 0, 0)
         w_quantize(2, 1, 1)
-        relu(0, 3, 1, "S")
         h_turn(0, 0, 1)
+        relu(0, 3, 1, "S")
         h_turn(0, 1, 0)
-        relu(1, 0, 1, "S")
         h_interleave(0, 0, "V", 0, 512)
         h_turn(0, 1, 1)
+        relu(1, 0, 1, "S")
         relu(1, 1, 1, "S")
         trunk(0, 0, 2)
+        h_copy(0, 0, 0, "V")
         h_copy(0, 1, 1, "S")
         trunk(0, 1, 2)
-        h_copy(0, 0, 0, "V")
+        h_copy(0, 0, 1, "V")
         relu(0, 0, 2, "S")
         trunk(0, 2, 2)
-        h_copy(0, 0, 1, "V")
+        h_copy(0, 1, 0, "V")
         relu(0, 1, 2, "S")
         trunk(0, 3, 2)
-        h_copy(0, 1, 0, "V")
-        relu(0, 2, 2, "S")
-        trunk(1, 2, 1)
         b_scale(0, 2, 2)
-        relu(0, 3, 2, "S")
+        trunk(1, 2, 1)
+        relu(0, 2, 2, "S")
         trunk(1, 3, 1)
-        relu(1, 2, 1, "S")
+        relu(0, 3, 2, "S")
         hf_quantize(0, 0, 0, 4)
         h_turn(0, 2, 0)
+        relu(1, 2, 1, "S")
         h_turn(0, 2, 1)
         relu(1, 3, 1, "S")
         h_turn(1, 0, 0)
         h_turn(1, 0, 1)
-        h_copy(0, 2, 1, "S")
         h_copy(0, 2, 0, "V")
+        h_copy(0, 2, 1, "S")
         trunk(1, 0, 2)
-        h_copy(1, 0, 0, "S")
         b_scale(1, 1, 1)
+        h_copy(1, 0, 0, "S")
         trunk(1, 1, 2)
-        h_copy(1, 0, 1, "S")
         hf_quantize(0, 2, 0, 2)
+        h_copy(1, 0, 1, "S")
         trunk(1, 2, 2)
         widen_inv()
-        relu(1, 0, 2, "S")
         h_interleave(1, 0, "V", 0, 512)
+        relu(1, 0, 2, "S")
         trunk(1, 3, 2)
         relu(1, 1, 2, "S")
         policy_mm(0, 0, 0)
         relu(1, 2, 2, "S")
         b_scale(1, 2, 2)
-        relu(1, 3, 2, "S")
         policy_mm(0, 0, 1)
-        hs_quantize(0)
+        relu(1, 3, 2, "S")
         policy_mm(0, 1, 0)
+        hs_quantize(0)
         policy_out(0, 0, 0, "S", True)
         policy_mm(0, 1, 1)
         policy_out(0, 0, 1, "S", True)
         b_quantize()
         policy_mm(0, 2, 0)
         policy_out(0, 1, 0, "S", True)
-        h_interleave(0, 1, "V", 0, 512)
         policy_mm(0, 2, 1)
+        h_interleave(0, 1, "V", 0, 512)
         policy_out(0, 1, 1, "S", True)
         h_interleave(1, 1, "S", 0, 256)
         value_mm(0, 0)
@@ -547,33 +563,33 @@ def tile_policy_value_heads_s8_kernel(
         value_mm(1, 0)
         value_mm(2, 0)
         policy_out(0, 2, 0, "S", True)
-        value_out(0, 0, True)
         value_mm(3, 0)
+        value_out(0, 0, True)
         policy_out(0, 2, 1, "S", True)
         h_interleave(1, 1, "S", 256, 512)
-        value_out(1, 0, True)
         h_turn(1, 1, 0)
-        value_out(2, 0, True)
+        value_out(1, 0, True)
         h_turn(1, 2, 0)
-        h_copy(1, 1, 0, "S")
+        value_out(2, 0, True)
         h_turn(1, 1, 1)
+        h_copy(1, 1, 0, "S")
+        h_turn(1, 2, 1)
         value_out(3, 0, True)
         hs_quantize(1)
-        h_turn(1, 2, 1)
         h_copy(1, 2, 0, "S")
         policy_mm(0, 3, 0)
         h_copy(1, 1, 1, "S")
-        h_interleave(1, 2, "V", 0, 256)
         policy_mm(0, 3, 1)
+        h_interleave(1, 2, "V", 0, 256)
         h_copy(1, 2, 1, "S")
         hf_quantize(1, 1, 0, 2)
         value_mm(0, 1)
         policy_out(0, 3, 0, "S", True)
-        h_interleave(1, 2, "V", 256, 512)
         value_mm(1, 1)
+        h_interleave(1, 2, "V", 256, 512)
+        policy_mm(1, 0, 0)
         policy_out(0, 3, 1, "S", True)
         h_interleave(0, 2, "S", 0, 256)
-        policy_mm(1, 0, 0)
         value_out(0, 1, True)
         value_mm(2, 1)
         value_out(1, 1, True)
@@ -588,8 +604,8 @@ def tile_policy_value_heads_s8_kernel(
         policy_mm(1, 1, 1)
         policy_out(1, 0, 1, "S", True)
         hf_quantize(1, 1, 1, 2)
-        value_mm(0, 2)
         policy_out(1, 1, 0, "S", True)
+        value_mm(0, 2)
         value_mm(1, 2)
         policy_out(1, 1, 1, "S", True)
         policy_mm(1, 2, 0)

@@ -18,9 +18,26 @@ ACT = mybir.ActivationFunctionType
 ALU = mybir.AluOpType
 
 P = 128
-NF = F // 512
-NS = M // 512
-RESULT_BUFS = {1024: 10, 512: 8, 256: 4}
+PACK = 4
+PASS = P * PACK
+BANK = 512
+BANKS = 8
+HALF = BANK // 2
+NF = F // PASS
+NS = M // PASS
+NG = K // PASS
+PLANES = PACK * BANK
+UNIT = 2 * PASS
+VECTOR, SCALAR = "vector", "scalar"
+
+PLANE_BUFS = 8
+GROUPED_BUFS = 4
+TURNED_UNITS = 8
+WIDE_BUFS = 10
+SINGLE_BUFS = 8
+PIECE_BUFS = 4
+W_CUT = 384
+W_FILL = 128
 
 
 def tile_policy_value_heads_s8_kernel(
@@ -35,10 +52,16 @@ def tile_policy_value_heads_s8_kernel(
         def persistent(name, width, dtype):
             return keep.tile([P, width], dtype, name=name, align_bytes=64)
 
+        def staged(name, shape, dtype, tag, bufs):
+            return stage.tile(shape, dtype, name=name, tag=tag, align_bytes=64, bufs=bufs)
+
+        def wide_tile(name, width, dtype):
+            return staged(name, [P, width], dtype, "rows1024", WIDE_BUFS)
+
         banks_taken = []
 
         def new_bank():
-            bank = psum.tile([P, 512], F32, name=f"bank{len(banks_taken) % 8}")
+            bank = psum.tile([P, BANK], F32, name=f"bank{len(banks_taken) % BANKS}")
             banks_taken.append(bank)
             return bank
 
@@ -48,69 +71,39 @@ def tile_policy_value_heads_s8_kernel(
         make_identity(nc, ident[:])
         ps = keep.tile([P, NF, A], U8, name="ps", align_bytes=64)
         nc.vector.memset(ps[:].rearrange("p g n -> p (g n)").bitcast(I32), 0)
-
         one = persistent("one", 1, F32)
         nc.vector.memset(one[:], 1.0)
-        w_raw, x_raw = {}, {}
-        x_view = x.rearrange("(s q t) k -> s q t k", s=NS, t=4)
 
-        def load_w(f, g):
-            w_raw[f, g] = stage.tile([P, 4, 512], BF16, name=f"w_raw{f}{g}", tag="plain", align_bytes=64, bufs=8)
-            nc.sync.dma_start(
-                out=w_raw[f, g][:],
-                in_=w[512 * g : 512 * (g + 1), 512 * f : 512 * (f + 1)].rearrange("(p j) c -> p j c", j=4),
-            )
-
-        def wide_tile(name, dtype):
-            width = 1024 if dtype == F32 else 2048
-            return stage.tile([P, width], dtype, name=name, tag="rows1024", align_bytes=64, bufs=RESULT_BUFS[1024])
-
-        x_pair = {}
-
-        def load_x(s, t, count=1):
-            if t % 2 == 0:
-                x_pair[s, t // 2] = wide_tile(f"x_raw{s}{t}", BF16)
-            rows = x_pair[s, t // 2][:, K * (t % 2) : K * (t % 2 + count)]
-            nc.sync.dma_start(out=rows, in_=x_view[s, :, t : t + count].rearrange("q t k -> q (t k)"))
-            for i in range(count):
-                x_raw[s, t + i] = rows[:, K * i : K * (i + 1)]
-
-        inv16 = keep.tile([P, NS, 4], BF16, name="inv16", align_bytes=64)
-        bscale = keep.tile([P, NS, 4], F32, name="bscale", align_bytes=64)
-
-        def load_bscale():
-            nc.sync.dma_start(out=bscale[:], in_=backup_scale.rearrange("o (s q t) -> q (o s) t", s=NS, t=4))
-
-        def load_inv():
-            nc.sync.dma_start(out=inv16[:], in_=invtemp.rearrange("(s q t) -> q s t", s=NS, t=4))
-
+        w_raw, x_raw, x_pair, b_raw = {}, {}, {}, {}
+        x_view = x.rearrange("(s q t) k -> s q t k", s=NS, t=PACK)
+        b_view = backup_bytes.rearrange("(p j) m -> p j m", j=PACK)
+        inv16 = keep.tile([P, NS, PACK], BF16, name="inv16", align_bytes=64)
+        bscale = keep.tile([P, NS, PACK], F32, name="bscale", align_bytes=64)
         pw = keep.tile([P, NF, 2 * A], U8, name="pw", align_bytes=64)
         vg = persistent("vg", F, BF16)
-        b_raw = {}
-        b_view = backup_bytes.rearrange("(p j) m -> p j m", j=4)
 
-        def load_gain():
-            nc.sync.dma_start(out=vg[:], in_=vgain.partition_broadcast(P))
+        def load_b(j):
+            b_raw[j] = persistent(f"b_raw{j}", M, U8)
+            nc.sync.dma_start(out=b_raw[j][:], in_=b_view[:, j])
 
-        def load_b(j, count):
-            rows = persistent(f"b_raw{j}", count * M, U8)
-            nc.sync.dma_start(out=rows[:], in_=b_view[:, j : j + count].rearrange("p j m -> p (j m)"))
-            for i in range(count):
-                b_raw[j + i] = rows[:, M * i : M * (i + 1)]
+        def load_w(f, g):
+            w_raw[f, g] = staged(f"w_raw{f}{g}", [P, PACK, BANK], BF16, "plain", PLANE_BUFS)
+            nc.sync.dma_start(
+                out=w_raw[f, g][:],
+                in_=w[PASS * g : PASS * (g + 1), BANK * f : BANK * (f + 1)].rearrange("(p j) c -> p j c", j=PACK),
+            )
 
-        def load_p():
-            for c in range(4):
-                nc.sync.dma_start(
-                    out=ps[32 * c : 32 * c + 4].bitcast(I32),
-                    in_=p_scales[:, 4 * c : 4 * c + 4, :].rearrange("g r n -> r g n").bitcast(I32),
-                )
-            nc.sync.dma_start(out=pw[:].bitcast(I32), in_=p_words.rearrange("g p n -> p g n").bitcast(I32))
+        def load_x(s, t):
+            if t % 2 == 0:
+                x_pair[s, t // 2] = wide_tile(f"x_raw{s}{t}", 2 * K, BF16)
+            x_raw[s, t] = x_pair[s, t // 2][:, K * (t % 2) : K * (t % 2 + 1)]
+            nc.sync.dma_start(out=x_raw[s, t], in_=x_view[s, :, t])
 
-        for j in range(4):
-            load_b(j, 1)
+        for j in range(PACK):
+            load_b(j)
         load_w(0, 0)
-        load_bscale()
-        for t in range(4):
+        nc.sync.dma_start(out=bscale[:], in_=backup_scale.rearrange("o (s q t) -> q (o s) t", s=NS, t=PACK))
+        for t in range(PACK):
             load_x(0, t)
         load_w(0, 1)
         load_x(1, 0)
@@ -121,12 +114,17 @@ def tile_policy_value_heads_s8_kernel(
         load_w(1, 1)
         load_w(2, 0)
         load_w(2, 1)
-        load_inv()
-        load_p()
-        load_gain()
+        nc.sync.dma_start(out=inv16[:], in_=invtemp.rearrange("(s q t) -> q s t", s=NS, t=PACK))
+        for c in range(4):
+            nc.sync.dma_start(
+                out=ps[32 * c : 32 * c + 4].bitcast(I32),
+                in_=p_scales[:, 4 * c : 4 * c + 4, :].rearrange("g r n -> r g n").bitcast(I32),
+            )
+        nc.sync.dma_start(out=pw[:].bitcast(I32), in_=p_words.rearrange("g p n -> p g n").bitcast(I32))
+        nc.sync.dma_start(out=vg[:], in_=vgain.partition_broadcast(P))
 
         def copy(engine, out, in_):
-            if engine == "S":
+            if engine == SCALAR:
                 nc.scalar.copy(out=out, in_=in_)
             else:
                 nc.vector.tensor_copy(out=out, in_=in_)
@@ -134,38 +132,19 @@ def tile_policy_value_heads_s8_kernel(
         def mx_tiles(name, columns):
             return persistent(name + "_codes", columns, U32), persistent(name + "_scales", columns, U8)
 
-        def quantize(mx, grouped, lo, hi, shift=0):
+        def quantize(mx, first, grouped):
             codes, scales = mx
-            nc.vector.quantize_mx(
-                out=codes[:, lo:hi].bitcast(FP8X4),
-                scales=scales[:, lo:hi],
-                in_=grouped[:, 4 * (lo - shift) : 4 * (hi - shift)],
-            )
+            last = first + grouped.shape[1] // PACK
+            nc.vector.quantize_mx(out=codes[:, first:last].bitcast(FP8X4), scales=scales[:, first:last], in_=grouped)
 
-        def operand(mx, lo, width):
+        def operand(mx, first, width):
             codes, scales = mx
-            return codes[:, lo : lo + width].bitcast(FP8X4), scales[:, lo : lo + width]
+            return codes[:, first : first + width].bitcast(FP8X4), scales[:, first : first + width]
 
         def interleave(engine, grouped, planes, lo, hi):
-            out = grouped.rearrange("p (c i t) -> p c t i", i=4, t=4)
+            out = grouped.rearrange("p (c i t) -> p c t i", i=4, t=PACK)
             in_ = planes.rearrange("p t (c i) -> p c t i", i=4)
             copy(engine, out[:, lo // 4 : hi // 4], in_[:, lo // 4 : hi // 4])
-
-        inv = persistent("inv", 8, F32)
-
-        def widen_inv():
-            nc.scalar.copy(out=inv[:], in_=inv16[:].rearrange("p s t -> p (s t)"))
-
-        w_mx, w_grp = {}, {}
-
-        def w_interleave(f, g, engine, lo=0, hi=512):
-            if f not in w_grp:
-                w_grp[f] = stage.tile([P, 4096], BF16, name="w_grp", tag="grp", align_bytes=64, bufs=4)
-                w_mx[f] = mx_tiles(f"w{f}", 1024)
-            interleave(engine, w_grp[f][:, 2048 * g : 2048 * (g + 1)], w_raw[f, g][:], lo, hi)
-
-        def w_quantize(f, first, last):
-            quantize(w_mx[f], w_grp[f], 512 * first, 512 * (last + 1))
 
         def turn(sources):
             bank = new_bank()
@@ -180,34 +159,6 @@ def tile_policy_value_heads_s8_kernel(
                 bank[:].rearrange("p (a u q) -> p a q u", a=2, u=2),
             )
 
-        x_bank = {}
-        x_grp = [wide_tile(f"x_grp{a}", BF16) for a in range(2)]
-        x_mx = [mx_tiles(f"x{s}", 1024) for s in range(NS)]
-
-        x_sorted = {}
-
-        def x_sort(s, t, engine):
-            x_sorted[s, t] = stage.tile([P, 512], F32, name="x_sorted", align_bytes=64, bufs=2)
-            copy(
-                engine,
-                x_sorted[s, t][:].rearrange("p (g u q) -> p g u q", g=2, u=2),
-                x_raw[s, t].bitcast(F32).rearrange("p (g q u) -> p g u q", g=2, u=2),
-            )
-
-        def x_turn(s, t):
-            if (s, t) in x_sorted:
-                sources = [x_sorted[s, t][:, P * i : P * (i + 1)] for i in range(4)]
-            else:
-                words = x_raw[s, t].bitcast(F32)
-                sources = [words[:, 256 * g + u : 256 * (g + 1) : 2] for g in range(2) for u in range(2)]
-            x_bank[s, t] = turn(sources)
-
-        def x_copy(s, t, engine):
-            pair_up(engine, x_grp[t // 2][:, 1024 * (t % 2) : 1024 * (t % 2 + 1)], x_bank[s, t])
-
-        def x_quantize(s, t, count=1):
-            quantize(x_mx[s], x_grp[t // 2], 256 * t, 256 * (t + count), 512 * (t // 2))
-
         def product(out, stationary, moving, index, count):
             nc.tensor.matmul_mx(
                 out=out,
@@ -219,82 +170,99 @@ def tile_policy_value_heads_s8_kernel(
                 stop=(index == count - 1),
             )
 
+        inv = persistent("inv", NS * PACK, F32)
+
+        w_mx, w_grp = {}, {}
+
+        def w_interleave(f, g, engine, lo=0, hi=BANK):
+            if f not in w_grp:
+                w_grp[f] = staged("w_grp", [P, NG * PLANES], BF16, "grp", GROUPED_BUFS)
+                w_mx[f] = mx_tiles(f"w{f}", NG * BANK)
+            interleave(engine, w_grp[f][:, PLANES * g : PLANES * (g + 1)], w_raw[f, g][:], lo, hi)
+
+        def w_quantize(f, g):
+            quantize(w_mx[f], BANK * g, w_grp[f][:, PLANES * g : PLANES * (g + 1)])
+
+        x_bank = {}
+        x_grp = [wide_tile(f"x_grp{a}", 2 * UNIT, BF16) for a in range(2)]
+        x_mx = [mx_tiles(f"x{s}", PACK * NG * P) for s in range(NS)]
+
+        def x_staged(t):
+            return x_grp[t // 2][:, UNIT * (t % 2) : UNIT * (t % 2 + 1)]
+
+        def x_turn(s, t):
+            words = x_raw[s, t].bitcast(F32)
+            x_bank[s, t] = turn([words[:, 2 * P * g + u : 2 * P * (g + 1) : 2] for g in range(NG) for u in range(2)])
+
+        def x_copy(s, t):
+            pair_up(SCALAR, x_staged(t), x_bank[s, t])
+
+        def x_quantize(s, t):
+            quantize(x_mx[s], NG * P * t, x_staged(t))
+
         h_bank, h_plain = {}, {}
 
-        def trunk(s, t, f, passes=range(2)):
+        def trunk(s, t, f, passes=range(NG)):
             if (s, t, f) not in h_bank:
                 h_bank[s, t, f] = new_bank()
             for g in passes:
-                product(
-                    h_bank[s, t, f][:], operand(x_mx[s], 256 * t + P * g, P), operand(w_mx[f], 512 * g, 512), g, 2
-                )
+                stationary = operand(x_mx[s], NG * P * t + P * g, P)
+                product(h_bank[s, t, f][:], stationary, operand(w_mx[f], BANK * g, BANK), g, NG)
 
-        def relu(s, t, f, engine):
+        def relu(s, t, f):
             if (s, f) not in h_plain:
-                h_plain[s, f] = stage.tile(
-                    [P, 2048], BF16, name=f"h_plain{s}{f}", tag="plain", align_bytes=64, bufs=8
-                )
-            out = h_plain[s, f][:, 512 * t : 512 * (t + 1)].rearrange("p (u m e) -> p u m e", u=2, e=2)
-            in_ = h_bank[s, t, f][:].rearrange("p (m u e) -> p u m e", u=2, e=2)
-            if engine == "S":
-                nc.scalar.activation(out=out, in_=in_, func=ACT.Relu)
-            else:
-                nc.vector.tensor_relu(out=out, in_=in_)
+                h_plain[s, f] = staged(f"h_plain{s}{f}", [P, PLANES], BF16, "plain", PLANE_BUFS)
+            nc.scalar.activation(
+                out=h_plain[s, f][:, BANK * t : BANK * (t + 1)].rearrange("p (u m e) -> p u m e", u=2, e=2),
+                in_=h_bank[s, t, f][:].rearrange("p (m u e) -> p u m e", u=2, e=2),
+                func=ACT.Relu,
+            )
 
-        ht_bank, hf_place, hs_grp, hs_mx = {}, {}, {}, {}
-        hf_grp = persistent("hf_grp", 8 * 1024, BF16)
-        hf_mx = mx_tiles("hf", 12 * 256)
+        ht_bank, hf_place = {}, {}
+        hf_grp = persistent("hf_grp", TURNED_UNITS * UNIT, BF16)
+        hf_mx = mx_tiles("hf", NS * NF * PASS)
 
         def h_turn(s, f, a):
             hf_place[s, f, a] = len(hf_place)
             words = h_plain[s, f][:].bitcast(F32)
             ht_bank[s, f, a] = turn([words[:, P * i : P * (i + 1)] for i in range(4 * a, 4 * a + 4)])
 
+        def hf_staged(s, f, a, count):
+            first = UNIT * (hf_place[s, f, a] % TURNED_UNITS)
+            return hf_grp[:, first : first + UNIT * count]
+
         def h_copy(s, f, a, engine):
-            first = 1024 * (hf_place[s, f, a] % 8)
-            pair_up(engine, hf_grp[:, first : first + 1024], ht_bank[s, f, a])
+            pair_up(engine, hf_staged(s, f, a, 1), ht_bank[s, f, a])
 
         def hf_quantize(s, f, a, count):
-            place = hf_place[s, f, a]
-            quantize(hf_mx, hf_grp, 256 * place, 256 * (place + count), 256 * (place - place % 8))
+            quantize(hf_mx, 2 * P * hf_place[s, f, a], hf_staged(s, f, a, count))
 
         def hf_operand(s, f, t):
-            return operand(hf_mx, 256 * hf_place[s, f, t // 2] + P * (t % 2), P)
+            return operand(hf_mx, 2 * P * hf_place[s, f, t // 2] + P * (t % 2), P)
 
-        def h_interleave(s, f, engine, lo=0, hi=512):
+        hs_grp, hs_mx = {}, {}
+
+        def h_interleave(s, f, engine, lo=0, hi=BANK):
             if f not in hs_grp:
-                hs_grp[f] = stage.tile([P, 4096], BF16, name="hs_grp", tag="grp", align_bytes=64, bufs=4)
-                hs_mx[f] = mx_tiles(f"hs{f}", 1024)
-            planes = h_plain[s, f][:].rearrange("p (t c) -> p t c", t=4)
-            interleave(engine, hs_grp[f][:, 2048 * s : 2048 * (s + 1)], planes, lo, hi)
+                hs_grp[f] = staged("hs_grp", [P, NS * PLANES], BF16, "grp", GROUPED_BUFS)
+                hs_mx[f] = mx_tiles(f"hs{f}", NS * BANK)
+            planes = h_plain[s, f][:].rearrange("p (t c) -> p t c", t=PACK)
+            interleave(engine, hs_grp[f][:, PLANES * s : PLANES * (s + 1)], planes, lo, hi)
 
-        def h_interleave_pool(s, f, lo, hi):
-            if f not in hs_grp:
-                hs_grp[f] = stage.tile([P, 4096], BF16, name="hs_grp", tag="grp", align_bytes=64, bufs=4)
-                hs_mx[f] = mx_tiles(f"hs{f}", 1024)
-            nc.gpsimd.tensor_scalar(
-                out=hs_grp[f][:, 2048 * s : 2048 * (s + 1)].rearrange("p (c t) -> p c t", t=4)[:, lo:hi],
-                in0=h_plain[s, f][:].rearrange("p (t c) -> p c t", t=4)[:, lo:hi],
-                scalar1=1.0,
-                scalar2=0.0,
-                op0=ALU.mult,
-                op1=ALU.add,
-            )
-
-        def hs_quantize(f, first=0, last=1):
-            quantize(hs_mx[f], hs_grp[f], 512 * first, 512 * (last + 1))
+        def hs_quantize(f):
+            quantize(hs_mx[f], 0, hs_grp[f][:])
 
         b_bank = {}
-        b_pair = [wide_tile(f"b_wide{a}", BF16) for a in range(2)]
-        b_wide = [b_pair[j // 2][:, M * (j % 2) : M * (j % 2 + 1)] for j in range(4)]
-        b_turned = [wide_tile(f"b_turned{a}", BF16) for a in range(2)]
-        b_grp = persistent("b_grp", NS * 2048, BF16)
-        b_mx = mx_tiles("b", 1024)
+        b_pair = [wide_tile(f"b_wide{a}", 2 * M, BF16) for a in range(2)]
+        b_wide = [b_pair[j // 2][:, M * (j % 2) : M * (j % 2 + 1)] for j in range(PACK)]
+        b_turned = [wide_tile(f"b_turned{a}", 2 * M, BF16) for a in range(2)]
+        b_grp = persistent("b_grp", NS * PACK * PASS, BF16)
+        b_mx = mx_tiles("b", NS * R)
 
         def b_widen(j):
             nc.vector.tensor_scalar(
                 out=b_wide[j].rearrange("p (u q e) -> p q u e", u=2, e=2),
-                in0=b_raw[j].bitcast(FP8).rearrange("p (q u e) -> p q u e", u=2, e=2),
+                in0=b_raw[j][:].bitcast(FP8).rearrange("p (q u e) -> p q u e", u=2, e=2),
                 scalar1=one[:],
                 scalar2=None,
                 op0=ALU.mult,
@@ -302,50 +270,37 @@ def tile_policy_value_heads_s8_kernel(
 
         def b_turn(j):
             words = b_wide[j].bitcast(F32)
-            starts = [256 * u + P * s for s in range(NS) for u in range(2)]
+            starts = [NS * P * u + P * s for s in range(NS) for u in range(2)]
             b_bank[j] = turn([words[:, c : c + P] for c in starts])
 
-        def b_copy(j, engine):
-            copy(
-                engine,
-                b_turned[j // 2][:].bitcast(F32).rearrange("p (s j q u) -> p j s q u", s=NS, j=2, u=2)[:, j % 2],
-                b_bank[j][:].rearrange("p (s u q) -> p s q u", s=NS, u=2),
+        def b_copy(j):
+            nc.scalar.copy(
+                out=b_turned[j // 2][:].bitcast(F32).rearrange("p (s j q u) -> p j s q u", s=NS, j=2, u=2)[:, j % 2],
+                in_=b_bank[j][:].rearrange("p (s u q) -> p s q u", s=NS, u=2),
             )
 
-        def b_scale(s, j, count):
-            cols = slice(2048 * s + 512 * j, 2048 * s + 512 * (j + count))
-            first = 1024 * s + 512 * (j % 2)
+        def b_scale(s, j, count=1):
+            source, target = UNIT * s + PASS * (j % 2), PACK * PASS * s + PASS * j
             nc.vector.tensor_tensor(
-                out=b_grp[:, cols].rearrange("p (r t) -> p r t", t=4),
-                in0=b_turned[j // 2][:, first : first + 512 * count].rearrange("p (r t) -> p r t", t=4),
-                in1=bscale[:, s, :].unsqueeze(1).to_broadcast([P, P * count, 4]),
+                out=b_grp[:, target : target + PASS * count].rearrange("p (r t) -> p r t", t=PACK),
+                in0=b_turned[j // 2][:, source : source + PASS * count].rearrange("p (r t) -> p r t", t=PACK),
+                in1=bscale[:, s, :].unsqueeze(1).to_broadcast([P, P * count, PACK]),
                 op=ALU.mult,
             )
 
-        def b_scale_out(j, s):
-            first = 2048 * s + 512 * j
-            nc.vector.tensor_tensor(
-                out=b_grp[:, first : first + 512].rearrange("p (r u e) -> p r u e", u=2, e=2),
-                in0=b_bank[j][:, 256 * s : 256 * (s + 1)].bitcast(BF16).rearrange("p (u r e) -> p r u e", u=2, e=2),
-                in1=bscale[:, s, :].rearrange("p (u e) -> p u e", u=2).unsqueeze(1).to_broadcast([P, P, 2, 2]),
-                op=ALU.mult,
-            )
-
-        def b_quantize(first=0, last=1):
-            quantize(b_mx, b_grp, 512 * first, 512 * (last + 1))
-
-        p_view = policy.rearrange("(s q t) a -> s t q a", s=NS, t=4)
-        v_view = value.rearrange("(p j) f -> p j f", j=4)
+        p_view = policy.rearrange("(s q t) a -> s t q a", s=NS, t=PACK)
+        v_view = value.rearrange("(p j) f -> p j f", j=PACK)
         p_bank, p_rows, v_bank, v_rows = {}, {}, {}, {}
 
-        def p_operand(f, lo, width):
-            return pw[:, f, 2 * lo : 2 * (lo + width)].bitcast(FP4X4), ps[:, f, lo : lo + width]
+        def single_tile():
+            return staged("result", [P, BANK], F32, "rows512", SINGLE_BUFS)
 
-        def result_tile(width):
-            return stage.tile([P, width], F32, name="result", tag=f"rows{width}", align_bytes=64, bufs=RESULT_BUFS[width])
+        def p_operand(f, first, width):
+            return pw[:, f, 2 * first : 2 * (first + width)].bitcast(FP4X4), ps[:, f, first : first + width]
 
-        def scaled_copy(engine, out, in_, factor):
-            if engine == "S":
+        def scaled_copy(engine, out, in_, s, t):
+            factor = inv[:, PACK * s + t : PACK * s + t + 1]
+            if engine == SCALAR:
                 nc.scalar.activation(out=out, in_=in_, func=ACT.Copy, scale=factor)
             else:
                 nc.vector.tensor_scalar(out=out, in0=in_, scalar1=factor, scalar2=None, op0=ALU.mult)
@@ -353,276 +308,197 @@ def tile_policy_value_heads_s8_kernel(
         def policy_mm(s, t, n):
             p_bank[s, t, n] = new_bank()
             for f in range(NF):
-                product(p_bank[s, t, n][:], hf_operand(s, f, t), p_operand(f, 512 * n, 512), f, NF)
+                product(p_bank[s, t, n][:], hf_operand(s, f, t), p_operand(f, BANK * n, BANK), f, NF)
 
-        def policy_out(s, t, n, engine, whole_rows):
-            factor = inv[:, 4 * s + t : 4 * s + t + 1]
-            if whole_rows:
-                if n == 0:
-                    p_rows[s, t] = result_tile(1024)
-                scaled_copy(engine, p_rows[s, t][:, 512 * n : 512 * (n + 1)], p_bank[s, t, n][:], factor)
-                if n == 1:
-                    nc.sync.dma_start(out=p_view[s, t], in_=p_rows[s, t][:])
-            else:
-                result = result_tile(512)
-                scaled_copy(engine, result[:], p_bank[s, t, n][:], factor)
-                nc.sync.dma_start(out=p_view[s, t, :, 512 * n : 512 * (n + 1)], in_=result[:])
+        def policy_rows(s, t, n):
+            if n == 0:
+                p_rows[s, t] = wide_tile("result", A, F32)
+            scaled_copy(SCALAR, p_rows[s, t][:, BANK * n : BANK * (n + 1)], p_bank[s, t, n][:], s, t)
+            if n == 1:
+                nc.sync.dma_start(out=p_view[s, t], in_=p_rows[s, t][:])
 
-        def piece_mm(s, t, first, count):
-            p_bank[s, t, 2 + first] = new_bank()
-            for j in range(count):
+        def policy_single(s, t, n, engine):
+            result = single_tile()
+            scaled_copy(engine, result[:], p_bank[s, t, n][:], s, t)
+            nc.sync.dma_start(out=p_view[s, t, :, BANK * n : BANK * (n + 1)], in_=result[:])
+
+        def policy_piece(s, t, c, engine):
+            bank = new_bank()
+            for j in range(2):
                 for f in range(NF):
-                    moving = p_operand(f, P * (first + j), P)
-                    product(p_bank[s, t, 2 + first][:, P * j : P * (j + 1)], hf_operand(s, f, t), moving, f, NF)
-
-        def piece_out(s, t, first, count, engine):
-            result = result_tile(256)
-            width = P * count
-            factor = inv[:, 4 * s + t : 4 * s + t + 1]
-            scaled_copy(engine, result[:, 0:width], p_bank[s, t, 2 + first][:, 0:width], factor)
-            nc.sync.dma_start(out=p_view[s, t, :, P * first : P * first + width], in_=result[:, 0:width])
+                    moving = p_operand(f, HALF * c + P * j, P)
+                    product(bank[:, P * j : P * (j + 1)], hf_operand(s, f, t), moving, f, NF)
+            result = staged("result", [P, HALF], F32, "rows256", PIECE_BUFS)
+            scaled_copy(engine, result[:], bank[:, 0:HALF], s, t)
+            nc.sync.dma_start(out=p_view[s, t, :, HALF * c : HALF * (c + 1)], in_=result[:])
 
         def value_mm(j, f):
             v_bank[j, f] = new_bank()
             for s in range(NS):
-                product(v_bank[j, f][:], operand(b_mx, 512 * s + P * j, P), operand(hs_mx[f], 512 * s, 512), s, NS)
+                product(v_bank[j, f][:], operand(b_mx, R * s + P * j, P), operand(hs_mx[f], BANK * s, BANK), s, NS)
 
-        def value_out(j, f, paired):
-            cols = slice(512 * f, 512 * (f + 1))
-            if paired:
-                if j % 2 == 0:
-                    v_rows[f] = result_tile(1024)
-                result = v_rows[f][:, 512 * (j % 2) : 512 * (j % 2 + 1)]
-            else:
-                single = result_tile(512)
-                result = single[:]
+        def apply_gain(j, f, result):
             nc.vector.tensor_tensor(
                 out=result.rearrange("p (m u e) -> p m u e", u=2, e=2),
                 in0=v_bank[j, f][:].rearrange("p (u m e) -> p m u e", u=2, e=2),
-                in1=vg[:, cols].rearrange("p (m u e) -> p m u e", u=2, e=2),
+                in1=vg[:, BANK * f : BANK * (f + 1)].rearrange("p (m u e) -> p m u e", u=2, e=2),
                 op=ALU.mult,
             )
-            if not paired:
-                nc.sync.dma_start(out=v_view[:, j, cols], in_=result)
-            elif j % 2 == 1:
+
+        def value_paired(j, f):
+            if j % 2 == 0:
+                v_rows[f] = wide_tile("result", 2 * BANK, F32)
+            apply_gain(j, f, v_rows[f][:, BANK * (j % 2) : BANK * (j % 2 + 1)])
+            if j % 2 == 1:
                 nc.sync.dma_start(
-                    out=v_view[:, j - 1 : j + 1, cols], in_=v_rows[f][:].rearrange("p (j c) -> p j c", j=2)
+                    out=v_view[:, j - 1 : j + 1, BANK * f : BANK * (f + 1)],
+                    in_=v_rows[f][:].rearrange("p (j c) -> p j c", j=2),
                 )
 
-        b_widen(0)
-        b_widen(1)
-        b_turn(0)
-        b_widen(2)
-        b_turn(1)
-        b_widen(3)
-        b_copy(0, "S")
-        b_turn(2)
-        w_interleave(0, 0, "V", 0, 512)
-        b_copy(1, "S")
-        b_turn(3)
-        b_copy(2, "S")
-        x_turn(0, 0)
-        b_scale(0, 0, 1)
-        b_copy(3, "S")
-        x_turn(0, 1)
-        x_copy(0, 0, "S")
-        w_quantize(0, 0, 0)
-        x_turn(0, 2)
-        b_scale(1, 0, 1)
-        x_copy(0, 1, "S")
-        x_turn(0, 3)
-        x_quantize(0, 0, 1)
-        x_copy(0, 2, "S")
-        x_quantize(0, 1, 1)
-        trunk(0, 0, 0, [0])
-        w_interleave(0, 1, "V", 0, 384)
-        x_copy(0, 3, "S")
-        trunk(0, 1, 0, [0])
-        w_interleave(0, 1, "S", 384, 512)
-        x_quantize(0, 2, 1)
-        x_turn(1, 0)
-        x_quantize(0, 3, 1)
-        w_quantize(0, 1, 1)
-        x_turn(1, 1)
-        x_copy(1, 0, "S")
-        w_interleave(1, 0, "V", 0, 384)
-        trunk(0, 2, 0, [0])
-        trunk(0, 3, 0, [0])
-        x_copy(1, 1, "S")
-        trunk(0, 0, 0, [1])
-        x_quantize(1, 0, 1)
-        trunk(0, 1, 0, [1])
-        w_interleave(1, 0, "S", 384, 512)
-        trunk(0, 2, 0, [1])
-        x_quantize(1, 1, 1)
-        trunk(0, 3, 0, [1])
-        x_turn(1, 2)
-        w_quantize(1, 0, 0)
-        x_turn(1, 3)
-        w_interleave(1, 1, "V", 0, 256)
-        relu(0, 0, 0, "S")
-        b_scale(0, 1, 1)
-        relu(0, 1, 0, "S")
-        trunk(1, 0, 0)
-        x_copy(1, 2, "S")
-        trunk(1, 1, 0)
-        x_copy(1, 3, "S")
-        x_quantize(1, 2, 1)
-        trunk(0, 0, 1, [0])
-        relu(0, 2, 0, "S")
-        trunk(0, 1, 1, [0])
-        x_quantize(1, 3, 1)
-        relu(0, 3, 0, "S")
-        w_interleave(1, 1, "V", 256, 512)
-        trunk(1, 2, 0)
-        relu(1, 0, 0, "S")
-        w_interleave(2, 0, "V", 0, 128)
-        trunk(1, 3, 0)
-        w_quantize(1, 1, 1)
-        relu(1, 1, 0, "S")
-        trunk(0, 2, 1, [0])
-        w_interleave(2, 0, "V", 128, 512)
-        relu(1, 2, 0, "S")
-        trunk(0, 3, 1, [0])
-        trunk(0, 0, 1, [1])
-        trunk(0, 1, 1, [1])
-        relu(1, 3, 0, "S")
-        trunk(0, 2, 1, [1])
-        w_interleave(2, 1, "V", 0, 512)
-        trunk(0, 3, 1, [1])
-        relu(0, 0, 1, "S")
-        trunk(1, 0, 1)
-        relu(0, 1, 1, "S")
-        trunk(1, 1, 1)
-        w_quantize(2, 0, 0)
-        relu(0, 2, 1, "S")
-        h_turn(0, 0, 0)
-        w_quantize(2, 1, 1)
-        h_turn(0, 0, 1)
-        relu(0, 3, 1, "S")
-        h_turn(0, 1, 0)
-        h_interleave(0, 0, "V", 0, 512)
-        h_turn(0, 1, 1)
-        relu(1, 0, 1, "S")
-        relu(1, 1, 1, "S")
-        trunk(0, 0, 2)
-        h_copy(0, 0, 0, "V")
-        h_copy(0, 1, 1, "S")
-        trunk(0, 1, 2)
-        h_copy(0, 0, 1, "V")
-        relu(0, 0, 2, "S")
-        trunk(0, 2, 2)
-        h_copy(0, 1, 0, "V")
-        relu(0, 1, 2, "S")
-        trunk(0, 3, 2)
+        def value_single(j, f):
+            result = single_tile()
+            apply_gain(j, f, result[:])
+            nc.sync.dma_start(out=v_view[:, j, BANK * f : BANK * (f + 1)], in_=result[:])
+
+        for j in range(PACK):
+            b_widen(j)
+            b_turn(j)
+            b_copy(j)
+        w_interleave(0, 0, VECTOR)
+        b_scale(0, 0)
+        w_quantize(0, 0)
+        b_scale(1, 0)
+
+        for t in range(PACK):
+            x_turn(0, t)
+            x_copy(0, t)
+        for t in (0, 1):
+            x_quantize(0, t)
+            trunk(0, t, 0, [0])
+        w_interleave(0, 1, VECTOR, 0, W_CUT)
+        w_interleave(0, 1, SCALAR, W_CUT)
+        for t in (2, 3):
+            x_quantize(0, t)
+        w_quantize(0, 1)
+        for t in (0, 1):
+            x_turn(1, t)
+            x_copy(1, t)
+        for t in (2, 3):
+            trunk(0, t, 0, [0])
+        for t in range(PACK):
+            trunk(0, t, 0, [1])
+        w_interleave(1, 0, VECTOR, 0, W_CUT)
+        w_interleave(1, 0, SCALAR, W_CUT)
+        for t in (0, 1):
+            x_quantize(1, t)
+        w_quantize(1, 0)
+        for t in (0, 1):
+            relu(0, t, 0)
+
+        for t in (2, 3):
+            x_turn(1, t)
+            x_copy(1, t)
+        w_interleave(1, 1, VECTOR, 0, HALF)
+        b_scale(0, 1)
+        for t in (2, 3):
+            x_quantize(1, t)
+        for t in (0, 1):
+            trunk(1, t, 0)
+        for t in (0, 1):
+            trunk(0, t, 1, [0])
+        for t in (2, 3):
+            relu(0, t, 0)
+            trunk(1, t, 0)
+        w_interleave(1, 1, VECTOR, HALF)
+        w_interleave(2, 0, VECTOR, 0, W_FILL)
+        w_quantize(1, 1)
+        for t in range(PACK):
+            relu(1, t, 0)
+        for t in (2, 3):
+            trunk(0, t, 1, [0])
+        for t in range(PACK):
+            trunk(0, t, 1, [1])
+            relu(0, t, 1)
+        w_interleave(2, 0, VECTOR, W_FILL)
+        w_interleave(2, 1, VECTOR)
+        for g in range(NG):
+            w_quantize(2, g)
+        h_interleave(0, 0, VECTOR)
+
+        for t in (0, 1):
+            trunk(1, t, 1)
+            relu(1, t, 1)
+        for f, a, engine in ((0, 0, VECTOR), (0, 1, VECTOR), (1, 0, VECTOR), (1, 1, SCALAR)):
+            h_turn(0, f, a)
+            h_copy(0, f, a, engine)
         b_scale(0, 2, 2)
-        trunk(1, 2, 1)
-        relu(0, 2, 2, "S")
-        trunk(1, 3, 1)
-        relu(0, 3, 2, "S")
         hf_quantize(0, 0, 0, 4)
-        h_turn(0, 2, 0)
-        relu(1, 2, 1, "S")
-        h_turn(0, 2, 1)
-        relu(1, 3, 1, "S")
-        h_turn(1, 0, 0)
-        h_turn(1, 0, 1)
-        h_copy(0, 2, 0, "V")
-        h_copy(0, 2, 1, "S")
-        trunk(1, 0, 2)
-        b_scale(1, 1, 1)
-        h_copy(1, 0, 0, "S")
-        trunk(1, 1, 2)
+        for t in range(PACK):
+            trunk(0, t, 2)
+            relu(0, t, 2)
+        for t in (2, 3):
+            trunk(1, t, 1)
+            relu(1, t, 1)
+        for s, f, a, engine in ((0, 2, 0, VECTOR), (0, 2, 1, SCALAR), (1, 0, 0, SCALAR), (1, 0, 1, SCALAR)):
+            h_turn(s, f, a)
+            h_copy(s, f, a, engine)
+        b_scale(1, 1)
         hf_quantize(0, 2, 0, 2)
-        h_copy(1, 0, 1, "S")
-        trunk(1, 2, 2)
-        widen_inv()
-        h_interleave(1, 0, "V", 0, 512)
-        relu(1, 0, 2, "S")
-        trunk(1, 3, 2)
-        relu(1, 1, 2, "S")
-        policy_mm(0, 0, 0)
-        relu(1, 2, 2, "S")
+        nc.scalar.copy(out=inv[:], in_=inv16[:].rearrange("p s t -> p (s t)"))
+        for t in range(PACK):
+            trunk(1, t, 2)
+            relu(1, t, 2)
+
+        h_interleave(1, 0, VECTOR)
         b_scale(1, 2, 2)
-        policy_mm(0, 0, 1)
-        relu(1, 3, 2, "S")
-        policy_mm(0, 1, 0)
         hs_quantize(0)
-        policy_out(0, 0, 0, "S", True)
-        policy_mm(0, 1, 1)
-        policy_out(0, 0, 1, "S", True)
-        b_quantize()
-        policy_mm(0, 2, 0)
-        policy_out(0, 1, 0, "S", True)
-        policy_mm(0, 2, 1)
-        h_interleave(0, 1, "V", 0, 512)
-        policy_out(0, 1, 1, "S", True)
-        h_interleave(1, 1, "S", 0, 256)
-        value_mm(0, 0)
+        quantize(b_mx, 0, b_grp[:])
+        h_interleave(0, 1, VECTOR)
         hf_quantize(1, 0, 0, 2)
-        value_mm(1, 0)
-        value_mm(2, 0)
-        policy_out(0, 2, 0, "S", True)
-        value_mm(3, 0)
-        value_out(0, 0, True)
-        policy_out(0, 2, 1, "S", True)
-        h_interleave(1, 1, "S", 256, 512)
-        h_turn(1, 1, 0)
-        value_out(1, 0, True)
-        h_turn(1, 2, 0)
-        value_out(2, 0, True)
-        h_turn(1, 1, 1)
-        h_copy(1, 1, 0, "S")
-        h_turn(1, 2, 1)
-        value_out(3, 0, True)
+        for t in range(3):
+            for n in range(2):
+                policy_mm(0, t, n)
+            if t == 2:
+                h_interleave(1, 1, SCALAR, 0, HALF)
+            for n in range(2):
+                policy_rows(0, t, n)
+        h_interleave(1, 1, SCALAR, HALF)
+        for j in range(PACK):
+            value_mm(j, 0)
+            value_paired(j, 0)
         hs_quantize(1)
-        h_copy(1, 2, 0, "S")
-        policy_mm(0, 3, 0)
-        h_copy(1, 1, 1, "S")
-        policy_mm(0, 3, 1)
-        h_interleave(1, 2, "V", 0, 256)
-        h_copy(1, 2, 1, "S")
+
+        for a in range(2):
+            for f in (1, 2):
+                h_turn(1, f, a)
+                h_copy(1, f, a, SCALAR)
+        h_interleave(1, 2, VECTOR, 0, HALF)
         hf_quantize(1, 1, 0, 2)
-        value_mm(0, 1)
-        policy_out(0, 3, 0, "S", True)
-        value_mm(1, 1)
-        h_interleave(1, 2, "V", 256, 512)
-        policy_mm(1, 0, 0)
-        policy_out(0, 3, 1, "S", True)
-        h_interleave(0, 2, "S", 0, 256)
-        value_out(0, 1, True)
-        value_mm(2, 1)
-        value_out(1, 1, True)
-        h_interleave(0, 2, "V", 256, 512)
-        value_mm(3, 1)
-        policy_out(1, 0, 0, "S", True)
-        policy_mm(1, 0, 1)
-        value_out(2, 1, True)
-        policy_mm(1, 1, 0)
-        value_out(3, 1, True)
+        h_interleave(1, 2, VECTOR, HALF)
+        for n in range(2):
+            policy_mm(0, 3, n)
+            policy_rows(0, 3, n)
+        h_interleave(0, 2, SCALAR, 0, HALF)
+
+        for n in range(2):
+            for j in (2 * n, 2 * n + 1):
+                value_mm(j, 1)
+                value_paired(j, 1)
+            if n == 0:
+                h_interleave(0, 2, VECTOR, HALF)
+            policy_mm(1, 0, n)
+            policy_rows(1, 0, n)
         hs_quantize(2)
-        policy_mm(1, 1, 1)
-        policy_out(1, 0, 1, "S", True)
         hf_quantize(1, 1, 1, 2)
-        policy_out(1, 1, 0, "S", True)
-        value_mm(0, 2)
-        value_mm(1, 2)
-        policy_out(1, 1, 1, "S", True)
-        policy_mm(1, 2, 0)
-        value_out(0, 2, False)
-        value_mm(2, 2)
-        value_out(1, 2, False)
-        value_mm(3, 2)
-        policy_out(1, 2, 0, "S", False)
-        policy_mm(1, 2, 1)
-        value_out(2, 2, False)
-        piece_mm(1, 3, 0, 2)
-        value_out(3, 2, False)
-        piece_mm(1, 3, 2, 2)
-        piece_mm(1, 3, 4, 2)
-        policy_out(1, 2, 1, "S", False)
-        piece_out(1, 3, 0, 2, "V")
-        piece_mm(1, 3, 6, 2)
-        piece_out(1, 3, 2, 2, "S")
-        piece_out(1, 3, 4, 2, "V")
-        piece_out(1, 3, 6, 2, "S")
+        for n in range(2):
+            policy_mm(1, 1, n)
+            policy_rows(1, 1, n)
+
+        for n in range(2):
+            for j in (2 * n, 2 * n + 1):
+                value_mm(j, 2)
+                value_single(j, 2)
+            policy_mm(1, 2, n)
+            policy_single(1, 2, n, SCALAR)
+        for c, engine in enumerate((VECTOR, SCALAR, VECTOR, SCALAR)):
+            policy_piece(1, 3, c, engine)

@@ -34,8 +34,7 @@ PLANE_BUFS = 8
 GROUPED_BUFS = 4
 TURNED_UNITS = 8
 WIDE_BUFS = 10
-SINGLE_BUFS = 8
-PIECE_BUFS = 4
+SINGLE_BUFS = 10
 W_CUT = 384
 W_FILL = 128
 
@@ -70,9 +69,11 @@ def tile_policy_value_heads_s8_kernel(
         ident = persistent("ident", P, F32)
         make_identity(nc, ident[:])
         ps = keep.tile([P, NF, A], U8, name="ps", align_bytes=64)
-        nc.vector.memset(ps[:].rearrange("p g n -> p (g n)").bitcast(I32), 0)
         one = persistent("one", 1, F32)
         nc.vector.memset(one[:], 1.0)
+        ps_words = ps[:].rearrange("p g n -> p (g n)").bitcast(I32)
+        for part in (ps_words[:, 0:1], ps_words[:, 1:]):
+            nc.vector.memset(part, 0)
 
         w_raw, x_raw, x_pair, b_raw = {}, {}, {}, {}
         x_view = x.rearrange("(s q t) k -> s q t k", s=NS, t=PACK)
@@ -322,15 +323,19 @@ def tile_policy_value_heads_s8_kernel(
             scaled_copy(engine, result[:], p_bank[s, t, n][:], s, t)
             nc.sync.dma_start(out=p_view[s, t, :, BANK * n : BANK * (n + 1)], in_=result[:])
 
-        def policy_piece(s, t, c, engine):
-            bank = new_bank()
-            for j in range(2):
-                for f in range(NF):
-                    moving = p_operand(f, HALF * c + P * j, P)
-                    product(bank[:, P * j : P * (j + 1)], hf_operand(s, f, t), moving, f, NF)
-            result = staged("result", [P, HALF], F32, "rows256", PIECE_BUFS)
-            scaled_copy(engine, result[:], bank[:, 0:HALF], s, t)
-            nc.sync.dma_start(out=p_view[s, t, :, HALF * c : HALF * (c + 1)], in_=result[:])
+        def policy_parts(s, t, n, parts):
+            result = single_tile()
+            first = 0
+            for engine, widths in parts:
+                bank, done = new_bank(), 0
+                for width in widths:
+                    for f in range(NF):
+                        moving = p_operand(f, BANK * n + first + done, width)
+                        product(bank[:, done : done + width], hf_operand(s, f, t), moving, f, NF)
+                    done += width
+                scaled_copy(engine, result[:, first : first + done], bank[:, 0:done], s, t)
+                first += done
+            nc.sync.dma_start(out=p_view[s, t, :, BANK * n : BANK * (n + 1)], in_=result[:])
 
         def value_mm(j, f):
             v_bank[j, f] = new_bank()
@@ -478,14 +483,14 @@ def tile_policy_value_heads_s8_kernel(
         for n in range(2):
             policy_mm(0, 3, n)
             policy_rows(0, 3, n)
-        h_interleave(0, 2, SCALAR, 0, HALF)
+        h_interleave(0, 2, SCALAR, 0, W_CUT)
 
         for n in range(2):
             for j in (2 * n, 2 * n + 1):
                 value_mm(j, 1)
                 value_paired(j, 1)
             if n == 0:
-                h_interleave(0, 2, VECTOR, HALF)
+                h_interleave(0, 2, VECTOR, W_CUT)
             policy_mm(1, 0, n)
             policy_rows(1, 0, n)
         hs_quantize(2)
@@ -500,5 +505,5 @@ def tile_policy_value_heads_s8_kernel(
                 value_single(j, 2)
             policy_mm(1, 2, n)
             policy_single(1, 2, n, SCALAR)
-        for c, engine in enumerate((VECTOR, SCALAR, VECTOR, SCALAR)):
-            policy_piece(1, 3, c, engine)
+        policy_parts(1, 3, 0, ((VECTOR, [HALF]), (VECTOR, [HALF])))
+        policy_parts(1, 3, 1, ((VECTOR, [HALF]), (SCALAR, [HALF])))

from contextlib import ExitStack

import concourse.mybir as mybir
from concourse.masks import make_identity

M, K, F, A, R = 1024, 1024, 1536, 1024, 512
FLOPS = 2 * (M * K * F + M * F * A + R * M * F)

F32 = mybir.dt.float32
BF16 = mybir.dt.bfloat16
I32 = mybir.dt.int32
U32 = mybir.dt.uint32
U8 = mybir.dt.uint8
FP8 = mybir.dt.float8_e4m3fn
FP8X4 = mybir.dt.float8_e4m3fn_x4
FP4X4 = mybir.dt.float4_e2m1fn_x4
ACT = mybir.ActivationFunctionType
ALU = mybir.AluOpType

P = 128
PACK = 4
PASS = P * PACK
BANK = 512
BANKS = 8
HALF = BANK // 2
NF = F // PASS
NS = M // PASS
NG = K // PASS
PLANES = PACK * BANK
UNIT = 2 * PASS
VECTOR, SCALAR = "vector", "scalar"

PLANE_BUFS = 8
GROUPED_BUFS = 4
TURNED_UNITS = 8
WIDE_BUFS = 10
SINGLE_BUFS = 10
W_CUT = 384
W_FILL = 128


def tile_policy_value_heads_s8_kernel(
    tc, x, w, p_words, p_scales, backup_bytes, backup_scale, invtemp, vgain, policy, value
):
    nc = tc.nc
    with ExitStack() as ctx:
        keep = ctx.enter_context(tc.tile_pool(name="keep", bufs=1))
        stage = ctx.enter_context(tc.tile_pool(name="stage", bufs=3))
        psum = ctx.enter_context(tc.psum_pool(name="psum", bufs=1))

        def persistent(name, width, dtype):
            return keep.tile([P, width], dtype, name=name, align_bytes=64)

        def staged(name, shape, dtype, tag, bufs):
            return stage.tile(shape, dtype, name=name, tag=tag, align_bytes=64, bufs=bufs)

        def wide_tile(name, width, dtype):
            return staged(name, [P, width], dtype, "rows1024", WIDE_BUFS)

        banks_taken = []

        def new_bank():
            bank = psum.tile([P, BANK], F32, name=f"bank{len(banks_taken) % BANKS}")
            banks_taken.append(bank)
            return bank

        ctx.enter_context(tc.manual_schedule())

        ident = persistent("ident", P, F32)
        make_identity(nc, ident[:])
        ps = keep.tile([P, NF, A], U8, name="ps", align_bytes=64)
        one = persistent("one", 1, F32)
        nc.vector.memset(one[:], 1.0)
        ps_words = ps[:].rearrange("p g n -> p (g n)").bitcast(I32)
        for part in (ps_words[:, 0:1], ps_words[:, 1:]):
            nc.vector.memset(part, 0)

        w_raw, x_raw, x_pair, b_raw = {}, {}, {}, {}
        x_view = x.rearrange("(s q t) k -> s q t k", s=NS, t=PACK)
        b_view = backup_bytes.rearrange("(p j) m -> p j m", j=PACK)
        inv16 = keep.tile([P, NS, PACK], BF16, name="inv16", align_bytes=64)
        bscale = keep.tile([P, NS, PACK], F32, name="bscale", align_bytes=64)
        pw = keep.tile([P, NF, 2 * A], U8, name="pw", align_bytes=64)
        vg = persistent("vg", F, BF16)

        def load_b(j):
            b_raw[j] = persistent(f"b_raw{j}", M, U8)
            nc.sync.dma_start(out=b_raw[j][:], in_=b_view[:, j])

        def load_w(f, g):
            w_raw[f, g] = staged(f"w_raw{f}{g}", [P, PACK, BANK], BF16, "plain", PLANE_BUFS)
            nc.sync.dma_start(
                out=w_raw[f, g][:],
                in_=w[PASS * g : PASS * (g + 1), BANK * f : BANK * (f + 1)].rearrange("(p j) c -> p j c", j=PACK),
            )

        def load_x(s, t):
            if t % 2 == 0:
                x_pair[s, t // 2] = wide_tile(f"x_raw{s}{t}", 2 * K, BF16)
            x_raw[s, t] = x_pair[s, t // 2][:, K * (t % 2) : K * (t % 2 + 1)]
            nc.sync.dma_start(out=x_raw[s, t], in_=x_view[s, :, t])

        for j in range(PACK):
            load_b(j)
        load_w(0, 0)
        nc.sync.dma_start(out=bscale[:], in_=backup_scale.rearrange("o (s q t) -> q (o s) t", s=NS, t=PACK))
        for t in range(PACK):
            load_x(0, t)
        load_w(0, 1)
        load_x(1, 0)
        load_x(1, 1)
        load_w(1, 0)
        load_x(1, 2)
        load_x(1, 3)
        load_w(1, 1)
        load_w(2, 0)
        load_w(2, 1)
        nc.sync.dma_start(out=inv16[:], in_=invtemp.rearrange("(s q t) -> q s t", s=NS, t=PACK))
        for c in range(4):
            nc.sync.dma_start(
                out=ps[32 * c : 32 * c + 4].bitcast(I32),
                in_=p_scales[:, 4 * c : 4 * c + 4, :].rearrange("g r n -> r g n").bitcast(I32),
            )
        nc.sync.dma_start(out=pw[:].bitcast(I32), in_=p_words.rearrange("g p n -> p g n").bitcast(I32))
        nc.sync.dma_start(out=vg[:], in_=vgain.partition_broadcast(P))

        def copy(engine, out, in_):
            if engine == SCALAR:
                nc.scalar.copy(out=out, in_=in_)
            else:
                nc.vector.tensor_copy(out=out, in_=in_)

        def mx_tiles(name, columns):
            return persistent(name + "_codes", columns, U32), persistent(name + "_scales", columns, U8)

        def quantize(mx, first, grouped):
            codes, scales = mx
            last = first + grouped.shape[1] // PACK
            nc.vector.quantize_mx(out=codes[:, first:last].bitcast(FP8X4), scales=scales[:, first:last], in_=grouped)

        def operand(mx, first, width):
            codes, scales = mx
            return codes[:, first : first + width].bitcast(FP8X4), scales[:, first : first + width]

        def interleave(engine, grouped, planes, lo, hi):
            out = grouped.rearrange("p (c i t) -> p c t i", i=4, t=PACK)
            in_ = planes.rearrange("p t (c i) -> p c t i", i=4)
            copy(engine, out[:, lo // 4 : hi // 4], in_[:, lo // 4 : hi // 4])

        def turn(sources):
            bank = new_bank()
            for i, words in enumerate(sources):
                nc.tensor.transpose(bank[:, P * i : P * (i + 1)], words, ident[:])
            return bank

        def pair_up(engine, grouped, bank):
            copy(
                engine,
                grouped.bitcast(F32).rearrange("p (a q u) -> p a q u", a=2, u=2),
                bank[:].rearrange("p (a u q) -> p a q u", a=2, u=2),
            )

        def product(out, stationary, moving, index, count):
            nc.tensor.matmul_mx(
                out=out,
                lhsT=stationary[0],
                lhsT_scale=stationary[1],
                rhs=moving[0],
                rhs_scale=moving[1],
                start=(index == 0),
                stop=(index == count - 1),
            )

        inv = persistent("inv", NS * PACK, F32)

        w_mx, w_grp = {}, {}

        def w_interleave(f, g, engine, lo=0, hi=BANK):
            if f not in w_grp:
                w_grp[f] = staged("w_grp", [P, NG * PLANES], BF16, "grp", GROUPED_BUFS)
                w_mx[f] = mx_tiles(f"w{f}", NG * BANK)
            interleave(engine, w_grp[f][:, PLANES * g : PLANES * (g + 1)], w_raw[f, g][:], lo, hi)

        def w_quantize(f, g):
            quantize(w_mx[f], BANK * g, w_grp[f][:, PLANES * g : PLANES * (g + 1)])

        x_bank = {}
        x_grp = [wide_tile(f"x_grp{a}", 2 * UNIT, BF16) for a in range(2)]
        x_mx = [mx_tiles(f"x{s}", PACK * NG * P) for s in range(NS)]

        def x_staged(t):
            return x_grp[t // 2][:, UNIT * (t % 2) : UNIT * (t % 2 + 1)]

        def x_turn(s, t):
            words = x_raw[s, t].bitcast(F32)
            x_bank[s, t] = turn([words[:, 2 * P * g + u : 2 * P * (g + 1) : 2] for g in range(NG) for u in range(2)])

        def x_copy(s, t):
            pair_up(SCALAR, x_staged(t), x_bank[s, t])

        def x_quantize(s, t):
            quantize(x_mx[s], NG * P * t, x_staged(t))

        h_bank, h_plain = {}, {}

        def trunk(s, t, f, passes=range(NG)):
            if (s, t, f) not in h_bank:
                h_bank[s, t, f] = new_bank()
            for g in passes:
                stationary = operand(x_mx[s], NG * P * t + P * g, P)
                product(h_bank[s, t, f][:], stationary, operand(w_mx[f], BANK * g, BANK), g, NG)

        def relu(s, t, f):
            if (s, f) not in h_plain:
                h_plain[s, f] = staged(f"h_plain{s}{f}", [P, PLANES], BF16, "plain", PLANE_BUFS)
            nc.scalar.activation(
                out=h_plain[s, f][:, BANK * t : BANK * (t + 1)].rearrange("p (u m e) -> p u m e", u=2, e=2),
                in_=h_bank[s, t, f][:].rearrange("p (m u e) -> p u m e", u=2, e=2),
                func=ACT.Relu,
            )

        ht_bank, hf_place = {}, {}
        hf_grp = persistent("hf_grp", TURNED_UNITS * UNIT, BF16)
        hf_mx = mx_tiles("hf", NS * NF * PASS)

        def h_turn(s, f, a):
            hf_place[s, f, a] = len(hf_place)
            words = h_plain[s, f][:].bitcast(F32)
            ht_bank[s, f, a] = turn([words[:, P * i : P * (i + 1)] for i in range(4 * a, 4 * a + 4)])

        def hf_staged(s, f, a, count):
            first = UNIT * (hf_place[s, f, a] % TURNED_UNITS)
            return hf_grp[:, first : first + UNIT * count]

        def h_copy(s, f, a, engine):
            pair_up(engine, hf_staged(s, f, a, 1), ht_bank[s, f, a])

        def hf_quantize(s, f, a, count):
            quantize(hf_mx, 2 * P * hf_place[s, f, a], hf_staged(s, f, a, count))

        def hf_operand(s, f, t):
            return operand(hf_mx, 2 * P * hf_place[s, f, t // 2] + P * (t % 2), P)

        hs_grp, hs_mx = {}, {}

        def h_interleave(s, f, engine, lo=0, hi=BANK):
            if f not in hs_grp:
                hs_grp[f] = staged("hs_grp", [P, NS * PLANES], BF16, "grp", GROUPED_BUFS)
                hs_mx[f] = mx_tiles(f"hs{f}", NS * BANK)
            planes = h_plain[s, f][:].rearrange("p (t c) -> p t c", t=PACK)
            interleave(engine, hs_grp[f][:, PLANES * s : PLANES * (s + 1)], planes, lo, hi)

        def hs_quantize(f):
            quantize(hs_mx[f], 0, hs_grp[f][:])

        b_bank = {}
        b_pair = [wide_tile(f"b_wide{a}", 2 * M, BF16) for a in range(2)]
        b_wide = [b_pair[j // 2][:, M * (j % 2) : M * (j % 2 + 1)] for j in range(PACK)]
        b_turned = [wide_tile(f"b_turned{a}", 2 * M, BF16) for a in range(2)]
        b_grp = persistent("b_grp", NS * PACK * PASS, BF16)
        b_mx = mx_tiles("b", NS * R)

        def b_widen(j):
            nc.vector.tensor_scalar(
                out=b_wide[j].rearrange("p (u q e) -> p q u e", u=2, e=2),
                in0=b_raw[j][:].bitcast(FP8).rearrange("p (q u e) -> p q u e", u=2, e=2),
                scalar1=one[:],
                scalar2=None,
                op0=ALU.mult,
            )

        def b_turn(j):
            words = b_wide[j].bitcast(F32)
            starts = [NS * P * u + P * s for s in range(NS) for u in range(2)]
            b_bank[j] = turn([words[:, c : c + P] for c in starts])

        def b_copy(j):
            nc.scalar.copy(
                out=b_turned[j // 2][:].bitcast(F32).rearrange("p (s j q u) -> p j s q u", s=NS, j=2, u=2)[:, j % 2],
                in_=b_bank[j][:].rearrange("p (s u q) -> p s q u", s=NS, u=2),
            )

        def b_scale(s, j, count=1):
            source, target = UNIT * s + PASS * (j % 2), PACK * PASS * s + PASS * j
            nc.vector.tensor_tensor(
                out=b_grp[:, target : target + PASS * count].rearrange("p (r t) -> p r t", t=PACK),
                in0=b_turned[j // 2][:, source : source + PASS * count].rearrange("p (r t) -> p r t", t=PACK),
                in1=bscale[:, s, :].unsqueeze(1).to_broadcast([P, P * count, PACK]),
                op=ALU.mult,
            )

        p_view = policy.rearrange("(s q t) a -> s t q a", s=NS, t=PACK)
        v_view = value.rearrange("(p j) f -> p j f", j=PACK)
        p_bank, p_rows, v_bank, v_rows = {}, {}, {}, {}

        def single_tile():
            return staged("result", [P, BANK], F32, "rows512", SINGLE_BUFS)

        def p_operand(f, first, width):
            return pw[:, f, 2 * first : 2 * (first + width)].bitcast(FP4X4), ps[:, f, first : first + width]

        def scaled_copy(engine, out, in_, s, t):
            factor = inv[:, PACK * s + t : PACK * s + t + 1]
            if engine == SCALAR:
                nc.scalar.activation(out=out, in_=in_, func=ACT.Copy, scale=factor)
            else:
                nc.vector.tensor_scalar(out=out, in0=in_, scalar1=factor, scalar2=None, op0=ALU.mult)

        def policy_mm(s, t, n):
            p_bank[s, t, n] = new_bank()
            for f in range(NF):
                product(p_bank[s, t, n][:], hf_operand(s, f, t), p_operand(f, BANK * n, BANK), f, NF)

        def policy_rows(s, t, n):
            if n == 0:
                p_rows[s, t] = wide_tile("result", A, F32)
            scaled_copy(SCALAR, p_rows[s, t][:, BANK * n : BANK * (n + 1)], p_bank[s, t, n][:], s, t)
            if n == 1:
                nc.sync.dma_start(out=p_view[s, t], in_=p_rows[s, t][:])

        def policy_single(s, t, n, engine):
            result = single_tile()
            scaled_copy(engine, result[:], p_bank[s, t, n][:], s, t)
            nc.sync.dma_start(out=p_view[s, t, :, BANK * n : BANK * (n + 1)], in_=result[:])

        def policy_parts(s, t, n, parts):
            result = single_tile()
            first = 0
            for engine, widths in parts:
                bank, done = new_bank(), 0
                for width in widths:
                    for f in range(NF):
                        moving = p_operand(f, BANK * n + first + done, width)
                        product(bank[:, done : done + width], hf_operand(s, f, t), moving, f, NF)
                    done += width
                scaled_copy(engine, result[:, first : first + done], bank[:, 0:done], s, t)
                first += done
            nc.sync.dma_start(out=p_view[s, t, :, BANK * n : BANK * (n + 1)], in_=result[:])

        def value_mm(j, f):
            v_bank[j, f] = new_bank()
            for s in range(NS):
                product(v_bank[j, f][:], operand(b_mx, R * s + P * j, P), operand(hs_mx[f], BANK * s, BANK), s, NS)

        def apply_gain(j, f, result):
            nc.vector.tensor_tensor(
                out=result.rearrange("p (m u e) -> p m u e", u=2, e=2),
                in0=v_bank[j, f][:].rearrange("p (u m e) -> p m u e", u=2, e=2),
                in1=vg[:, BANK * f : BANK * (f + 1)].rearrange("p (m u e) -> p m u e", u=2, e=2),
                op=ALU.mult,
            )

        def value_paired(j, f):
            if j % 2 == 0:
                v_rows[f] = wide_tile("result", 2 * BANK, F32)
            apply_gain(j, f, v_rows[f][:, BANK * (j % 2) : BANK * (j % 2 + 1)])
            if j % 2 == 1:
                nc.sync.dma_start(
                    out=v_view[:, j - 1 : j + 1, BANK * f : BANK * (f + 1)],
                    in_=v_rows[f][:].rearrange("p (j c) -> p j c", j=2),
                )

        def value_single(j, f):
            result = single_tile()
            apply_gain(j, f, result[:])
            nc.sync.dma_start(out=v_view[:, j, BANK * f : BANK * (f + 1)], in_=result[:])

        for j in range(PACK):
            b_widen(j)
            b_turn(j)
            b_copy(j)
        w_interleave(0, 0, VECTOR)
        b_scale(0, 0)
        w_quantize(0, 0)
        b_scale(1, 0)

        for t in range(PACK):
            x_turn(0, t)
            x_copy(0, t)
        for t in (0, 1):
            x_quantize(0, t)
            trunk(0, t, 0, [0])
        w_interleave(0, 1, VECTOR, 0, W_CUT)
        w_interleave(0, 1, SCALAR, W_CUT)
        for t in (2, 3):
            x_quantize(0, t)
        w_quantize(0, 1)
        for t in (0, 1):
            x_turn(1, t)
            x_copy(1, t)
        for t in (2, 3):
            trunk(0, t, 0, [0])
        for t in range(PACK):
            trunk(0, t, 0, [1])
        w_interleave(1, 0, VECTOR, 0, W_CUT)
        w_interleave(1, 0, SCALAR, W_CUT)
        for t in (0, 1):
            x_quantize(1, t)
        w_quantize(1, 0)
        for t in (0, 1):
            relu(0, t, 0)

        for t in (2, 3):
            x_turn(1, t)
            x_copy(1, t)
        w_interleave(1, 1, VECTOR, 0, HALF)
        b_scale(0, 1)
        for t in (2, 3):
            x_quantize(1, t)
        for t in (0, 1):
            trunk(1, t, 0)
        for t in (0, 1):
            trunk(0, t, 1, [0])
        for t in (2, 3):
            relu(0, t, 0)
            trunk(1, t, 0)
        w_interleave(1, 1, VECTOR, HALF)
        w_interleave(2, 0, VECTOR, 0, W_FILL)
        w_quantize(1, 1)
        for t in range(PACK):
            relu(1, t, 0)
        for t in (2, 3):
            trunk(0, t, 1, [0])
        for t in range(PACK):
            trunk(0, t, 1, [1])
            relu(0, t, 1)
        w_interleave(2, 0, VECTOR, W_FILL)
        w_interleave(2, 1, VECTOR)
        for g in range(NG):
            w_quantize(2, g)
        h_interleave(0, 0, VECTOR)

        for t in (0, 1):
            trunk(1, t, 1)
            relu(1, t, 1)
        for f, a, engine in ((0, 0, VECTOR), (0, 1, VECTOR), (1, 0, VECTOR), (1, 1, SCALAR)):
            h_turn(0, f, a)
            h_copy(0, f, a, engine)
        b_scale(0, 2, 2)
        hf_quantize(0, 0, 0, 4)
        for t in range(PACK):
            trunk(0, t, 2)
            relu(0, t, 2)
        for t in (2, 3):
            trunk(1, t, 1)
            relu(1, t, 1)
        for s, f, a, engine in ((0, 2, 0, VECTOR), (0, 2, 1, SCALAR), (1, 0, 0, SCALAR), (1, 0, 1, SCALAR)):
            h_turn(s, f, a)
            h_copy(s, f, a, engine)
        b_scale(1, 1)
        hf_quantize(0, 2, 0, 2)
        nc.scalar.copy(out=inv[:], in_=inv16[:].rearrange("p s t -> p (s t)"))
        for t in range(PACK):
            trunk(1, t, 2)
            relu(1, t, 2)

        h_interleave(1, 0, VECTOR)
        b_scale(1, 2, 2)
        hs_quantize(0)
        quantize(b_mx, 0, b_grp[:])
        h_interleave(0, 1, VECTOR)
        hf_quantize(1, 0, 0, 2)
        for t in range(3):
            for n in range(2):
                policy_mm(0, t, n)
            if t == 2:
                h_interleave(1, 1, SCALAR, 0, HALF)
            for n in range(2):
                policy_rows(0, t, n)
        h_interleave(1, 1, SCALAR, HALF)
        for j in range(PACK):
            value_mm(j, 0)
            value_paired(j, 0)
        hs_quantize(1)

        for a in range(2):
            for f in (1, 2):
                h_turn(1, f, a)
                h_copy(1, f, a, SCALAR)
        h_interleave(1, 2, VECTOR, 0, HALF)
        hf_quantize(1, 1, 0, 2)
        h_interleave(1, 2, VECTOR, HALF)
        for n in range(2):
            policy_mm(0, 3, n)
            policy_rows(0, 3, n)
        h_interleave(0, 2, SCALAR, 0, W_CUT)

        for n in range(2):
            for j in (2 * n, 2 * n + 1):
                value_mm(j, 1)
                value_paired(j, 1)
            if n == 0:
                h_interleave(0, 2, VECTOR, W_CUT)
            policy_mm(1, 0, n)
            policy_rows(1, 0, n)
        hs_quantize(2)
        hf_quantize(1, 1, 1, 2)
        for n in range(2):
            policy_mm(1, 1, n)
            policy_rows(1, 1, n)

        for n in range(2):
            for j in (2 * n, 2 * n + 1):
                value_mm(j, 2)
                value_single(j, 2)
            policy_mm(1, 2, n)
            policy_single(1, 2, n, SCALAR)
        policy_parts(1, 3, 0, ((VECTOR, [HALF]), (VECTOR, [HALF])))
        policy_parts(1, 3, 1, ((VECTOR, [HALF]), (SCALAR, [HALF])))
